import numpy as np
import ml_dtypes


def mxq(x, axis, fmt="e4m3"):
    dtype, down = {"e4m3": (ml_dtypes.float8_e4m3fn, 7), "e5m2": (ml_dtypes.float8_e5m2, 14)}[fmt]
    v = np.moveaxis(np.asarray(x, np.float32).astype(ml_dtypes.bfloat16).astype(np.float64), axis, -1)
    blocks = v.reshape(v.shape[:-1] + (-1, 32))
    amax = np.abs(blocks).max(-1, keepdims=True)
    byte = np.maximum(np.where(amax > 0, np.frexp(amax)[1] - 1 + 127, 0) - down, 1)
    scale = np.exp2(byte - 127.0)
    codes = (blocks / scale).astype(np.float32).astype(dtype).astype(np.float64)
    return np.moveaxis((codes * scale).reshape(v.shape), -1, axis)


WIDE = False


def mx_kscale(k):
    if not WIDE:
        return np.ones(k)
    levels = np.array([10, -10, 5, -5, 0])
    if k % 512:
        return np.exp2(np.random.permutation(np.resize(levels, k // 32))).repeat(32)
    a = np.empty((k // 512, 16))
    for p in range(k // 512):
        a[p, :8] = np.random.permutation(np.resize(levels, 8))
        for g in range(8):
            far = levels[np.abs(levels - a[p, g]) >= 10]
            a[p, g + 8] = far[np.random.randint(len(far))]
    return np.exp2(a.ravel()).repeat(32)


def f64(x):
    return np.asarray(x).astype(np.float64)


def striped(idx):
    return np.tile(idx.reshape(-1, 16).T, (8, 1)).astype(np.uint16)


def unstriped(offs):
    return offs[:16].T.reshape(-1).astype(np.int64)


E2M1 = np.array([0.0, 0.5, 1.0, 1.5, 2.0, 3.0, 4.0, 6.0, -0.0, -0.5, -1.0, -1.5, -2.0, -3.0, -4.0, -6.0])


def pack_weight(w, fmt):
    k, n = w.shape
    w = f64(np.asarray(w, np.float32).astype(ml_dtypes.bfloat16)).reshape(k // 32, 32, n)
    amax = np.abs(w).max(1)
    if fmt == "e4m3":
        byte = np.frexp(amax)[1] - 1 + 127 - 7
    else:
        mant, ex = np.frexp(amax / 6.0)
        byte = np.where(mant > 0.5, ex, ex - 1) + 127
    byte = np.clip(np.where(amax > 0, byte, 1), 1, 254)
    scaled = (w * np.exp2(127.0 - byte)[:, None, :]).reshape(k, n).astype(np.float32)
    by_word = np.ascontiguousarray(scaled.reshape(k // 512, 128, 4, n).transpose(0, 1, 3, 2))
    if fmt == "e4m3":
        words = by_word.astype(ml_dtypes.float8_e4m3fn).view(np.uint8)
    else:
        c = by_word.astype(ml_dtypes.float4_e2m1fn).view(np.uint8) & 0xF
        words = (c[..., 0::2] | (c[..., 1::2] << 4)).reshape(k // 512, 128, 2 * n)
    return np.ascontiguousarray(words), np.ascontiguousarray(byte.astype(np.uint8).reshape(k // 512, 16, n))


def unpack_weight(words, scales, fmt):
    g, _, n = scales.shape
    words = np.ascontiguousarray(words).reshape(g, 128, n, -1)
    if fmt == "e4m3":
        vals = words.view(ml_dtypes.float8_e4m3fn).astype(np.float64)
    else:
        nib = np.empty((g, 128, n, 4), np.uint8)
        nib[..., 0::2] = words & 0xF
        nib[..., 1::2] = words >> 4
        vals = E2M1[nib]
    vals = vals * np.repeat(np.exp2(scales.astype(np.float64) - 127.0), 8, axis=1)[..., None]
    return vals.transpose(0, 1, 3, 2).reshape(g * 512, n)


def gelu(v):
    return 0.5 * v * (1.0 + np.tanh(np.sqrt(2.0 / np.pi) * (v + 0.044715 * v**3)))


K, T, S, H, N = 1536, 2048, 1024, 512, 640


def setup_inputs():
    n = np.random.standard_normal
    s = mx_kscale(K)[:, None]
    u = mx_kscale(H)[:, None]
    tab_words, tab_scales = pack_weight(n((K, T)) * s, "e4m3")
    wx = n((K, H)) / np.sqrt(K) / s
    wd = 3.0 * n((K, H)) / np.sqrt(K) / s * u.T
    wd_words, wd_scales = pack_weight(wd, "e2m1")
    wo = 2.0 * n((H, N)) / np.sqrt(H) / u
    return {
        "tab_words": tab_words,
        "tab_scales": tab_scales,
        "offs": striped(np.random.permutation(T)[:S]),
        "wx": wx.astype(np.float32),
        "wd_words": wd_words,
        "wd_scales": wd_scales,
        "wo": wo.astype(np.float32),
    }


def reference(tab_words, tab_scales, offs, wx, wd_words, wd_scales, wo):
    v = unpack_weight(tab_words, tab_scales, "e4m3")[:, unstriped(offs)]
    wd = unpack_weight(wd_words, wd_scales, "e2m1")
    x = mxq(f64(wx), 0, "e4m3").T @ v
    a = wd.T @ v
    p = x / (1.0 + x * x)
    h = a * (p * p)
    return mxq(f64(wo), 0, "e4m3").T @ mxq(h, 0, "e4m3")

@@ -1,0 +1,309 @@
+from contextlib import ExitStack
+
+import concourse.mybir as mybir
+
+K, T, S, H, N = 1536, 2048, 1024, 512, 640
+FLOPS = 2 * S * (2 * K * H + H * N)
+
+F32 = mybir.dt.float32
+BF16 = mybir.dt.bfloat16
+I32 = mybir.dt.int32
+U32 = mybir.dt.uint32
+U16 = mybir.dt.uint16
+U8 = mybir.dt.uint8
+FP8X4 = mybir.dt.float8_e4m3fn_x4
+FP4X4 = mybir.dt.float4_e2m1fn_x4
+ACT = mybir.ActivationFunctionType
+ALU = mybir.AluOpType
+
+P = 128
+PASSES = K // 512
+HALF = 512
+HALVES = S // HALF
+EARLY = 6
+X_BANK = (0, 1, 2, 3, 4, 5, 0, 1)
+A_BANK = (6, 7, 6, 7, 2, 3, 6, 7)
+CHUNKS = ((0, 512), (512, 256), (768, 128), (896, 128))
+OUT_BANKS = ((4, 5, 2, 3, 0), (1, 6, 7), (4, 5), (2, 3))
+
+
+def tile_list_bead_well_energies_kernel(tc, tab_words, tab_scales, offs, wx, wd_words, wd_scales, wo, out):
+    nc = tc.nc
+    with ExitStack() as ctx:
+        keep = ctx.enter_context(tc.tile_pool(name="keep", bufs=1))
+        ring = ctx.enter_context(tc.tile_pool(name="ring", bufs=4))
+        stage = ctx.enter_context(tc.tile_pool(name="stage", bufs=4))
+        pair = ctx.enter_context(tc.tile_pool(name="pair", bufs=2))
+        psum = ctx.enter_context(tc.psum_pool(name="psum", bufs=1))
+
+        offsets = keep.tile([P, S // 16], U16, name="offsets")
+        nc.sync.dma_start(offsets[:], offs)
+
+        ts_all = keep.tile([P, T // 4], I32, name="ts_all", align_bytes=64)
+        nc.vector.memset(ts_all[:], 0)
+        ws_raw = keep.tile([P, PASSES, H // 4], I32, name="ws_raw", align_bytes=64)
+        nc.vector.memset(ws_raw[:], 0)
+        ts_low = [keep.tile([P, S // 4], I32, name=f"ts_low{a}", align_bytes=64) for a in range(1, PASSES)]
+        for tile in ts_low:
+            nc.gpsimd.memset(tile[96:128, :], 0)
+
+        ts_i32 = tab_scales.bitcast(I32)
+        for q in range(4):
+            nc.scalar.dma_start(ts_all[32 * q : 32 * q + 4 * PASSES, :], ts_i32[:, 4 * q : 4 * q + 4, :])
+
+        warm = keep.tile([P, 1], F32, name="warm")
+        nc.gpsimd.memset(warm[:], 1.0)
+        warm_out = keep.tile([P, 1], F32, name="warm_out")
+        nc.scalar.activation(warm_out[:], warm[:], ACT.Abs_reciprocal_sqrt)
+
+        wx_raw, tab = [], []
+        for a in range(PASSES):
+            tab.append(stage.tile([P, T], I32, name=f"tab{a}", tag="stage", align_bytes=64))
+            nc.sync.dma_start(tab[a][:], tab_words[a].rearrange("p t i -> p (t i)").bitcast(I32))
+            wx_raw.append(stage.tile([P, 4, H], F32, name=f"wx_raw{a}", tag="stage", align_bytes=64))
+            nc.sync.dma_start(wx_raw[a][:], wx[512 * a : 512 * (a + 1), :].rearrange("(p j) c -> p j c", j=4))
+        wd_raw = stage.tile([P, PASSES, H // 2], I32, name="wd_raw", tag="stage", align_bytes=64)
+        nc.sync.dma_start(wd_raw[:], wd_words.bitcast(I32).rearrange("a p c -> p a c"))
+        wo_raw = stage.tile([P, 4, N], F32, name="wo_raw", tag="stage", align_bytes=64)
+        wo_rows = wo.rearrange("(u t e) n -> e u t n", t=4, e=4)
+        for e in range(4):
+            nc.sync.dma_start(wo_raw[e:P:4, :, :], wo_rows[e])
+        ws_i32 = wd_scales.bitcast(I32)
+        for q in range(4):
+            nc.gpsimd.dma_start(ws_raw[32 * q : 32 * q + 4, :, :], ws_i32[:, 4 * q : 4 * q + 4, :].rearrange("a r c -> r a c"))
+
+        ts_pick = keep.tile([P, S // 4], I32, name="ts_pick", align_bytes=64)
+        v_planes = [ts_pick] + ts_low
+        wd_codes = keep.tile([P, PASSES, H // 2], I32, name="wd_codes", align_bytes=64)
+        wd_planes = keep.tile([P, PASSES, H // 4], I32, name="wd_planes", align_bytes=64)
+
+        def gather_scales():
+            nc.vector.tensor_copy(ts_pick[:].bitcast(U8), ts_all[:].bitcast(U8).indirect(offsets[:]))
+            for a in range(1, PASSES):
+                nc.gpsimd.dma_start(ts_low[a - 1][0:112, :], ts_pick[4 * a : 4 * a + 112, :])
+
+        def order_wd_codes(a):
+            nc.vector.tensor_copy(
+                wd_codes[:, a, :].rearrange("p (t u k) -> p t u k", t=4, k=2),
+                wd_raw[:, a, :].rearrange("p (u t k) -> p t u k", t=4, k=2),
+            )
+
+        def order_wd_planes():
+            nc.vector.tensor_copy(
+                wd_planes[:].rearrange("p a (t u) -> p a t u", t=4),
+                ws_raw[:].rearrange("p a (u t) -> p a t u", t=4),
+            )
+
+        wx_bf = [keep.tile([P, 4, P * 4], BF16, name=f"wx_bf{a}", align_bytes=64) for a in range(PASSES)]
+        wx_codes = [keep.tile([P, H], U32, name=f"wx_codes{a}", align_bytes=64) for a in range(PASSES)]
+        wx_planes = [keep.tile([P, H], U8, name=f"wx_planes{a}", align_bytes=64) for a in range(PASSES)]
+        v_codes = [[keep.tile([P, HALF], I32, name=f"v_codes{a}_{b}", align_bytes=64) for b in range(HALVES)] for a in range(PASSES)]
+
+        def cast_wx(a, t, on_vector):
+            dst = wx_bf[a][:, t, :].rearrange("p (u e j) -> p u j e", e=4, j=4)
+            src = wx_raw[a][:].rearrange("p j (u t e) -> p t u j e", t=4, e=4)[:, t]
+            if on_vector:
+                nc.vector.tensor_copy(dst, src)
+            else:
+                nc.scalar.copy(dst, src)
+
+        def quant_wx(a, t0, t1):
+            nc.vector.quantize_mx(
+                out=wx_codes[a][:, P * t0 : P * t1].bitcast(FP8X4),
+                scales=wx_planes[a][:, P * t0 : P * t1],
+                in_=wx_bf[a][:, t0:t1, :].rearrange("p t c -> p (t c)"),
+            )
+
+        def gather(a, b):
+            cols = slice(b * HALF // 16, (b + 1) * HALF // 16)
+            nc.vector.tensor_copy(v_codes[a][b][:].bitcast(U32), tab[a][:].bitcast(U32).indirect(offsets[:, cols]))
+
+        units = [(b, t) for b in range(HALVES) for t in range(4)]
+        x_ps = {}
+        a_ps = {}
+
+        def mm_x(a, i):
+            b, t = units[i]
+            if a == 0:
+                x_ps[b, t] = psum.tile([P, HALF], F32, name=f"x{i}", tag=f"bank{X_BANK[i]}")
+            nc.tensor.matmul_mx(
+                out=x_ps[b, t][:],
+                lhsT=wx_codes[a][:, P * t : P * (t + 1)].bitcast(FP8X4),
+                lhsT_scale=wx_planes[a][:, P * t : P * (t + 1)],
+                rhs=v_codes[a][b][:].bitcast(FP8X4),
+                rhs_scale=ts_pick[:].bitcast(U8)[4 * a : P, HALF * b : HALF * (b + 1)],
+                start=(a == 0),
+                stop=(a == PASSES - 1),
+            )
+
+        def mm_a(i):
+            b, t = units[i]
+            a_ps[b, t] = psum.tile([P, HALF], F32, name=f"a{i}", tag=f"bank{A_BANK[i]}")
+            for a in range(PASSES):
+                nc.tensor.matmul_mx(
+                    out=a_ps[b, t][:],
+                    lhsT=wd_codes[:, a, 64 * t : 64 * (t + 1)].bitcast(U8).bitcast(FP4X4),
+                    lhsT_scale=wd_planes[:, a, 32 * t : 32 * (t + 1)].bitcast(U8),
+                    rhs=v_codes[a][b][:].bitcast(FP8X4),
+                    rhs_scale=v_planes[a][:].bitcast(U8)[:, HALF * b : HALF * (b + 1)],
+                    start=(a == 0),
+                    stop=(a == PASSES - 1),
+                )
+
+        last = PASSES - 1
+        for a in range(last):
+            for t in range(4):
+                cast_wx(a, t, False)
+            gather(a, 0)
+            gather(a, 1)
+            if a == 0:
+                gather_scales()
+            quant_wx(a, 0, 4)
+            if a == 1:
+                order_wd_planes()
+            for i in range(EARLY):
+                mm_x(a, i)
+        gather(last, 0)
+        gather(last, 1)
+        cast_wx(last, 0, True)
+        cast_wx(last, 1, True)
+        for t in range(4):
+            quant_wx(last, t, t + 1)
+            if t + 2 < 4:
+                cast_wx(last, t + 2, True)
+            mm_x(last, t)
+        for i in range(4, EARLY):
+            mm_x(last, i)
+        for a in range(PASSES):
+            order_wd_codes(a)
+        mm_a(0)
+        mm_a(1)
+
+        wo_bf = keep.tile([P, N, 4], BF16, name="wo_bf", align_bytes=64)
+        wo_codes = keep.tile([P, N], U32, name="wo_codes", align_bytes=64)
+        wo_planes = keep.tile([P, N], U8, name="wo_planes", align_bytes=64)
+        for n in range(N // P):
+            cols = slice(P * n, P * (n + 1))
+            nc.gpsimd.tensor_scalar(
+                wo_bf[:, cols, :], wo_raw[:, :, cols].rearrange("p t n -> p n t"), 1.0, 0.0, ALU.mult, ALU.add
+            )
+
+        def quant_wo(n0, n1):
+            nc.vector.quantize_mx(
+                out=wo_codes[:, n0:n1].bitcast(FP8X4),
+                scales=wo_planes[:, n0:n1],
+                in_=wo_bf[:, n0:n1, :].rearrange("p n t -> p (n t)"),
+            )
+
+        s_sb, w_sb, q_sb, p_sb, m_sb = {}, {}, {}, {}, {}
+
+        def step_s(u):
+            s_sb[u] = ring.tile([P, HALF], F32, name="s_sb")
+            nc.scalar.activation(s_sb[u][:], x_ps[u][:], ACT.Square)
+
+        def step_w(u):
+            w_sb[u] = ring.tile([P, HALF], F32, name="w_sb")
+            nc.scalar.activation(w_sb[u][:], s_sb[u][:], ACT.Abs_reciprocal_sqrt, bias=1.0)
+
+        def step_q(u):
+            q_sb[u] = ring.tile([P, HALF], F32, name="q_sb")
+            nc.scalar.activation(q_sb[u][:], w_sb[u][:], ACT.Square)
+
+        def step_p(u):
+            b, t = u
+            if t == 0:
+                p_sb[b] = pair.tile([P, 4, HALF], F32, name="p_sb")
+            nc.vector.tensor_tensor(p_sb[b][:, t, :], x_ps[u][:], q_sb[u][:], ALU.mult)
+
+        def step_m(u):
+            b, t = u
+            if t == 0:
+                m_sb[b] = pair.tile([P, 4, HALF], F32, name="m_sb")
+            nc.vector.tensor_tensor(m_sb[b][:, t, :], a_ps[u][:], p_sb[b][:, t, :], ALU.mult)
+
+        h_bf = keep.tile([P, S, 4], BF16, name="h_bf", align_bytes=64)
+        h_codes = keep.tile([P, S], U32, name="h_codes", align_bytes=64)
+        h_planes = keep.tile([P, S], U8, name="h_planes", align_bytes=64)
+
+        def step_h(j0, width):
+            b = j0 // HALF
+            cols = slice(j0 - HALF * b, j0 - HALF * b + width)
+            nc.vector.tensor_tensor(
+                h_bf[:, j0 : j0 + width, :].rearrange("p (c i) t -> p c t i", i=4),
+                m_sb[b][:, :, cols].rearrange("p t (c i) -> p c t i", i=4),
+                p_sb[b][:, :, cols].rearrange("p t (c i) -> p c t i", i=4),
+                ALU.mult,
+            )
+
+        def quant_h(j0, width):
+            cols = slice(j0, j0 + width)
+            nc.vector.quantize_mx(
+                out=h_codes[:, cols].bitcast(FP8X4),
+                scales=h_planes[:, cols],
+                in_=h_bf[:, cols, :].rearrange("p j t -> p (j t)"),
+            )
+
+        out_tiles = out.rearrange("(n p) j -> p n j", p=P)
+
+        def energies(c, on_vector):
+            j0, width = CHUNKS[c]
+            per_bank = HALF // width
+            for g, bank in enumerate(OUT_BANKS[c]):
+                n0 = g * per_bank
+                count = min(per_bank, N // P - n0)
+                acc = psum.tile([P, count, width], F32, name=f"o{c}_{g}", tag=f"bank{bank}")
+                for n in range(count):
+                    cols = slice(P * (n0 + n), P * (n0 + n + 1))
+                    nc.tensor.matmul_mx(
+                        out=acc[:, n, :],
+                        lhsT=wo_codes[:, cols].bitcast(FP8X4),
+                        lhsT_scale=wo_planes[:, cols],
+                        rhs=h_codes[:, j0 : j0 + width].bitcast(FP8X4),
+                        rhs_scale=h_planes[:, j0 : j0 + width],
+                        start=True,
+                        stop=True,
+                    )
+                res = keep.tile([P, count, width], F32, name=f"res{c}_{g}")
+                if g in on_vector:
+                    nc.vector.tensor_copy(res[:], acc[:])
+                else:
+                    nc.scalar.copy(res[:], acc[:])
+                nc.sync.dma_start(out_tiles[:, n0 : n0 + count, j0 : j0 + width], res[:])
+
+        for i in range(0, len(units), 2):
+            for step in (step_s, step_w, step_q, step_p):
+                step(units[i])
+                step(units[i + 1])
+            if i == 0:
+                for k in range(EARLY, len(units)):
+                    for a in range(PASSES):
+                        mm_x(a, k)
+            if i == 4:
+                step_h(0, 256)
+            if i == 6:
+                quant_h(256, 256)
+            step_m(units[i])
+            step_m(units[i + 1])
+            if i == 0:
+                mm_a(2)
+                mm_a(3)
+            if i == 2:
+                mm_a(4)
+                mm_a(5)
+                mm_a(6)
+                mm_a(7)
+                quant_wo(0, 512)
+                quant_wo(512, 640)
+            if i == 4:
+                quant_h(0, 256)
+                step_h(256, 256)
+        energies(0, ())
+        step_h(512, 256)
+        step_h(768, 128)
+        quant_h(512, 256)
+        step_h(896, 128)
+        quant_h(768, 128)
+        energies(1, ())
+        quant_h(896, 128)
+        energies(2, ())
+        energies(3, (0,))

@@ -23,8 +23,8 @@ HALVES = S // HALF
 EARLY = 6
 X_BANK = (0, 1, 2, 3, 4, 5, 0, 1)
 A_BANK = (6, 7, 6, 7, 2, 3, 6, 7)
-CHUNKS = ((0, 512), (512, 256), (768, 128), (896, 128))
-OUT_BANKS = ((4, 5, 2, 3, 0), (1, 6, 7), (4, 5), (2, 3))
+CHUNKS = ((0, 256), (256, 256), (512, 256), (768, 128), (896, 128))
+OUT_BANKS = ((4, 5, 2), (3, 0, 1), (6, 7, 4), (5, 2), (3, 0))
 
 
 def tile_list_bead_well_energies_kernel(tc, tab_words, tab_scales, offs, wx, wd_words, wd_scales, wo, out):
@@ -33,26 +33,26 @@ def tile_list_bead_well_energies_kernel(tc, tab_words, tab_scales, offs, wx, wd_
         keep = ctx.enter_context(tc.tile_pool(name="keep", bufs=1))
         ring = ctx.enter_context(tc.tile_pool(name="ring", bufs=4))
         stage = ctx.enter_context(tc.tile_pool(name="stage", bufs=4))
+        swap = ctx.enter_context(tc.tile_pool(name="swap", bufs=1))
         pair = ctx.enter_context(tc.tile_pool(name="pair", bufs=2))
         psum = ctx.enter_context(tc.psum_pool(name="psum", bufs=1))
 
         offsets = keep.tile([P, S // 16], U16, name="offsets")
         nc.sync.dma_start(offsets[:], offs)
 
-        ts_all = keep.tile([P, T // 4], I32, name="ts_all", align_bytes=64)
-        nc.vector.memset(ts_all[:], 0)
+        ts_all = swap.tile([P, T // 4], I32, name="ts_all", tag="swap10", align_bytes=64)
+        nc.gpsimd.memset(ts_all[:], 0)
+        ts_i32 = tab_scales.bitcast(I32)
+        for q in range(4):
+            nc.gpsimd.dma_start(ts_all[32 * q : 32 * q + 4 * PASSES, :], ts_i32[:, 4 * q : 4 * q + 4, :])
         ws_raw = keep.tile([P, PASSES, H // 4], I32, name="ws_raw", align_bytes=64)
         nc.vector.memset(ws_raw[:], 0)
         ts_low = [keep.tile([P, S // 4], I32, name=f"ts_low{a}", align_bytes=64) for a in range(1, PASSES)]
         for tile in ts_low:
-            nc.gpsimd.memset(tile[96:128, :], 0)
-
-        ts_i32 = tab_scales.bitcast(I32)
-        for q in range(4):
-            nc.scalar.dma_start(ts_all[32 * q : 32 * q + 4 * PASSES, :], ts_i32[:, 4 * q : 4 * q + 4, :])
+            nc.vector.memset(tile[96:128, :], 0)
 
         warm = keep.tile([P, 1], F32, name="warm")
-        nc.gpsimd.memset(warm[:], 1.0)
+        nc.vector.memset(warm[:], 1.0)
         warm_out = keep.tile([P, 1], F32, name="warm_out")
         nc.scalar.activation(warm_out[:], warm[:], ACT.Abs_reciprocal_sqrt)
 
@@ -94,10 +94,10 @@ def tile_list_bead_well_energies_kernel(tc, tab_words, tab_scales, offs, wx, wd_
                 ws_raw[:].rearrange("p a (u t) -> p a t u", t=4),
             )
 
-        wx_bf = [keep.tile([P, 4, P * 4], BF16, name=f"wx_bf{a}", align_bytes=64) for a in range(PASSES)]
+        wx_bf = [swap.tile([P, 4, P * 4], BF16, name=f"wx_bf{a}", tag=tag, align_bytes=64) for a, tag in enumerate(("swap11", "wx_bf1", "swap21"))]
         wx_codes = [keep.tile([P, H], U32, name=f"wx_codes{a}", align_bytes=64) for a in range(PASSES)]
         wx_planes = [keep.tile([P, H], U8, name=f"wx_planes{a}", align_bytes=64) for a in range(PASSES)]
-        v_codes = [[keep.tile([P, HALF], I32, name=f"v_codes{a}_{b}", align_bytes=64) for b in range(HALVES)] for a in range(PASSES)]
+        v_codes = [[None] * HALVES for a in range(PASSES)]
 
         def cast_wx(a, t, on_vector):
             dst = wx_bf[a][:, t, :].rearrange("p (u e j) -> p u j e", e=4, j=4)
@@ -116,6 +116,7 @@ def tile_list_bead_well_energies_kernel(tc, tab_words, tab_scales, offs, wx, wd_
 
         def gather(a, b):
             cols = slice(b * HALF // 16, (b + 1) * HALF // 16)
+            v_codes[a][b] = swap.tile([P, HALF], I32, name=f"v_codes{a}_{b}", tag=f"swap{a}{b}", align_bytes=64)
             nc.vector.tensor_copy(v_codes[a][b][:].bitcast(U32), tab[a][:].bitcast(U32).indirect(offsets[:, cols]))
 
         units = [(b, t) for b in range(HALVES) for t in range(4)]
@@ -158,13 +159,12 @@ def tile_list_bead_well_energies_kernel(tc, tab_words, tab_scales, offs, wx, wd_
             gather(a, 1)
             if a == 0:
                 gather_scales()
-            quant_wx(a, 0, 4)
-            if a == 1:
-                order_wd_planes()
+                quant_wx(0, 0, 4)
+        gather(last, 0)
+        quant_wx(1, 0, 4)
+        for a in range(last):
             for i in range(EARLY):
                 mm_x(a, i)
-        gather(last, 0)
-        gather(last, 1)
         cast_wx(last, 0, True)
         cast_wx(last, 1, True)
         for t in range(4):
@@ -172,12 +172,14 @@ def tile_list_bead_well_energies_kernel(tc, tab_words, tab_scales, offs, wx, wd_
             if t + 2 < 4:
                 cast_wx(last, t + 2, True)
             mm_x(last, t)
-        for i in range(4, EARLY):
-            mm_x(last, i)
+        order_wd_planes()
         for a in range(PASSES):
             order_wd_codes(a)
+        gather(last, 1)
         mm_a(0)
         mm_a(1)
+        for i in range(4, EARLY):
+            mm_x(last, i)
 
         wo_bf = keep.tile([P, N, 4], BF16, name="wo_bf", align_bytes=64)
         wo_codes = keep.tile([P, N], U32, name="wo_codes", align_bytes=64)
@@ -225,10 +227,10 @@ def tile_list_bead_well_energies_kernel(tc, tab_words, tab_scales, offs, wx, wd_
         h_codes = keep.tile([P, S], U32, name="h_codes", align_bytes=64)
         h_planes = keep.tile([P, S], U8, name="h_planes", align_bytes=64)
 
-        def step_h(j0, width):
+        def step_h(j0, width, engine):
             b = j0 // HALF
             cols = slice(j0 - HALF * b, j0 - HALF * b + width)
-            nc.vector.tensor_tensor(
+            engine.tensor_tensor(
                 h_bf[:, j0 : j0 + width, :].rearrange("p (c i) t -> p c t i", i=4),
                 m_sb[b][:, :, cols].rearrange("p t (c i) -> p c t i", i=4),
                 p_sb[b][:, :, cols].rearrange("p t (c i) -> p c t i", i=4),
@@ -278,8 +280,11 @@ def tile_list_bead_well_energies_kernel(tc, tab_words, tab_scales, offs, wx, wd_
                 for k in range(EARLY, len(units)):
                     for a in range(PASSES):
                         mm_x(a, k)
+            if i == 2:
+                quant_wo(0, 512)
+                quant_wo(512, 640)
             if i == 4:
-                step_h(0, 256)
+                step_h(0, 256, nc.vector)
             if i == 6:
                 quant_h(256, 256)
             step_m(units[i])
@@ -292,18 +297,17 @@ def tile_list_bead_well_energies_kernel(tc, tab_words, tab_scales, offs, wx, wd_
                 mm_a(5)
                 mm_a(6)
                 mm_a(7)
-                quant_wo(0, 512)
-                quant_wo(512, 640)
             if i == 4:
                 quant_h(0, 256)
-                step_h(256, 256)
+                step_h(256, 256, nc.vector)
         energies(0, ())
-        step_h(512, 256)
-        step_h(768, 128)
-        quant_h(512, 256)
-        step_h(896, 128)
-        quant_h(768, 128)
         energies(1, ())
-        quant_h(896, 128)
+        step_h(512, 256, nc.vector)
+        step_h(768, 128, nc.vector)
+        quant_h(512, 256)
+        step_h(896, 128, nc.vector)
+        quant_h(768, 128)
         energies(2, ())
-        energies(3, (0,))
+        quant_h(896, 128)
+        energies(3, ())
+        energies(4, (0,))

@@ -44,24 +44,33 @@ def tile_list_bead_well_energies_kernel(tc, tab_words, tab_scales, offs, wx, wd_
         nc.gpsimd.memset(ts_all[:], 0)
         ts_i32 = tab_scales.bitcast(I32)
         for q in range(4):
-            nc.gpsimd.dma_start(ts_all[32 * q : 32 * q + 4 * PASSES, :], ts_i32[:, 4 * q : 4 * q + 4, :])
+            nc.sync.dma_start(ts_all[32 * q : 32 * q + 4 * PASSES, :], ts_i32[:, 4 * q : 4 * q + 4, :])
         ws_raw = keep.tile([P, PASSES, H // 4], I32, name="ws_raw", align_bytes=64)
         nc.vector.memset(ws_raw[:], 0)
         ts_low = [keep.tile([P, S // 4], I32, name=f"ts_low{a}", align_bytes=64) for a in range(1, PASSES)]
         for tile in ts_low:
             nc.vector.memset(tile[96:128, :], 0)
 
-        warm = keep.tile([P, 1], F32, name="warm")
-        nc.vector.memset(warm[:], 1.0)
-        warm_out = keep.tile([P, 1], F32, name="warm_out")
-        nc.scalar.activation(warm_out[:], warm[:], ACT.Abs_reciprocal_sqrt)
+        wx_raw, tab = {}, {}
 
-        wx_raw, tab = [], []
-        for a in range(PASSES):
-            tab.append(stage.tile([P, T], I32, name=f"tab{a}", tag="stage", align_bytes=64))
+        def load_tab(a):
+            tab[a] = stage.tile([P, T], I32, name=f"tab{a}", tag="stage", align_bytes=64)
             nc.sync.dma_start(tab[a][:], tab_words[a].rearrange("p t i -> p (t i)").bitcast(I32))
-            wx_raw.append(stage.tile([P, 4, H], F32, name=f"wx_raw{a}", tag="stage", align_bytes=64))
+
+        def load_wx(a):
+            wx_raw[a] = stage.tile([P, 4, H], F32, name=f"wx_raw{a}", tag="stage", align_bytes=64)
             nc.sync.dma_start(wx_raw[a][:], wx[512 * a : 512 * (a + 1), :].rearrange("(p j) c -> p j c", j=4))
+
+        load_tab(0)
+        load_wx(0)
+        warm = stage.tile([P, 1], F32, name="warm", tag="stage", align_bytes=64)
+        nc.vector.memset(warm[:], 1.0)
+        warm_out = stage.tile([P, 1], F32, name="warm_out", tag="stage", align_bytes=64)
+        nc.scalar.activation(warm_out[:], warm[:], ACT.Abs_reciprocal_sqrt)
+        load_tab(1)
+        load_wx(1)
+        load_tab(2)
+        load_wx(2)
         wd_raw = stage.tile([P, PASSES, H // 2], I32, name="wd_raw", tag="stage", align_bytes=64)
         nc.sync.dma_start(wd_raw[:], wd_words.bitcast(I32).rearrange("a p c -> p a c"))
         wo_raw = stage.tile([P, 4, N], F32, name="wo_raw", tag="stage", align_bytes=64)
@@ -74,8 +83,6 @@ def tile_list_bead_well_energies_kernel(tc, tab_words, tab_scales, offs, wx, wd_
 
         ts_pick = keep.tile([P, S // 4], I32, name="ts_pick", align_bytes=64)
         v_planes = [ts_pick] + ts_low
-        wd_codes = keep.tile([P, PASSES, H // 2], I32, name="wd_codes", align_bytes=64)
-        wd_planes = keep.tile([P, PASSES, H // 4], I32, name="wd_planes", align_bytes=64)
 
         def gather_scales():
             nc.vector.tensor_copy(ts_pick[:].bitcast(U8), ts_all[:].bitcast(U8).indirect(offsets[:]))
@@ -94,13 +101,14 @@ def tile_list_bead_well_energies_kernel(tc, tab_words, tab_scales, offs, wx, wd_
                 ws_raw[:].rearrange("p a (u t) -> p a t u", t=4),
             )
 
-        wx_bf = [swap.tile([P, 4, P * 4], BF16, name=f"wx_bf{a}", tag=tag, align_bytes=64) for a, tag in enumerate(("swap11", "wx_bf1", "swap21"))]
+        wx_bf = [swap.tile([P, 4, P * 4], BF16, name=f"wx_bf{a}", tag=tag, align_bytes=64) for a, tag in enumerate(("swap11", "wx_bf1"))]
+        wx_bf_last = [swap.tile([P, P * 4], BF16, name=f"wx_bf_last{t}", tag=tag, align_bytes=64) for t, tag in enumerate(("last0", "wd_planes", "wd_codes", "swap21"))]
         wx_codes = [keep.tile([P, H], U32, name=f"wx_codes{a}", align_bytes=64) for a in range(PASSES)]
         wx_planes = [keep.tile([P, H], U8, name=f"wx_planes{a}", align_bytes=64) for a in range(PASSES)]
         v_codes = [[None] * HALVES for a in range(PASSES)]
 
         def cast_wx(a, t, on_vector):
-            dst = wx_bf[a][:, t, :].rearrange("p (u e j) -> p u j e", e=4, j=4)
+            dst = (wx_bf_last[t][:] if a == PASSES - 1 else wx_bf[a][:, t, :]).rearrange("p (u e j) -> p u j e", e=4, j=4)
             src = wx_raw[a][:].rearrange("p j (u t e) -> p t u j e", t=4, e=4)[:, t]
             if on_vector:
                 nc.vector.tensor_copy(dst, src)
@@ -111,7 +119,7 @@ def tile_list_bead_well_energies_kernel(tc, tab_words, tab_scales, offs, wx, wd_
             nc.vector.quantize_mx(
                 out=wx_codes[a][:, P * t0 : P * t1].bitcast(FP8X4),
                 scales=wx_planes[a][:, P * t0 : P * t1],
-                in_=wx_bf[a][:, t0:t1, :].rearrange("p t c -> p (t c)"),
+                in_=wx_bf_last[t0][:] if a == PASSES - 1 else wx_bf[a][:, t0:t1, :].rearrange("p t c -> p (t c)"),
             )
 
         def gather(a, b):
@@ -162,20 +170,23 @@ def tile_list_bead_well_energies_kernel(tc, tab_words, tab_scales, offs, wx, wd_
                 quant_wx(0, 0, 4)
         gather(last, 0)
         quant_wx(1, 0, 4)
-        for a in range(last):
-            for i in range(EARLY):
-                mm_x(a, i)
-        cast_wx(last, 0, True)
-        cast_wx(last, 1, True)
+        for i in range(EARLY):
+            mm_x(0, i)
+        for i in range(4):
+            mm_x(1, i)
+        for t in range(4):
+            cast_wx(last, t, t % 2 == 0)
         for t in range(4):
             quant_wx(last, t, t + 1)
-            if t + 2 < 4:
-                cast_wx(last, t + 2, True)
             mm_x(last, t)
+        wd_planes = swap.tile([P, PASSES, H // 4], I32, name="wd_planes", tag="wd_planes", align_bytes=64)
+        wd_codes = swap.tile([P, PASSES, H // 2], I32, name="wd_codes", tag="wd_codes", align_bytes=64)
         order_wd_planes()
         for a in range(PASSES):
             order_wd_codes(a)
         gather(last, 1)
+        for i in range(4, EARLY):
+            mm_x(1, i)
         mm_a(0)
         mm_a(1)
         for i in range(4, EARLY):
@@ -284,7 +295,7 @@ def tile_list_bead_well_energies_kernel(tc, tab_words, tab_scales, offs, wx, wd_
                 quant_wo(0, 512)
                 quant_wo(512, 640)
             if i == 4:
-                step_h(0, 256, nc.vector)
+                quant_h(0, 256)
             if i == 6:
                 quant_h(256, 256)
             step_m(units[i])
@@ -297,8 +308,8 @@ def tile_list_bead_well_energies_kernel(tc, tab_words, tab_scales, offs, wx, wd_
                 mm_a(5)
                 mm_a(6)
                 mm_a(7)
+                step_h(0, 256, nc.vector)
             if i == 4:
-                quant_h(0, 256)
                 step_h(256, 256, nc.vector)
         energies(0, ())
         energies(1, ())

@@ -20,66 +20,52 @@ P = 128
 PASSES = K // 512
 HALF = 512
 HALVES = S // HALF
-EARLY = 6
-X_BANK = (0, 1, 2, 3, 4, 5, 0, 1)
-A_BANK = (6, 7, 6, 7, 2, 3, 6, 7)
-CHUNKS = ((0, 256), (256, 256), (512, 256), (768, 128), (896, 128))
-OUT_BANKS = ((4, 5, 2), (3, 0, 1), (6, 7, 4), (5, 2), (3, 0))
+UNIT = 128
+UNITS = S // UNIT
+EARLY = 7
+X_BANK = (0, 1, 2, 3, 4, 5, 6, 4)
+A_BANK = (7, 0, 7, 0, 7, 0, 7, 0)
+PICK = (512, 512, 256)
 
 
 def tile_list_bead_well_energies_kernel(tc, tab_words, tab_scales, offs, wx, wd_words, wd_scales, wo, out):
     nc = tc.nc
     with ExitStack() as ctx:
         keep = ctx.enter_context(tc.tile_pool(name="keep", bufs=1))
-        ring = ctx.enter_context(tc.tile_pool(name="ring", bufs=4))
-        stage = ctx.enter_context(tc.tile_pool(name="stage", bufs=4))
-        swap = ctx.enter_context(tc.tile_pool(name="swap", bufs=1))
-        pair = ctx.enter_context(tc.tile_pool(name="pair", bufs=2))
+        ring = ctx.enter_context(tc.tile_pool(name="ring", bufs=3))
+        stage = ctx.enter_context(tc.tile_pool(name="stage", bufs=1))
         psum = ctx.enter_context(tc.psum_pool(name="psum", bufs=1))
 
         offsets = keep.tile([P, S // 16], U16, name="offsets")
         nc.sync.dma_start(offsets[:], offs)
 
-        ts_all = swap.tile([P, T // 4], I32, name="ts_all", tag="swap10", align_bytes=64)
+        ts_all = stage.tile([P, T // 4], I32, name="ts_all", tag="slot3", align_bytes=64)
         nc.gpsimd.memset(ts_all[:], 0)
         ts_i32 = tab_scales.bitcast(I32)
         for q in range(4):
-            nc.sync.dma_start(ts_all[32 * q : 32 * q + 4 * PASSES, :], ts_i32[:, 4 * q : 4 * q + 4, :])
-        ws_raw = keep.tile([P, PASSES, H // 4], I32, name="ws_raw", align_bytes=64)
+            nc.gpsimd.dma_start(ts_all[32 * q : 32 * q + 4 * PASSES, :], ts_i32[:, 4 * q : 4 * q + 4, :])
+        ws_raw = stage.tile([P, PASSES, H // 4], I32, name="ws_raw", tag="slot4", align_bytes=64)
         nc.vector.memset(ws_raw[:], 0)
         ts_low = [keep.tile([P, S // 4], I32, name=f"ts_low{a}", align_bytes=64) for a in range(1, PASSES)]
         for tile in ts_low:
             nc.vector.memset(tile[96:128, :], 0)
+        warm = keep.tile([P, 1], F32, name="warm")
+        nc.vector.memset(warm[:], 1.0)
+        warm_out = keep.tile([P, 1], F32, name="warm_out")
+        nc.scalar.activation(warm_out[:], warm[:], ACT.Abs_reciprocal_sqrt)
+        ws_i32 = wd_scales.bitcast(I32)
+        for q in range(4):
+            nc.scalar.dma_start(ws_raw[32 * q : 32 * q + 4, :, :], ws_i32[:, 4 * q : 4 * q + 4, :].rearrange("a r c -> r a c"))
 
         wx_raw, tab = {}, {}
 
-        def load_tab(a):
-            tab[a] = stage.tile([P, T], I32, name=f"tab{a}", tag="stage", align_bytes=64)
+        def load_tab(a, slot):
+            tab[a] = stage.tile([P, T], I32, name=f"tab{a}", tag=slot, align_bytes=64)
             nc.sync.dma_start(tab[a][:], tab_words[a].rearrange("p t i -> p (t i)").bitcast(I32))
 
-        def load_wx(a):
-            wx_raw[a] = stage.tile([P, 4, H], F32, name=f"wx_raw{a}", tag="stage", align_bytes=64)
+        def load_wx(a, slot):
+            wx_raw[a] = stage.tile([P, 4, H], F32, name=f"wx_raw{a}", tag=slot, align_bytes=64)
             nc.sync.dma_start(wx_raw[a][:], wx[512 * a : 512 * (a + 1), :].rearrange("(p j) c -> p j c", j=4))
-
-        load_tab(0)
-        load_wx(0)
-        warm = stage.tile([P, 1], F32, name="warm", tag="stage", align_bytes=64)
-        nc.vector.memset(warm[:], 1.0)
-        warm_out = stage.tile([P, 1], F32, name="warm_out", tag="stage", align_bytes=64)
-        nc.scalar.activation(warm_out[:], warm[:], ACT.Abs_reciprocal_sqrt)
-        load_tab(1)
-        load_wx(1)
-        load_tab(2)
-        load_wx(2)
-        wd_raw = stage.tile([P, PASSES, H // 2], I32, name="wd_raw", tag="stage", align_bytes=64)
-        nc.sync.dma_start(wd_raw[:], wd_words.bitcast(I32).rearrange("a p c -> p a c"))
-        wo_raw = stage.tile([P, 4, N], F32, name="wo_raw", tag="stage", align_bytes=64)
-        wo_rows = wo.rearrange("(u t e) n -> e u t n", t=4, e=4)
-        for e in range(4):
-            nc.sync.dma_start(wo_raw[e:P:4, :, :], wo_rows[e])
-        ws_i32 = wd_scales.bitcast(I32)
-        for q in range(4):
-            nc.gpsimd.dma_start(ws_raw[32 * q : 32 * q + 4, :, :], ws_i32[:, 4 * q : 4 * q + 4, :].rearrange("a r c -> r a c"))
 
         ts_pick = keep.tile([P, S // 4], I32, name="ts_pick", align_bytes=64)
         v_planes = [ts_pick] + ts_low
@@ -89,11 +75,15 @@ def tile_list_bead_well_energies_kernel(tc, tab_words, tab_scales, offs, wx, wd_
             for a in range(1, PASSES):
                 nc.gpsimd.dma_start(ts_low[a - 1][0:112, :], ts_pick[4 * a : 4 * a + 112, :])
 
-        def order_wd_codes(a):
-            nc.vector.tensor_copy(
-                wd_codes[:, a, :].rearrange("p (t u k) -> p t u k", t=4, k=2),
-                wd_raw[:, a, :].rearrange("p (u t k) -> p t u k", t=4, k=2),
-            )
+        wd_planes = keep.tile([P, PASSES, H // 4], I32, name="wd_planes", align_bytes=64)
+        wd_codes = keep.tile([P, PASSES, H // 2], I32, name="wd_codes", align_bytes=64)
+
+        def order_wd_codes():
+            for a in range(PASSES):
+                nc.vector.tensor_copy(
+                    wd_codes[:, a, :].rearrange("p (t u k) -> p t u k", t=4, k=2),
+                    wd_raw[:, a, :].rearrange("p (u t k) -> p t u k", t=4, k=2),
+                )
 
         def order_wd_planes():
             nc.vector.tensor_copy(
@@ -101,105 +91,117 @@ def tile_list_bead_well_energies_kernel(tc, tab_words, tab_scales, offs, wx, wd_
                 ws_raw[:].rearrange("p a (u t) -> p a t u", t=4),
             )
 
-        wx_bf = [swap.tile([P, 4, P * 4], BF16, name=f"wx_bf{a}", tag=tag, align_bytes=64) for a, tag in enumerate(("swap11", "wx_bf1"))]
-        wx_bf_last = [swap.tile([P, P * 4], BF16, name=f"wx_bf_last{t}", tag=tag, align_bytes=64) for t, tag in enumerate(("last0", "wd_planes", "wd_codes", "swap21"))]
+        wx_bf = [[keep.tile([P, P * 4], BF16, name=f"wx_bf{a}_{t}", align_bytes=64) for t in range(4)] for a in range(PASSES)]
         wx_codes = [keep.tile([P, H], U32, name=f"wx_codes{a}", align_bytes=64) for a in range(PASSES)]
         wx_planes = [keep.tile([P, H], U8, name=f"wx_planes{a}", align_bytes=64) for a in range(PASSES)]
-        v_codes = [[None] * HALVES for a in range(PASSES)]
 
         def cast_wx(a, t, on_vector):
-            dst = (wx_bf_last[t][:] if a == PASSES - 1 else wx_bf[a][:, t, :]).rearrange("p (u e j) -> p u j e", e=4, j=4)
+            dst = wx_bf[a][t][:].rearrange("p (u e j) -> p u j e", e=4, j=4)
             src = wx_raw[a][:].rearrange("p j (u t e) -> p t u j e", t=4, e=4)[:, t]
             if on_vector:
                 nc.vector.tensor_copy(dst, src)
             else:
                 nc.scalar.copy(dst, src)
 
-        def quant_wx(a, t0, t1):
+        def quant_wx(a, t):
             nc.vector.quantize_mx(
-                out=wx_codes[a][:, P * t0 : P * t1].bitcast(FP8X4),
-                scales=wx_planes[a][:, P * t0 : P * t1],
-                in_=wx_bf_last[t0][:] if a == PASSES - 1 else wx_bf[a][:, t0:t1, :].rearrange("p t c -> p (t c)"),
+                out=wx_codes[a][:, P * t : P * (t + 1)].bitcast(FP8X4),
+                scales=wx_planes[a][:, P * t : P * (t + 1)],
+                in_=wx_bf[a][t][:],
             )
 
-        def gather(a, b):
-            cols = slice(b * HALF // 16, (b + 1) * HALF // 16)
-            v_codes[a][b] = swap.tile([P, HALF], I32, name=f"v_codes{a}_{b}", tag=f"swap{a}{b}", align_bytes=64)
-            nc.vector.tensor_copy(v_codes[a][b][:].bitcast(U32), tab[a][:].bitcast(U32).indirect(offsets[:, cols]))
+        v_codes = {}
 
-        units = [(b, t) for b in range(HALVES) for t in range(4)]
-        x_ps = {}
-        a_ps = {}
+        def gather(a):
+            width = PICK[a]
+            for b in range(S // width):
+                cols = slice(b * width // 16, (b + 1) * width // 16)
+                v_codes[a, b] = keep.tile([P, width], I32, name=f"v_codes{a}_{b}", align_bytes=64)
+                nc.vector.tensor_copy(v_codes[a, b][:].bitcast(U32), tab[a][:].bitcast(U32).indirect(offsets[:, cols]))
+
+        def v_unit(a, i):
+            b, j0 = divmod(i * UNIT, PICK[a])
+            return v_codes[a, b][:, j0 : j0 + UNIT].bitcast(FP8X4)
+
+        x_ps, a_ps = {}, {}
 
         def mm_x(a, i):
-            b, t = units[i]
             if a == 0:
-                x_ps[b, t] = psum.tile([P, HALF], F32, name=f"x{i}", tag=f"bank{X_BANK[i]}")
-            nc.tensor.matmul_mx(
-                out=x_ps[b, t][:],
-                lhsT=wx_codes[a][:, P * t : P * (t + 1)].bitcast(FP8X4),
-                lhsT_scale=wx_planes[a][:, P * t : P * (t + 1)],
-                rhs=v_codes[a][b][:].bitcast(FP8X4),
-                rhs_scale=ts_pick[:].bitcast(U8)[4 * a : P, HALF * b : HALF * (b + 1)],
-                start=(a == 0),
-                stop=(a == PASSES - 1),
-            )
-
-        def mm_a(i):
-            b, t = units[i]
-            a_ps[b, t] = psum.tile([P, HALF], F32, name=f"a{i}", tag=f"bank{A_BANK[i]}")
-            for a in range(PASSES):
+                x_ps[i] = psum.tile([P, 4, UNIT], F32, name=f"x{i}", tag=f"bank{X_BANK[i]}")
+            for t in range(4):
                 nc.tensor.matmul_mx(
-                    out=a_ps[b, t][:],
+                    out=x_ps[i][:, t, :],
+                    lhsT=wx_codes[a][:, P * t : P * (t + 1)].bitcast(FP8X4),
+                    lhsT_scale=wx_planes[a][:, P * t : P * (t + 1)],
+                    rhs=v_unit(a, i),
+                    rhs_scale=ts_pick[:].bitcast(U8)[4 * a : P, UNIT * i : UNIT * (i + 1)],
+                    start=(a == 0 and t == 0),
+                    stop=(a == PASSES - 1 and t == 3),
+                )
+
+        def mm_a(a, i):
+            if a == 0:
+                a_ps[i] = psum.tile([P, 4, UNIT], F32, name=f"a{i}", tag=f"bank{A_BANK[i]}")
+            for t in range(4):
+                nc.tensor.matmul_mx(
+                    out=a_ps[i][:, t, :],
                     lhsT=wd_codes[:, a, 64 * t : 64 * (t + 1)].bitcast(U8).bitcast(FP4X4),
                     lhsT_scale=wd_planes[:, a, 32 * t : 32 * (t + 1)].bitcast(U8),
-                    rhs=v_codes[a][b][:].bitcast(FP8X4),
-                    rhs_scale=v_planes[a][:].bitcast(U8)[:, HALF * b : HALF * (b + 1)],
-                    start=(a == 0),
-                    stop=(a == PASSES - 1),
+                    rhs=v_unit(a, i),
+                    rhs_scale=v_planes[a][:].bitcast(U8)[:, UNIT * i : UNIT * (i + 1)],
+                    start=(a == 0 and t == 0),
+                    stop=(a == PASSES - 1 and t == 3),
                 )
 
         last = PASSES - 1
-        for a in range(last):
-            for t in range(4):
-                cast_wx(a, t, False)
-            gather(a, 0)
-            gather(a, 1)
-            if a == 0:
-                gather_scales()
-                quant_wx(0, 0, 4)
-        gather(last, 0)
-        quant_wx(1, 0, 4)
+        load_tab(0, "slot0")
+        load_wx(0, "slot1")
+        load_wx(1, "slot2")
+        gather(0)
+        gather_scales()
+        load_tab(1, "slot0")
+        for t in range(4):
+            cast_wx(0, t, False)
+            quant_wx(0, t)
+        load_wx(2, "slot1")
+        order_wd_planes()
         for i in range(EARLY):
             mm_x(0, i)
-        for i in range(4):
+        for t in range(4):
+            cast_wx(1, t, False)
+            quant_wx(1, t)
+        load_tab(2, "slot3")
+        wd_raw = stage.tile([P, PASSES, H // 2], I32, name="wd_raw", tag="slot4", align_bytes=64)
+        nc.sync.dma_start(wd_raw[:], wd_words.bitcast(I32).rearrange("a p c -> p a c"))
+        gather(1)
+        for i in range(EARLY):
             mm_x(1, i)
         for t in range(4):
-            cast_wx(last, t, t % 2 == 0)
+            cast_wx(last, t, t < 2)
+            quant_wx(last, t)
+        wo_raw = stage.tile([P, 4, N], F32, name="wo_raw", tag="slot2", align_bytes=64)
+        wo_rows = wo.rearrange("(u t e) n -> t u e n", t=4, e=4)
         for t in range(4):
-            quant_wx(last, t, t + 1)
-            mm_x(last, t)
-        wd_planes = swap.tile([P, PASSES, H // 4], I32, name="wd_planes", tag="wd_planes", align_bytes=64)
-        wd_codes = swap.tile([P, PASSES, H // 2], I32, name="wd_codes", tag="wd_codes", align_bytes=64)
-        order_wd_planes()
-        for a in range(PASSES):
-            order_wd_codes(a)
-        gather(last, 1)
-        for i in range(4, EARLY):
-            mm_x(1, i)
-        mm_a(0)
-        mm_a(1)
-        for i in range(4, EARLY):
+            nc.sync.dma_start(wo_raw[:, t, :], wo_rows[t])
+        gather(last)
+        order_wd_codes()
+        for i in range(EARLY):
             mm_x(last, i)
+            if i == 3:
+                for a in range(PASSES):
+                    mm_a(a, 0)
 
         wo_bf = keep.tile([P, N, 4], BF16, name="wo_bf", align_bytes=64)
         wo_codes = keep.tile([P, N], U32, name="wo_codes", align_bytes=64)
         wo_planes = keep.tile([P, N], U8, name="wo_planes", align_bytes=64)
         for n in range(N // P):
             cols = slice(P * n, P * (n + 1))
-            nc.gpsimd.tensor_scalar(
-                wo_bf[:, cols, :], wo_raw[:, :, cols].rearrange("p t n -> p n t"), 1.0, 0.0, ALU.mult, ALU.add
-            )
+            dst = wo_bf[:, cols, :].rearrange("p (c i) t -> p c t i", i=4)
+            src = wo_raw[:, :, cols].rearrange("p t (c i) -> p c t i", i=4)
+            if True:
+                nc.vector.tensor_copy(dst, src)
+            else:
+                nc.scalar.copy(dst, src)
 
         def quant_wo(n0, n1):
             nc.vector.quantize_mx(
@@ -208,117 +210,78 @@ def tile_list_bead_well_energies_kernel(tc, tab_words, tab_scales, offs, wx, wd_
                 in_=wo_bf[:, n0:n1, :].rearrange("p n t -> p (n t)"),
             )
 
-        s_sb, w_sb, q_sb, p_sb, m_sb = {}, {}, {}, {}, {}
-
-        def step_s(u):
-            s_sb[u] = ring.tile([P, HALF], F32, name="s_sb")
-            nc.scalar.activation(s_sb[u][:], x_ps[u][:], ACT.Square)
-
-        def step_w(u):
-            w_sb[u] = ring.tile([P, HALF], F32, name="w_sb")
-            nc.scalar.activation(w_sb[u][:], s_sb[u][:], ACT.Abs_reciprocal_sqrt, bias=1.0)
-
-        def step_q(u):
-            q_sb[u] = ring.tile([P, HALF], F32, name="q_sb")
-            nc.scalar.activation(q_sb[u][:], w_sb[u][:], ACT.Square)
-
-        def step_p(u):
-            b, t = u
-            if t == 0:
-                p_sb[b] = pair.tile([P, 4, HALF], F32, name="p_sb")
-            nc.vector.tensor_tensor(p_sb[b][:, t, :], x_ps[u][:], q_sb[u][:], ALU.mult)
-
-        def step_m(u):
-            b, t = u
-            if t == 0:
-                m_sb[b] = pair.tile([P, 4, HALF], F32, name="m_sb")
-            nc.vector.tensor_tensor(m_sb[b][:, t, :], a_ps[u][:], p_sb[b][:, t, :], ALU.mult)
-
-        h_bf = keep.tile([P, S, 4], BF16, name="h_bf", align_bytes=64)
         h_codes = keep.tile([P, S], U32, name="h_codes", align_bytes=64)
         h_planes = keep.tile([P, S], U8, name="h_planes", align_bytes=64)
 
-        def step_h(j0, width, engine):
-            b = j0 // HALF
-            cols = slice(j0 - HALF * b, j0 - HALF * b + width)
-            engine.tensor_tensor(
-                h_bf[:, j0 : j0 + width, :].rearrange("p (c i) t -> p c t i", i=4),
-                m_sb[b][:, :, cols].rearrange("p t (c i) -> p c t i", i=4),
-                p_sb[b][:, :, cols].rearrange("p t (c i) -> p c t i", i=4),
-                ALU.mult,
-            )
+        q_sb, pp_sb, h_bf = {}, {}, {}
 
-        def quant_h(j0, width):
-            cols = slice(j0, j0 + width)
-            nc.vector.quantize_mx(
-                out=h_codes[:, cols].bitcast(FP8X4),
-                scales=h_planes[:, cols],
-                in_=h_bf[:, cols, :].rearrange("p j t -> p (j t)"),
-            )
+        def shape(i):
+            x_jt = x_ps[i][:].rearrange("p t j -> p j t")
+            s_sb = ring.tile([P, UNIT, 4], F32, name="s_sb")
+            nc.scalar.activation(s_sb[:], x_jt, ACT.Square)
+            w_sb = ring.tile([P, UNIT, 4], F32, name="w_sb")
+            nc.scalar.activation(w_sb[:], s_sb[:], ACT.Abs_reciprocal_sqrt, bias=1.0)
+            q_sb[i] = stage.tile([P, UNIT, 4], F32, name=f"q_sb{i}", tag=f"q{i}", align_bytes=64)
+            if i < 1:
+                nc.vector.tensor_tensor(q_sb[i][:], w_sb[:], w_sb[:], ALU.mult)
+            else:
+                nc.scalar.activation(q_sb[i][:], w_sb[:], ACT.Square)
+            p_sb = ring.tile([P, UNIT, 4], F32, name="p_sb")
+            nc.vector.tensor_tensor(p_sb[:], x_jt, q_sb[i][:], ALU.mult)
+            pp_sb[i] = ring.tile([P, UNIT, 4], F32, name="pp_sb")
+            if 1 <= i < UNITS - 1:
+                nc.gpsimd.tensor_tensor(pp_sb[i][:], p_sb[:], p_sb[:], ALU.mult)
+            else:
+                nc.scalar.activation(pp_sb[i][:], p_sb[:], ACT.Square)
+
+        def depth(i):
+            h_bf[i] = stage.tile([P, UNIT, 4], BF16, name=f"h_bf{i}", tag=f"q{i + 1}", align_bytes=64)
+            nc.vector.tensor_tensor(h_bf[i][:], a_ps[i][:].rearrange("p t j -> p j t"), pp_sb[i][:], ALU.mult)
 
         out_tiles = out.rearrange("(n p) j -> p n j", p=P)
 
-        def energies(c, on_vector):
-            j0, width = CHUNKS[c]
-            per_bank = HALF // width
-            for g, bank in enumerate(OUT_BANKS[c]):
-                n0 = g * per_bank
-                count = min(per_bank, N // P - n0)
-                acc = psum.tile([P, count, width], F32, name=f"o{c}_{g}", tag=f"bank{bank}")
+        def energies(i, parts):
+            cols = slice(UNIT * i, UNIT * (i + 1))
+            nc.vector.quantize_mx(
+                out=h_codes[:, cols].bitcast(FP8X4),
+                scales=h_planes[:, cols],
+                in_=h_bf[i][:].rearrange("p j t -> p (j t)"),
+            )
+            res = keep.tile([P, N // P, UNIT], F32, name=f"res{i}")
+            for n0, count, bank, on_vector in parts:
+                acc = psum.tile([P, count, UNIT], F32, name=f"o{i}_{n0}", tag=f"bank{bank}")
                 for n in range(count):
-                    cols = slice(P * (n0 + n), P * (n0 + n + 1))
+                    rows = slice(P * (n0 + n), P * (n0 + n + 1))
                     nc.tensor.matmul_mx(
                         out=acc[:, n, :],
-                        lhsT=wo_codes[:, cols].bitcast(FP8X4),
-                        lhsT_scale=wo_planes[:, cols],
-                        rhs=h_codes[:, j0 : j0 + width].bitcast(FP8X4),
-                        rhs_scale=h_planes[:, j0 : j0 + width],
+                        lhsT=wo_codes[:, rows].bitcast(FP8X4),
+                        lhsT_scale=wo_planes[:, rows],
+                        rhs=h_codes[:, cols].bitcast(FP8X4),
+                        rhs_scale=h_planes[:, cols],
                         start=True,
                         stop=True,
                     )
-                res = keep.tile([P, count, width], F32, name=f"res{c}_{g}")
-                if g in on_vector:
-                    nc.vector.tensor_copy(res[:], acc[:])
+                if on_vector:
+                    nc.vector.tensor_copy(res[:, n0 : n0 + count, :], acc[:])
                 else:
-                    nc.scalar.copy(res[:], acc[:])
-                nc.sync.dma_start(out_tiles[:, n0 : n0 + count, j0 : j0 + width], res[:])
+                    nc.scalar.copy(res[:, n0 : n0 + count, :], acc[:])
+            nc.sync.dma_start(out_tiles[:, :, cols], res[:])
 
-        for i in range(0, len(units), 2):
-            for step in (step_s, step_w, step_q, step_p):
-                step(units[i])
-                step(units[i + 1])
-            if i == 0:
-                for k in range(EARLY, len(units)):
-                    for a in range(PASSES):
-                        mm_x(a, k)
-            if i == 2:
+        for i in range(UNITS + 1):
+            if i < UNITS:
+                shape(i)
+            if i == 4:
+                for a in range(PASSES):
+                    mm_x(a, UNITS - 1)
+            if i > 0:
+                depth(i - 1)
+            if i + 1 < UNITS:
+                for a in range(PASSES):
+                    mm_a(a, i + 1)
+            if i == 1:
                 quant_wo(0, 512)
                 quant_wo(512, 640)
-            if i == 4:
-                quant_h(0, 256)
-            if i == 6:
-                quant_h(256, 256)
-            step_m(units[i])
-            step_m(units[i + 1])
-            if i == 0:
-                mm_a(2)
-                mm_a(3)
-            if i == 2:
-                mm_a(4)
-                mm_a(5)
-                mm_a(6)
-                mm_a(7)
-                step_h(0, 256, nc.vector)
-            if i == 4:
-                step_h(256, 256, nc.vector)
-        energies(0, ())
-        energies(1, ())
-        step_h(512, 256, nc.vector)
-        step_h(768, 128, nc.vector)
-        quant_h(512, 256)
-        step_h(896, 128, nc.vector)
-        quant_h(768, 128)
-        energies(2, ())
-        quant_h(896, 128)
-        energies(3, ())
-        energies(4, (0,))
+            if i >= 2:
+                nv = 3
+                energies(i - 2, ((0, nv, 2 + i % 2, True), (nv, 5 - nv, 1, False)))
+        energies(UNITS - 1, ((0, 3, 5, True), (3, 2, 6, False)))

@@ -72,8 +72,6 @@ def tile_list_bead_well_energies_kernel(tc, tab_words, tab_scales, offs, wx, wd_
 
         def gather_scales():
             nc.vector.tensor_copy(ts_pick[:].bitcast(U8), ts_all[:].bitcast(U8).indirect(offsets[:]))
-            for a in range(1, PASSES):
-                nc.gpsimd.dma_start(ts_low[a - 1][0:112, :], ts_pick[4 * a : 4 * a + 112, :])
 
         wd_planes = keep.tile([P, PASSES, H // 4], I32, name="wd_planes", align_bytes=64)
         wd_codes = keep.tile([P, PASSES, H // 2], I32, name="wd_codes", align_bytes=64)
@@ -173,6 +171,8 @@ def tile_list_bead_well_energies_kernel(tc, tab_words, tab_scales, offs, wx, wd_
         load_tab(2, "slot3")
         wd_raw = stage.tile([P, PASSES, H // 2], I32, name="wd_raw", tag="slot4", align_bytes=64)
         nc.sync.dma_start(wd_raw[:], wd_words.bitcast(I32).rearrange("a p c -> p a c"))
+        for a in range(1, PASSES):
+            nc.sync.dma_start(ts_low[a - 1][0:112, :], ts_pick[4 * a : 4 * a + 112, :])
         gather(1)
         for i in range(EARLY):
             mm_x(1, i)

@@ -23,8 +23,10 @@ HALVES = S // HALF
 UNIT = 128
 UNITS = S // UNIT
 EARLY = 7
-X_BANK = (0, 1, 2, 3, 4, 5, 6, 4)
+X_BANK = (0, 1, 2, 3, 4, 5, 6, 1)
 A_BANK = (7, 0, 7, 0, 7, 0, 7, 0)
+LAG = 1
+NEAR = 3
 PICK = (512, 512, 256)
 
 
@@ -32,7 +34,7 @@ def tile_list_bead_well_energies_kernel(tc, tab_words, tab_scales, offs, wx, wd_
     nc = tc.nc
     with ExitStack() as ctx:
         keep = ctx.enter_context(tc.tile_pool(name="keep", bufs=1))
-        ring = ctx.enter_context(tc.tile_pool(name="ring", bufs=3))
+        ring = ctx.enter_context(tc.tile_pool(name="ring", bufs=4))
         stage = ctx.enter_context(tc.tile_pool(name="stage", bufs=1))
         psum = ctx.enter_context(tc.psum_pool(name="psum", bufs=1))
 
@@ -194,25 +196,31 @@ def tile_list_bead_well_energies_kernel(tc, tab_words, tab_scales, offs, wx, wd_
         wo_bf = keep.tile([P, N, 4], BF16, name="wo_bf", align_bytes=64)
         wo_codes = keep.tile([P, N], U32, name="wo_codes", align_bytes=64)
         wo_planes = keep.tile([P, N], U8, name="wo_planes", align_bytes=64)
-        for n in range(N // P):
+
+        def cast_wo(n, engine):
             cols = slice(P * n, P * (n + 1))
+            if engine == "gpsimd":
+                nc.gpsimd.tensor_scalar(
+                    wo_bf[:, cols, :], wo_raw[:, :, cols].rearrange("p t n -> p n t"), 1.0, 0.0, ALU.mult, ALU.add
+                )
+                return
             dst = wo_bf[:, cols, :].rearrange("p (c i) t -> p c t i", i=4)
             src = wo_raw[:, :, cols].rearrange("p t (c i) -> p c t i", i=4)
-            if True:
+            if engine == "vector":
                 nc.vector.tensor_copy(dst, src)
             else:
                 nc.scalar.copy(dst, src)
 
-        def quant_wo(n0, n1):
+        def quant_wo(n):
+            cols = slice(P * n, P * (n + 1))
             nc.vector.quantize_mx(
-                out=wo_codes[:, n0:n1].bitcast(FP8X4),
-                scales=wo_planes[:, n0:n1],
-                in_=wo_bf[:, n0:n1, :].rearrange("p n t -> p (n t)"),
+                out=wo_codes[:, cols].bitcast(FP8X4),
+                scales=wo_planes[:, cols],
+                in_=wo_bf[:, cols, :].rearrange("p n t -> p (n t)"),
             )
 
         h_codes = keep.tile([P, S], U32, name="h_codes", align_bytes=64)
         h_planes = keep.tile([P, S], U8, name="h_planes", align_bytes=64)
-
         q_sb, pp_sb, h_bf = {}, {}, {}
 
         def shape(i):
@@ -224,64 +232,91 @@ def tile_list_bead_well_energies_kernel(tc, tab_words, tab_scales, offs, wx, wd_
             q_sb[i] = stage.tile([P, UNIT, 4], F32, name=f"q_sb{i}", tag=f"q{i}", align_bytes=64)
             if i < 1:
                 nc.vector.tensor_tensor(q_sb[i][:], w_sb[:], w_sb[:], ALU.mult)
+            elif i < 0:
+                nc.gpsimd.tensor_tensor(q_sb[i][:], w_sb[:], w_sb[:], ALU.mult)
             else:
                 nc.scalar.activation(q_sb[i][:], w_sb[:], ACT.Square)
             p_sb = ring.tile([P, UNIT, 4], F32, name="p_sb")
             nc.vector.tensor_tensor(p_sb[:], x_jt, q_sb[i][:], ALU.mult)
             pp_sb[i] = ring.tile([P, UNIT, 4], F32, name="pp_sb")
-            if 1 <= i < UNITS - 1:
+            if i<0:
                 nc.gpsimd.tensor_tensor(pp_sb[i][:], p_sb[:], p_sb[:], ALU.mult)
+            elif i<7:
+                nc.vector.tensor_tensor(pp_sb[i][:], p_sb[:], p_sb[:], ALU.mult)
             else:
                 nc.scalar.activation(pp_sb[i][:], p_sb[:], ACT.Square)
 
         def depth(i):
-            h_bf[i] = stage.tile([P, UNIT, 4], BF16, name=f"h_bf{i}", tag=f"q{i + 1}", align_bytes=64)
+            h_bf[i] = stage.tile([P, UNIT, 4], BF16, name=f"h_bf{i}", tag=f"q{i + 9}", align_bytes=64)
             nc.vector.tensor_tensor(h_bf[i][:], a_ps[i][:].rearrange("p t j -> p j t"), pp_sb[i][:], ALU.mult)
 
-        out_tiles = out.rearrange("(n p) j -> p n j", p=P)
-
-        def energies(i, parts):
+        def quant_h(i):
             cols = slice(UNIT * i, UNIT * (i + 1))
             nc.vector.quantize_mx(
                 out=h_codes[:, cols].bitcast(FP8X4),
                 scales=h_planes[:, cols],
                 in_=h_bf[i][:].rearrange("p j t -> p (j t)"),
             )
-            res = keep.tile([P, N // P, UNIT], F32, name=f"res{i}")
-            for n0, count, bank, on_vector in parts:
-                acc = psum.tile([P, count, UNIT], F32, name=f"o{i}_{n0}", tag=f"bank{bank}")
-                for n in range(count):
-                    rows = slice(P * (n0 + n), P * (n0 + n + 1))
-                    nc.tensor.matmul_mx(
-                        out=acc[:, n, :],
-                        lhsT=wo_codes[:, rows].bitcast(FP8X4),
-                        lhsT_scale=wo_planes[:, rows],
-                        rhs=h_codes[:, cols].bitcast(FP8X4),
-                        rhs_scale=h_planes[:, cols],
-                        start=True,
-                        stop=True,
-                    )
-                if on_vector:
-                    nc.vector.tensor_copy(res[:, n0 : n0 + count, :], acc[:])
-                else:
-                    nc.scalar.copy(res[:, n0 : n0 + count, :], acc[:])
-            nc.sync.dma_start(out_tiles[:, :, cols], res[:])
 
-        for i in range(UNITS + 1):
+        out_tiles = out.rearrange("(n p) j -> p n j", p=P)
+
+        def energies(j0, width, n0, count, bank, on_vector):
+            cols = slice(j0, j0 + width)
+            acc = psum.tile([P, count, width], F32, name=f"o{j0}_{n0}", tag=f"bank{bank}")
+            for n in range(count):
+                rows = slice(P * (n0 + n), P * (n0 + n + 1))
+                nc.tensor.matmul_mx(
+                    out=acc[:, n, :],
+                    lhsT=wo_codes[:, rows].bitcast(FP8X4),
+                    lhsT_scale=wo_planes[:, rows],
+                    rhs=h_codes[:, cols].bitcast(FP8X4),
+                    rhs_scale=h_planes[:, cols],
+                    start=True,
+                    stop=True,
+                )
+            res = keep.tile([P, count, width], F32, name=f"res{j0}_{n0}")
+            if on_vector:
+                nc.vector.tensor_copy(res[:], acc[:])
+            else:
+                nc.scalar.copy(res[:], acc[:])
+            nc.sync.dma_start(out_tiles[:, n0 : n0 + count, cols], res[:])
+
+        def far(j0):
+            energies(j0, 2 * UNIT, 2, 2, 3, False)
+            energies(j0, 2 * UNIT, 4, 1, 4 + (j0 // 256) % 2, False)
+
+        for i in range(UNITS + LAG):
             if i < UNITS:
                 shape(i)
-            if i == 4:
+            if i == 1:
                 for a in range(PASSES):
                     mm_x(a, UNITS - 1)
-            if i > 0:
-                depth(i - 1)
-            if i + 1 < UNITS:
+            if i == 0:
                 for a in range(PASSES):
-                    mm_a(a, i + 1)
-            if i == 1:
-                quant_wo(0, 512)
-                quant_wo(512, 640)
-            if i >= 2:
-                nv = 3
-                energies(i - 2, ((0, nv, 2 + i % 2, True), (nv, 5 - nv, 1, False)))
-        energies(UNITS - 1, ((0, 3, 5, True), (3, 2, 6, False)))
+                    mm_a(a, 1)
+            for n in range(N // P):
+                if i == (0,0,0,0,0)[n]:
+                    cast_wo(n, "vector")
+                if i == (0,0,0,0,0)[n] + 1:
+                    quant_wo(n)
+            k = i - LAG
+            if k > 0:
+                quant_h(k - 1)
+            if k < 0:
+                continue
+            depth(k)
+            if k + 2 < UNITS:
+                for a in range(PASSES):
+                    mm_a(a, k + 2)
+            if k in (2, 4, 6):
+                energies(UNIT * (k - 2), 2 * UNIT, 0, 2, 2, False)
+            if k - 0 in (2, 4, 6):
+                far(UNIT * (k - 0 - 2))
+        for kk in (2, 4, 6):
+            if kk + 0 > UNITS - 1:
+                far(UNIT * (kk - 2))
+        quant_h(UNITS - 1)
+        energies(768, UNIT, 0, 4, 6, False)
+        energies(768, UNIT, 4, 1, 1, False)
+        energies(896, UNIT, 0, 3, 7, True)
+        energies(896, UNIT, 3, 2, 0, False)

@@ -41,7 +41,7 @@ def tile_list_bead_well_energies_kernel(tc, tab_words, tab_scales, offs, wx, wd_
         offsets = keep.tile([P, S // 16], U16, name="offsets")
         nc.sync.dma_start(offsets[:], offs)
 
-        ts_all = stage.tile([P, T // 4], I32, name="ts_all", tag="slot3", align_bytes=64)
+        ts_all = keep.tile([P, T // 4], I32, name="ts_all", align_bytes=64)
         nc.gpsimd.memset(ts_all[:], 0)
         ts_i32 = tab_scales.bitcast(I32)
         for q in range(4):
@@ -69,12 +69,6 @@ def tile_list_bead_well_energies_kernel(tc, tab_words, tab_scales, offs, wx, wd_
             wx_raw[a] = stage.tile([P, 4, H], F32, name=f"wx_raw{a}", tag=slot, align_bytes=64)
             nc.sync.dma_start(wx_raw[a][:], wx[512 * a : 512 * (a + 1), :].rearrange("(p j) c -> p j c", j=4))
 
-        ts_pick = keep.tile([P, S // 4], I32, name="ts_pick", align_bytes=64)
-        v_planes = [ts_pick] + ts_low
-
-        def gather_scales():
-            nc.vector.tensor_copy(ts_pick[:].bitcast(U8), ts_all[:].bitcast(U8).indirect(offsets[:]))
-
         wd_planes = keep.tile([P, PASSES, H // 4], I32, name="wd_planes", align_bytes=64)
         wd_codes = keep.tile([P, PASSES, H // 2], I32, name="wd_codes", align_bytes=64)
 
@@ -91,7 +85,7 @@ def tile_list_bead_well_energies_kernel(tc, tab_words, tab_scales, offs, wx, wd_
                 ws_raw[:].rearrange("p a (u t) -> p a t u", t=4),
             )
 
-        wx_bf = [[keep.tile([P, P * 4], BF16, name=f"wx_bf{a}_{t}", align_bytes=64) for t in range(4)] for a in range(PASSES)]
+        wx_bf = [[stage.tile([P, P * 4], BF16, name=f"wx_bf{a}_{t}", tag=f"wxbf{a}{t}", align_bytes=64) for t in range(4)] for a in range(PASSES)]
         wx_codes = [keep.tile([P, H], U32, name=f"wx_codes{a}", align_bytes=64) for a in range(PASSES)]
         wx_planes = [keep.tile([P, H], U8, name=f"wx_planes{a}", align_bytes=64) for a in range(PASSES)]
 
@@ -155,36 +149,37 @@ def tile_list_bead_well_energies_kernel(tc, tab_words, tab_scales, offs, wx, wd_
 
         last = PASSES - 1
         load_tab(0, "slot0")
-        load_wx(0, "slot1")
-        load_wx(1, "slot2")
+        load_tab(1, "slot1")
+        load_wx(0, "slot2")
+        load_wx(1, "slot3")
         gather(0)
-        gather_scales()
-        load_tab(1, "slot0")
-        for t in range(4):
-            cast_wx(0, t, False)
-            quant_wx(0, t)
-        load_wx(2, "slot1")
-        order_wd_planes()
-        for i in range(EARLY):
-            mm_x(0, i)
-        for t in range(4):
-            cast_wx(1, t, False)
-            quant_wx(1, t)
-        load_tab(2, "slot3")
-        wd_raw = stage.tile([P, PASSES, H // 2], I32, name="wd_raw", tag="slot4", align_bytes=64)
-        nc.sync.dma_start(wd_raw[:], wd_words.bitcast(I32).rearrange("a p c -> p a c"))
-        for a in range(1, PASSES):
-            nc.sync.dma_start(ts_low[a - 1][0:112, :], ts_pick[4 * a : 4 * a + 112, :])
+        load_wx(2, "slot0")
+        load_tab(2, "slot5")
         gather(1)
-        for i in range(EARLY):
-            mm_x(1, i)
-        for t in range(4):
-            cast_wx(last, t, t < 2)
-            quant_wx(last, t)
+        order_wd_planes()
+        for a in range(PASSES):
+            for t in range(4):
+                cast_wx(a, t, t < (2,0,2)[a])
+                quant_wx(a, t)
+            if a == 0:
+                ts_pick = stage.tile([P, S // 4], I32, name="ts_pick", tag="wxbf01", align_bytes=64)
+                v_planes = [ts_pick] + ts_low
+                for b in range(2):
+                    nc.vector.tensor_copy(
+                        ts_pick[:].bitcast(U8)[:, HALF * b : HALF * (b + 1)],
+                        ts_all[:].bitcast(U8).indirect(offsets[:, 32 * b : 32 * (b + 1)]),
+                    )
+                for c in range(1, PASSES):
+                    nc.gpsimd.dma_start(ts_low[c - 1][0:112, :], ts_pick[4 * c : 4 * c + 112, :])
+            if a < last:
+                for i in range(EARLY):
+                    mm_x(a, i)
         wo_raw = stage.tile([P, 4, N], F32, name="wo_raw", tag="slot2", align_bytes=64)
         wo_rows = wo.rearrange("(u t e) n -> t u e n", t=4, e=4)
         for t in range(4):
             nc.sync.dma_start(wo_raw[:, t, :], wo_rows[t])
+        wd_raw = stage.tile([P, PASSES, H // 2], I32, name="wd_raw", tag="slot4", align_bytes=64)
+        nc.sync.dma_start(wd_raw[:], wd_words.bitcast(I32).rearrange("a p c -> p a c"))
         gather(last)
         order_wd_codes()
         for i in range(EARLY):
@@ -230,13 +225,13 @@ def tile_list_bead_well_energies_kernel(tc, tab_words, tab_scales, offs, wx, wd_
             w_sb = ring.tile([P, UNIT, 4], F32, name="w_sb")
             nc.scalar.activation(w_sb[:], s_sb[:], ACT.Abs_reciprocal_sqrt, bias=1.0)
             q_sb[i] = stage.tile([P, UNIT, 4], F32, name=f"q_sb{i}", tag=f"q{i}", align_bytes=64)
-            if i < 1:
+            if i<0:
                 nc.vector.tensor_tensor(q_sb[i][:], w_sb[:], w_sb[:], ALU.mult)
             elif i < 0:
                 nc.gpsimd.tensor_tensor(q_sb[i][:], w_sb[:], w_sb[:], ALU.mult)
             else:
                 nc.scalar.activation(q_sb[i][:], w_sb[:], ACT.Square)
-            p_sb = ring.tile([P, UNIT, 4], F32, name="p_sb")
+            p_sb = stage.tile([P, UNIT, 4], F32, name=f"p_sb{i}", tag=f"p{i % 3}" if i else "slot4", align_bytes=64)
             nc.vector.tensor_tensor(p_sb[:], x_jt, q_sb[i][:], ALU.mult)
             pp_sb[i] = ring.tile([P, UNIT, 4], F32, name="pp_sb")
             if i<0:
@@ -285,6 +280,9 @@ def tile_list_bead_well_energies_kernel(tc, tab_words, tab_scales, offs, wx, wd_
             energies(j0, 2 * UNIT, 2, 2, 3, False)
             energies(j0, 2 * UNIT, 4, 1, 4 + (j0 // 256) % 2, False)
 
+        for n in range(N // P):
+            cast_wo(n, "vector")
+            quant_wo(n)
         for i in range(UNITS + LAG):
             if i < UNITS:
                 shape(i)
@@ -294,11 +292,6 @@ def tile_list_bead_well_energies_kernel(tc, tab_words, tab_scales, offs, wx, wd_
             if i == 0:
                 for a in range(PASSES):
                     mm_a(a, 1)
-            for n in range(N // P):
-                if i == (0,0,0,0,0)[n]:
-                    cast_wo(n, "vector")
-                if i == (0,0,0,0,0)[n] + 1:
-                    quant_wo(n)
             k = i - LAG
             if k > 0:
                 quant_h(k - 1)

@@ -46,7 +46,7 @@ def tile_list_bead_well_energies_kernel(tc, tab_words, tab_scales, offs, wx, wd_
         ts_i32 = tab_scales.bitcast(I32)
         for q in range(4):
             nc.gpsimd.dma_start(ts_all[32 * q : 32 * q + 4 * PASSES, :], ts_i32[:, 4 * q : 4 * q + 4, :])
-        ws_raw = stage.tile([P, PASSES, H // 4], I32, name="ws_raw", tag="slot4", align_bytes=64)
+        ws_raw = keep.tile([P, PASSES, H // 4], I32, name="ws_raw", align_bytes=64)
         nc.vector.memset(ws_raw[:], 0)
         ts_low = [keep.tile([P, S // 4], I32, name=f"ts_low{a}", align_bytes=64) for a in range(1, PASSES)]
         for tile in ts_low:
@@ -69,7 +69,6 @@ def tile_list_bead_well_energies_kernel(tc, tab_words, tab_scales, offs, wx, wd_
             wx_raw[a] = stage.tile([P, 4, H], F32, name=f"wx_raw{a}", tag=slot, align_bytes=64)
             nc.sync.dma_start(wx_raw[a][:], wx[512 * a : 512 * (a + 1), :].rearrange("(p j) c -> p j c", j=4))
 
-        wd_planes = keep.tile([P, PASSES, H // 4], I32, name="wd_planes", align_bytes=64)
         wd_codes = keep.tile([P, PASSES, H // 2], I32, name="wd_codes", align_bytes=64)
 
         def order_wd_codes():
@@ -156,7 +155,6 @@ def tile_list_bead_well_energies_kernel(tc, tab_words, tab_scales, offs, wx, wd_
         load_wx(2, "slot0")
         load_tab(2, "slot5")
         gather(1)
-        order_wd_planes()
         for a in range(PASSES):
             for t in range(4):
                 cast_wx(a, t, t < (2,0,2)[a])
@@ -181,6 +179,8 @@ def tile_list_bead_well_energies_kernel(tc, tab_words, tab_scales, offs, wx, wd_
         wd_raw = stage.tile([P, PASSES, H // 2], I32, name="wd_raw", tag="slot4", align_bytes=64)
         nc.sync.dma_start(wd_raw[:], wd_words.bitcast(I32).rearrange("a p c -> p a c"))
         gather(last)
+        wd_planes = stage.tile([P, PASSES, H // 4], I32, name="wd_planes", tag="wxbf13", align_bytes=64)
+        order_wd_planes()
         order_wd_codes()
         for i in range(EARLY):
             mm_x(last, i)
@@ -236,7 +236,7 @@ def tile_list_bead_well_energies_kernel(tc, tab_words, tab_scales, offs, wx, wd_
             pp_sb[i] = ring.tile([P, UNIT, 4], F32, name="pp_sb")
             if i<0:
                 nc.gpsimd.tensor_tensor(pp_sb[i][:], p_sb[:], p_sb[:], ALU.mult)
-            elif i<7:
+            elif i<6:
                 nc.vector.tensor_tensor(pp_sb[i][:], p_sb[:], p_sb[:], ALU.mult)
             else:
                 nc.scalar.activation(pp_sb[i][:], p_sb[:], ACT.Square)
@@ -276,14 +276,15 @@ def tile_list_bead_well_energies_kernel(tc, tab_words, tab_scales, offs, wx, wd_
                 nc.scalar.copy(res[:], acc[:])
             nc.sync.dma_start(out_tiles[:, n0 : n0 + count, cols], res[:])
 
-        def far(j0):
-            energies(j0, 2 * UNIT, 2, 2, 3, False)
-            energies(j0, 2 * UNIT, 4, 1, 4 + (j0 // 256) % 2, False)
+        def unit_out(k):
+            near = 3
+            energies(UNIT * k, UNIT, 0, near, 2 if k < 5 else 2 + 2 * (k % 2), k == 7)
+            energies(UNIT * k, UNIT, near, N // P - near, 3 if k < 5 else 3 + 2 * (k % 2), False)
 
         for n in range(N // P):
             cast_wo(n, "vector")
             quant_wo(n)
-        for i in range(UNITS + LAG):
+        for i in range(UNITS + 1):
             if i < UNITS:
                 shape(i)
             if i == 1:
@@ -292,24 +293,16 @@ def tile_list_bead_well_energies_kernel(tc, tab_words, tab_scales, offs, wx, wd_
             if i == 0:
                 for a in range(PASSES):
                     mm_a(a, 1)
-            k = i - LAG
-            if k > 0:
-                quant_h(k - 1)
-            if k < 0:
                 continue
-            depth(k)
-            if k + 2 < UNITS:
+            if i >= 2:
+                quant_h(i - 2)
+            depth(i - 1)
+            if i + 1 < UNITS:
                 for a in range(PASSES):
-                    mm_a(a, k + 2)
-            if k in (2, 4, 6):
-                energies(UNIT * (k - 2), 2 * UNIT, 0, 2, 2, False)
-            if k - 0 in (2, 4, 6):
-                far(UNIT * (k - 0 - 2))
-        for kk in (2, 4, 6):
-            if kk + 0 > UNITS - 1:
-                far(UNIT * (kk - 2))
+                    mm_a(a, i + 1)
+            k = i - 2 - 0
+            if k >= 0:
+                unit_out(k)
         quant_h(UNITS - 1)
-        energies(768, UNIT, 0, 4, 6, False)
-        energies(768, UNIT, 4, 1, 1, False)
-        energies(896, UNIT, 0, 3, 7, True)
-        energies(896, UNIT, 3, 2, 0, False)
+        for k in range(UNITS - 1 - 0, UNITS):
+            unit_out(k)

@@ -18,16 +18,15 @@ ALU = mybir.AluOpType
 
 P = 128
 PASSES = K // 512
-HALF = 512
-HALVES = S // HALF
+LAST = PASSES - 1
 UNIT = 128
 UNITS = S // UNIT
-EARLY = 7
+EARLY = UNITS - 1
 X_BANK = (0, 1, 2, 3, 4, 5, 6, 1)
-A_BANK = (7, 0, 7, 0, 7, 0, 7, 0)
-LAG = 1
-NEAR = 3
-PICK = (512, 512, 256)
+A_BANK = (7, 0)
+CUTS = ((0, 1024), (0, 1024), (0, 256, 512, 1024))
+TWICE = 5
+NEAR = 2
 
 
 def tile_list_bead_well_energies_kernel(tc, tab_words, tab_scales, offs, wx, wd_words, wd_scales, wo, out):
@@ -46,8 +45,6 @@ def tile_list_bead_well_energies_kernel(tc, tab_words, tab_scales, offs, wx, wd_
         ts_i32 = tab_scales.bitcast(I32)
         for q in range(4):
             nc.gpsimd.dma_start(ts_all[32 * q : 32 * q + 4 * PASSES, :], ts_i32[:, 4 * q : 4 * q + 4, :])
-        ws_raw = keep.tile([P, PASSES, H // 4], I32, name="ws_raw", align_bytes=64)
-        nc.vector.memset(ws_raw[:], 0)
         ts_low = [keep.tile([P, S // 4], I32, name=f"ts_low{a}", align_bytes=64) for a in range(1, PASSES)]
         for tile in ts_low:
             nc.vector.memset(tile[96:128, :], 0)
@@ -55,11 +52,8 @@ def tile_list_bead_well_energies_kernel(tc, tab_words, tab_scales, offs, wx, wd_
         nc.vector.memset(warm[:], 1.0)
         warm_out = keep.tile([P, 1], F32, name="warm_out")
         nc.scalar.activation(warm_out[:], warm[:], ACT.Abs_reciprocal_sqrt)
-        ws_i32 = wd_scales.bitcast(I32)
-        for q in range(4):
-            nc.scalar.dma_start(ws_raw[32 * q : 32 * q + 4, :, :], ws_i32[:, 4 * q : 4 * q + 4, :].rearrange("a r c -> r a c"))
 
-        wx_raw, tab = {}, {}
+        wx_raw, tab, v_codes, wx_bf = {}, {}, {}, {}
 
         def load_tab(a, slot):
             tab[a] = stage.tile([P, T], I32, name=f"tab{a}", tag=slot, align_bytes=64)
@@ -69,56 +63,34 @@ def tile_list_bead_well_energies_kernel(tc, tab_words, tab_scales, offs, wx, wd_
             wx_raw[a] = stage.tile([P, 4, H], F32, name=f"wx_raw{a}", tag=slot, align_bytes=64)
             nc.sync.dma_start(wx_raw[a][:], wx[512 * a : 512 * (a + 1), :].rearrange("(p j) c -> p j c", j=4))
 
-        wd_codes = keep.tile([P, PASSES, H // 2], I32, name="wd_codes", align_bytes=64)
-
-        def order_wd_codes():
-            for a in range(PASSES):
+        def gather(a):
+            for j0, j1 in zip(CUTS[a], CUTS[a][1:]):
+                picked = keep.tile([P, j1 - j0], I32, name=f"v_codes{a}_{j0}", align_bytes=64)
                 nc.vector.tensor_copy(
-                    wd_codes[:, a, :].rearrange("p (t u k) -> p t u k", t=4, k=2),
-                    wd_raw[:, a, :].rearrange("p (u t k) -> p t u k", t=4, k=2),
+                    picked[:].bitcast(U32), tab[a][:].bitcast(U32).indirect(offsets[:, j0 // 16 : j1 // 16])
                 )
+                for j in range(j0, j1, UNIT):
+                    v_codes[a, j // UNIT] = picked[:, j - j0 : j - j0 + UNIT].bitcast(FP8X4)
 
-        def order_wd_planes():
-            nc.vector.tensor_copy(
-                wd_planes[:].rearrange("p a (t u) -> p a t u", t=4),
-                ws_raw[:].rearrange("p a (u t) -> p a t u", t=4),
-            )
-
-        wx_bf = [[stage.tile([P, P * 4], BF16, name=f"wx_bf{a}_{t}", tag=f"wxbf{a}{t}", align_bytes=64) for t in range(4)] for a in range(PASSES)]
         wx_codes = [keep.tile([P, H], U32, name=f"wx_codes{a}", align_bytes=64) for a in range(PASSES)]
         wx_planes = [keep.tile([P, H], U8, name=f"wx_planes{a}", align_bytes=64) for a in range(PASSES)]
 
-        def cast_wx(a, t, on_vector):
-            dst = wx_bf[a][t][:].rearrange("p (u e j) -> p u j e", e=4, j=4)
-            src = wx_raw[a][:].rearrange("p j (u t e) -> p t u j e", t=4, e=4)[:, t]
-            if on_vector:
-                nc.vector.tensor_copy(dst, src)
-            else:
-                nc.scalar.copy(dst, src)
-
-        def quant_wx(a, t):
-            nc.vector.quantize_mx(
-                out=wx_codes[a][:, P * t : P * (t + 1)].bitcast(FP8X4),
-                scales=wx_planes[a][:, P * t : P * (t + 1)],
-                in_=wx_bf[a][t][:],
+        def quant_wx(a, half, copy):
+            rounded = stage.tile([P, 2, P * 4], BF16, name=f"wx_bf{a}_{half}", tag=f"wx_bf{a}_{half}", align_bytes=64)
+            copy(
+                rounded[:].rearrange("p t (u e j) -> p t u j e", e=4, j=4),
+                wx_raw[a][:].rearrange("p j (u t e) -> p t u j e", t=4, e=4)[:, 2 * half : 2 * half + 2],
             )
-
-        v_codes = {}
-
-        def gather(a):
-            width = PICK[a]
-            for b in range(S // width):
-                cols = slice(b * width // 16, (b + 1) * width // 16)
-                v_codes[a, b] = keep.tile([P, width], I32, name=f"v_codes{a}_{b}", align_bytes=64)
-                nc.vector.tensor_copy(v_codes[a, b][:].bitcast(U32), tab[a][:].bitcast(U32).indirect(offsets[:, cols]))
-
-        def v_unit(a, i):
-            b, j0 = divmod(i * UNIT, PICK[a])
-            return v_codes[a, b][:, j0 : j0 + UNIT].bitcast(FP8X4)
+            cols = slice(2 * P * half, 2 * P * (half + 1))
+            nc.vector.quantize_mx(
+                out=wx_codes[a][:, cols].bitcast(FP8X4),
+                scales=wx_planes[a][:, cols],
+                in_=rounded[:].rearrange("p t c -> p (t c)"),
+            )
 
         x_ps, a_ps = {}, {}
 
-        def mm_x(a, i):
+        def mm_x(a, i, closes=False):
             if a == 0:
                 x_ps[i] = psum.tile([P, 4, UNIT], F32, name=f"x{i}", tag=f"bank{X_BANK[i]}")
             for t in range(4):
@@ -126,123 +98,125 @@ def tile_list_bead_well_energies_kernel(tc, tab_words, tab_scales, offs, wx, wd_
                     out=x_ps[i][:, t, :],
                     lhsT=wx_codes[a][:, P * t : P * (t + 1)].bitcast(FP8X4),
                     lhsT_scale=wx_planes[a][:, P * t : P * (t + 1)],
-                    rhs=v_unit(a, i),
+                    rhs=v_codes[a, i],
                     rhs_scale=ts_pick[:].bitcast(U8)[4 * a : P, UNIT * i : UNIT * (i + 1)],
                     start=(a == 0 and t == 0),
-                    stop=(a == PASSES - 1 and t == 3),
+                    stop=(closes and t == 3),
                 )
 
-        def mm_a(a, i):
-            if a == 0:
-                a_ps[i] = psum.tile([P, 4, UNIT], F32, name=f"a{i}", tag=f"bank{A_BANK[i]}")
-            for t in range(4):
-                nc.tensor.matmul_mx(
-                    out=a_ps[i][:, t, :],
-                    lhsT=wd_codes[:, a, 64 * t : 64 * (t + 1)].bitcast(U8).bitcast(FP4X4),
-                    lhsT_scale=wd_planes[:, a, 32 * t : 32 * (t + 1)].bitcast(U8),
-                    rhs=v_unit(a, i),
-                    rhs_scale=v_planes[a][:].bitcast(U8)[:, UNIT * i : UNIT * (i + 1)],
-                    start=(a == 0 and t == 0),
-                    stop=(a == PASSES - 1 and t == 3),
-                )
+        def mm_a(i):
+            a_ps[i] = psum.tile([P, 4, UNIT], F32, name=f"a{i}", tag=f"bank{A_BANK[i % 2]}")
+            for a in range(PASSES):
+                for t in range(4):
+                    nc.tensor.matmul_mx(
+                        out=a_ps[i][:, t, :],
+                        lhsT=wd_codes[:, a, 64 * t : 64 * (t + 1)].bitcast(U8).bitcast(FP4X4),
+                        lhsT_scale=wd_planes[:, a, 32 * t : 32 * (t + 1)].bitcast(U8),
+                        rhs=v_codes[a, i],
+                        rhs_scale=v_planes[a][:].bitcast(U8)[:, UNIT * i : UNIT * (i + 1)],
+                        start=(a == 0 and t == 0),
+                        stop=(a == LAST and t == 3),
+                    )
 
-        last = PASSES - 1
         load_tab(0, "slot0")
         load_tab(1, "slot1")
         load_wx(0, "slot2")
         load_wx(1, "slot3")
         gather(0)
         load_wx(2, "slot0")
-        load_tab(2, "slot5")
+        load_tab(2, "slot4")
         gather(1)
-        for a in range(PASSES):
-            for t in range(4):
-                cast_wx(a, t, t < (2,0,2)[a])
-                quant_wx(a, t)
-            if a == 0:
-                ts_pick = stage.tile([P, S // 4], I32, name="ts_pick", tag="wxbf01", align_bytes=64)
-                v_planes = [ts_pick] + ts_low
-                for b in range(2):
-                    nc.vector.tensor_copy(
-                        ts_pick[:].bitcast(U8)[:, HALF * b : HALF * (b + 1)],
-                        ts_all[:].bitcast(U8).indirect(offsets[:, 32 * b : 32 * (b + 1)]),
-                    )
-                for c in range(1, PASSES):
-                    nc.gpsimd.dma_start(ts_low[c - 1][0:112, :], ts_pick[4 * c : 4 * c + 112, :])
-            if a < last:
-                for i in range(EARLY):
-                    mm_x(a, i)
+        quant_wx(0, 0, nc.vector.tensor_copy)
+        quant_wx(0, 1, nc.scalar.copy)
+        ts_pick = stage.tile([P, S // 4], I32, name="ts_pick", tag="wx_bf0_0", align_bytes=64)
+        v_planes = [ts_pick] + ts_low
+        for j0 in range(0, S, 512):
+            nc.vector.tensor_copy(
+                ts_pick[:].bitcast(U8)[:, j0 : j0 + 512],
+                ts_all[:].bitcast(U8).indirect(offsets[:, j0 // 16 : (j0 + 512) // 16]),
+            )
+        for i in range(EARLY):
+            mm_x(0, i)
+        quant_wx(1, 0, nc.scalar.copy)
+        quant_wx(1, 1, nc.scalar.copy)
+        for i in range(TWICE):
+            mm_x(1, i)
+        quant_wx(LAST, 0, nc.vector.tensor_copy)
+        quant_wx(LAST, 1, nc.scalar.copy)
+        ws_raw = stage.tile([P, PASSES, H // 4], I32, name="ws_raw", tag="wx_bf1_1", align_bytes=64)
+        nc.vector.memset(ws_raw[:], 0)
+        ws_i32 = wd_scales.bitcast(I32)
+        for q in range(4):
+            nc.scalar.dma_start(ws_raw[32 * q : 32 * q + 4, :, :], ws_i32[:, 4 * q : 4 * q + 4, :].rearrange("a r c -> r a c"))
         wo_raw = stage.tile([P, 4, N], F32, name="wo_raw", tag="slot2", align_bytes=64)
         wo_rows = wo.rearrange("(u t e) n -> t u e n", t=4, e=4)
         for t in range(4):
             nc.sync.dma_start(wo_raw[:, t, :], wo_rows[t])
-        wd_raw = stage.tile([P, PASSES, H // 2], I32, name="wd_raw", tag="slot4", align_bytes=64)
+        wd_raw = stage.tile([P, PASSES, H // 2], I32, name="wd_raw", tag="slot5", align_bytes=64)
         nc.sync.dma_start(wd_raw[:], wd_words.bitcast(I32).rearrange("a p c -> p a c"))
-        gather(last)
-        wd_planes = stage.tile([P, PASSES, H // 4], I32, name="wd_planes", tag="wxbf13", align_bytes=64)
-        order_wd_planes()
-        order_wd_codes()
+        for a in range(1, PASSES):
+            nc.sync.dma_start(ts_low[a - 1][0:112, :], ts_pick[4 * a : 4 * a + 112, :])
+        gather(LAST)
+        wd_planes = stage.tile([P, PASSES, H // 4], I32, name="wd_planes", tag="wd_planes", align_bytes=64)
+        nc.vector.tensor_copy(
+            wd_planes[:].rearrange("p a (t u) -> p a t u", t=4),
+            ws_raw[:].rearrange("p a (u t) -> p a t u", t=4),
+        )
+        wd_codes = keep.tile([P, PASSES, H // 2], I32, name="wd_codes", align_bytes=64)
+        nc.vector.tensor_copy(
+            wd_codes[:].rearrange("p a (t u k) -> p a t u k", t=4, k=2),
+            wd_raw[:].rearrange("p a (u t k) -> p a t u k", t=4, k=2),
+        )
         for i in range(EARLY):
-            mm_x(last, i)
-            if i == 3:
-                for a in range(PASSES):
-                    mm_a(a, 0)
+            mm_x(LAST, i, closes=i < TWICE)
+            if i >= TWICE:
+                mm_x(1, i, closes=True)
+        mm_a(0)
 
         wo_bf = keep.tile([P, N, 4], BF16, name="wo_bf", align_bytes=64)
         wo_codes = keep.tile([P, N], U32, name="wo_codes", align_bytes=64)
         wo_planes = keep.tile([P, N], U8, name="wo_planes", align_bytes=64)
-
-        def cast_wo(n, engine):
-            cols = slice(P * n, P * (n + 1))
-            if engine == "gpsimd":
-                nc.gpsimd.tensor_scalar(
-                    wo_bf[:, cols, :], wo_raw[:, :, cols].rearrange("p t n -> p n t"), 1.0, 0.0, ALU.mult, ALU.add
-                )
-                return
-            dst = wo_bf[:, cols, :].rearrange("p (c i) t -> p c t i", i=4)
-            src = wo_raw[:, :, cols].rearrange("p t (c i) -> p c t i", i=4)
-            if engine == "vector":
-                nc.vector.tensor_copy(dst, src)
-            else:
-                nc.scalar.copy(dst, src)
-
-        def quant_wo(n):
-            cols = slice(P * n, P * (n + 1))
+        for n0, n1 in ((0, 512), (512, N)):
+            nc.vector.tensor_copy(
+                wo_bf[:, n0:n1, :].rearrange("p (c i) t -> p c t i", i=4),
+                wo_raw[:, :, n0:n1].rearrange("p t (c i) -> p c t i", i=4),
+            )
             nc.vector.quantize_mx(
-                out=wo_codes[:, cols].bitcast(FP8X4),
-                scales=wo_planes[:, cols],
-                in_=wo_bf[:, cols, :].rearrange("p n t -> p (n t)"),
+                out=wo_codes[:, n0:n1].bitcast(FP8X4),
+                scales=wo_planes[:, n0:n1],
+                in_=wo_bf[:, n0:n1, :].rearrange("p n t -> p (n t)"),
             )
 
         h_codes = keep.tile([P, S], U32, name="h_codes", align_bytes=64)
         h_planes = keep.tile([P, S], U8, name="h_planes", align_bytes=64)
         q_sb, pp_sb, h_bf = {}, {}, {}
 
-        def shape(i):
-            x_jt = x_ps[i][:].rearrange("p t j -> p j t")
-            s_sb = ring.tile([P, UNIT, 4], F32, name="s_sb")
-            nc.scalar.activation(s_sb[:], x_jt, ACT.Square)
-            w_sb = ring.tile([P, UNIT, 4], F32, name="w_sb")
+        def x_jt(i):
+            return x_ps[i][:].rearrange("p t j -> p j t")
+
+        def inverse(units):
+            n = len(units)
+            s_sb = ring.tile([P, n, UNIT, 4], F32, name="s_sb")
+            for c, i in enumerate(units):
+                nc.scalar.activation(s_sb[:, c], x_jt(i), ACT.Square)
+            w_sb = ring.tile([P, n, UNIT, 4], F32, name="w_sb")
             nc.scalar.activation(w_sb[:], s_sb[:], ACT.Abs_reciprocal_sqrt, bias=1.0)
-            q_sb[i] = stage.tile([P, UNIT, 4], F32, name=f"q_sb{i}", tag=f"q{i}", align_bytes=64)
-            if i<0:
-                nc.vector.tensor_tensor(q_sb[i][:], w_sb[:], w_sb[:], ALU.mult)
-            elif i < 0:
-                nc.gpsimd.tensor_tensor(q_sb[i][:], w_sb[:], w_sb[:], ALU.mult)
-            else:
-                nc.scalar.activation(q_sb[i][:], w_sb[:], ACT.Square)
-            p_sb = stage.tile([P, UNIT, 4], F32, name=f"p_sb{i}", tag=f"p{i % 3}" if i else "slot4", align_bytes=64)
-            nc.vector.tensor_tensor(p_sb[:], x_jt, q_sb[i][:], ALU.mult)
+            q_all = ring.tile([P, n, UNIT, 4], F32, name="q_sb")
+            nc.scalar.activation(q_all[:], w_sb[:], ACT.Square)
+            for c, i in enumerate(units):
+                q_sb[i] = q_all[:, c]
+
+        def shape(i):
+            p_sb = stage.tile([P, UNIT, 4], F32, name=f"p_sb{i}", tag=f"p{i % 3}" if i else "slot5", align_bytes=64)
+            nc.vector.tensor_tensor(p_sb[:], x_jt(i), q_sb[i], ALU.mult)
             pp_sb[i] = ring.tile([P, UNIT, 4], F32, name="pp_sb")
-            if i<0:
-                nc.gpsimd.tensor_tensor(pp_sb[i][:], p_sb[:], p_sb[:], ALU.mult)
-            elif i<6:
+            if i < UNITS - 2:
                 nc.vector.tensor_tensor(pp_sb[i][:], p_sb[:], p_sb[:], ALU.mult)
             else:
                 nc.scalar.activation(pp_sb[i][:], p_sb[:], ACT.Square)
 
         def depth(i):
-            h_bf[i] = stage.tile([P, UNIT, 4], BF16, name=f"h_bf{i}", tag=f"q{i + 9}", align_bytes=64)
+            h_bf[i] = ring.tile([P, UNIT, 4], BF16, name="h_bf", align_bytes=64)
             nc.vector.tensor_tensor(h_bf[i][:], a_ps[i][:].rearrange("p t j -> p j t"), pp_sb[i][:], ALU.mult)
 
         def quant_h(i):
@@ -255,13 +229,13 @@ def tile_list_bead_well_energies_kernel(tc, tab_words, tab_scales, offs, wx, wd_
 
         out_tiles = out.rearrange("(n p) j -> p n j", p=P)
 
-        def energies(j0, width, n0, count, bank, on_vector):
-            cols = slice(j0, j0 + width)
-            acc = psum.tile([P, count, width], F32, name=f"o{j0}_{n0}", tag=f"bank{bank}")
-            for n in range(count):
-                rows = slice(P * (n0 + n), P * (n0 + n + 1))
+        def energies(i, n0, n1, bank, copy):
+            cols = slice(UNIT * i, UNIT * (i + 1))
+            acc = psum.tile([P, n1 - n0, UNIT], F32, name=f"o{i}_{n0}", tag=f"bank{bank}")
+            for n in range(n0, n1):
+                rows = slice(P * n, P * (n + 1))
                 nc.tensor.matmul_mx(
-                    out=acc[:, n, :],
+                    out=acc[:, n - n0, :],
                     lhsT=wo_codes[:, rows].bitcast(FP8X4),
                     lhsT_scale=wo_planes[:, rows],
                     rhs=h_codes[:, cols].bitcast(FP8X4),
@@ -269,40 +243,32 @@ def tile_list_bead_well_energies_kernel(tc, tab_words, tab_scales, offs, wx, wd_
                     start=True,
                     stop=True,
                 )
-            res = keep.tile([P, count, width], F32, name=f"res{j0}_{n0}")
-            if on_vector:
-                nc.vector.tensor_copy(res[:], acc[:])
-            else:
-                nc.scalar.copy(res[:], acc[:])
-            nc.sync.dma_start(out_tiles[:, n0 : n0 + count, cols], res[:])
+            res = keep.tile([P, n1 - n0, UNIT], F32, name=f"res{i}_{n0}")
+            copy(res[:], acc[:])
+            nc.sync.dma_start(out_tiles[:, n0:n1, cols], res[:])
 
-        def unit_out(k):
-            near = 3
-            energies(UNIT * k, UNIT, 0, near, 2 if k < 5 else 2 + 2 * (k % 2), k == 7)
-            energies(UNIT * k, UNIT, near, N // P - near, 3 if k < 5 else 3 + 2 * (k % 2), False)
+        def unit_out(i):
+            bank = 2 if i < 5 else 2 + 2 * (i % 2)
+            energies(i, 0, NEAR, bank, nc.vector.tensor_copy if i == UNITS - 1 else nc.scalar.copy)
+            energies(i, NEAR, N // P, bank + 1, nc.scalar.copy)
 
-        for n in range(N // P):
-            cast_wo(n, "vector")
-            quant_wo(n)
-        for i in range(UNITS + 1):
+        groups = tuple((i,) for i in range(UNITS))
+        for i in range(UNITS + 2):
+            for units in groups:
+                if units[0] == i:
+                    inverse(units)
             if i < UNITS:
                 shape(i)
+            if i == 0:
+                mm_a(1)
             if i == 1:
                 for a in range(PASSES):
-                    mm_x(a, UNITS - 1)
-            if i == 0:
-                for a in range(PASSES):
-                    mm_a(a, 1)
-                continue
+                    mm_x(a, UNITS - 1, closes=a == LAST)
             if i >= 2:
                 quant_h(i - 2)
-            depth(i - 1)
-            if i + 1 < UNITS:
-                for a in range(PASSES):
-                    mm_a(a, i + 1)
-            k = i - 2 - 0
-            if k >= 0:
-                unit_out(k)
-        quant_h(UNITS - 1)
-        for k in range(UNITS - 1 - 0, UNITS):
-            unit_out(k)
+            if 1 <= i <= UNITS:
+                depth(i - 1)
+                if i + 1 < UNITS:
+                    mm_a(i + 1)
+            if i >= 2:
+                unit_out(i - 2)

@@ -45,6 +45,8 @@ def tile_list_bead_well_energies_kernel(tc, tab_words, tab_scales, offs, wx, wd_
         ts_i32 = tab_scales.bitcast(I32)
         for q in range(4):
             nc.gpsimd.dma_start(ts_all[32 * q : 32 * q + 4 * PASSES, :], ts_i32[:, 4 * q : 4 * q + 4, :])
+        ws_raw = keep.tile([P, PASSES, H // 4], I32, name="ws_raw", align_bytes=64)
+        nc.vector.memset(ws_raw[:], 0)
         ts_low = [keep.tile([P, S // 4], I32, name=f"ts_low{a}", align_bytes=64) for a in range(1, PASSES)]
         for tile in ts_low:
             nc.vector.memset(tile[96:128, :], 0)
@@ -52,6 +54,9 @@ def tile_list_bead_well_energies_kernel(tc, tab_words, tab_scales, offs, wx, wd_
         nc.vector.memset(warm[:], 1.0)
         warm_out = keep.tile([P, 1], F32, name="warm_out")
         nc.scalar.activation(warm_out[:], warm[:], ACT.Abs_reciprocal_sqrt)
+        ws_i32 = wd_scales.bitcast(I32)
+        for q in range(4):
+            nc.scalar.dma_start(ws_raw[32 * q : 32 * q + 4, :, :], ws_i32[:, 4 * q : 4 * q + 4, :].rearrange("a r c -> r a c"))
 
         wx_raw, tab, v_codes, wx_bf = {}, {}, {}, {}
 
@@ -135,6 +140,8 @@ def tile_list_bead_well_energies_kernel(tc, tab_words, tab_scales, offs, wx, wd_
                 ts_pick[:].bitcast(U8)[:, j0 : j0 + 512],
                 ts_all[:].bitcast(U8).indirect(offsets[:, j0 // 16 : (j0 + 512) // 16]),
             )
+        for a in range(1, PASSES):
+            nc.gpsimd.dma_start(ts_low[a - 1][0:112, :], ts_pick[4 * a : 4 * a + 112, :])
         for i in range(EARLY):
             mm_x(0, i)
         quant_wx(1, 0, nc.scalar.copy)
@@ -143,21 +150,14 @@ def tile_list_bead_well_energies_kernel(tc, tab_words, tab_scales, offs, wx, wd_
             mm_x(1, i)
         quant_wx(LAST, 0, nc.vector.tensor_copy)
         quant_wx(LAST, 1, nc.scalar.copy)
-        ws_raw = stage.tile([P, PASSES, H // 4], I32, name="ws_raw", tag="wx_bf1_1", align_bytes=64)
-        nc.vector.memset(ws_raw[:], 0)
-        ws_i32 = wd_scales.bitcast(I32)
-        for q in range(4):
-            nc.scalar.dma_start(ws_raw[32 * q : 32 * q + 4, :, :], ws_i32[:, 4 * q : 4 * q + 4, :].rearrange("a r c -> r a c"))
         wo_raw = stage.tile([P, 4, N], F32, name="wo_raw", tag="slot2", align_bytes=64)
         wo_rows = wo.rearrange("(u t e) n -> t u e n", t=4, e=4)
         for t in range(4):
             nc.sync.dma_start(wo_raw[:, t, :], wo_rows[t])
         wd_raw = stage.tile([P, PASSES, H // 2], I32, name="wd_raw", tag="slot5", align_bytes=64)
         nc.sync.dma_start(wd_raw[:], wd_words.bitcast(I32).rearrange("a p c -> p a c"))
-        for a in range(1, PASSES):
-            nc.sync.dma_start(ts_low[a - 1][0:112, :], ts_pick[4 * a : 4 * a + 112, :])
         gather(LAST)
-        wd_planes = stage.tile([P, PASSES, H // 4], I32, name="wd_planes", tag="wd_planes", align_bytes=64)
+        wd_planes = stage.tile([P, PASSES, H // 4], I32, name="wd_planes", tag="wx_bf1_1", align_bytes=64)
         nc.vector.tensor_copy(
             wd_planes[:].rearrange("p a (t u) -> p a t u", t=4),
             ws_raw[:].rearrange("p a (u t) -> p a t u", t=4),

@@ -21,12 +21,17 @@ PASSES = K // 512
 LAST = PASSES - 1
 UNIT = 128
 UNITS = S // UNIT
+ROW_TILES = N // P
+
 EARLY = UNITS - 1
-X_BANK = (0, 1, 2, 3, 4, 5, 6, 1)
-A_BANK = (7, 0)
-CUTS = ((0, 1024), (0, 1024), (0, 256, 512, 1024))
+LAST_X_BANK = 1
+A_BANKS = (7, 0)
+OUT_BANKS = ((2, 3), (4, 5))
+OUT_ALTERNATES_FROM = 5
 TWICE = 5
-NEAR = 2
+NEAR = 3
+SQUARE_ON_VECTOR = UNITS - 2
+LAST_CUTS = (0, 256, 512, S)
 
 
 def tile_list_bead_well_energies_kernel(tc, tab_words, tab_scales, offs, wx, wd_words, wd_scales, wo, out):
@@ -34,138 +39,141 @@ def tile_list_bead_well_energies_kernel(tc, tab_words, tab_scales, offs, wx, wd_
     with ExitStack() as ctx:
         keep = ctx.enter_context(tc.tile_pool(name="keep", bufs=1))
         ring = ctx.enter_context(tc.tile_pool(name="ring", bufs=4))
-        stage = ctx.enter_context(tc.tile_pool(name="stage", bufs=1))
+        shared = ctx.enter_context(tc.tile_pool(name="shared", bufs=1))
         psum = ctx.enter_context(tc.psum_pool(name="psum", bufs=1))
 
         offsets = keep.tile([P, S // 16], U16, name="offsets")
         nc.sync.dma_start(offsets[:], offs)
 
-        ts_all = keep.tile([P, T // 4], I32, name="ts_all", align_bytes=64)
-        nc.gpsimd.memset(ts_all[:], 0)
-        ts_i32 = tab_scales.bitcast(I32)
+        tab_rows = keep.tile([P, T // 4], I32, name="tab_rows", align_bytes=64)
+        nc.gpsimd.memset(tab_rows[:], 0)
+        tab_scales_i32 = tab_scales.bitcast(I32)
         for q in range(4):
-            nc.gpsimd.dma_start(ts_all[32 * q : 32 * q + 4 * PASSES, :], ts_i32[:, 4 * q : 4 * q + 4, :])
-        ws_raw = keep.tile([P, PASSES, H // 4], I32, name="ws_raw", align_bytes=64)
-        nc.vector.memset(ws_raw[:], 0)
-        ts_low = [keep.tile([P, S // 4], I32, name=f"ts_low{a}", align_bytes=64) for a in range(1, PASSES)]
-        for tile in ts_low:
+            nc.gpsimd.dma_start(tab_rows[32 * q : 32 * q + 4 * PASSES, :], tab_scales_i32[:, 4 * q : 4 * q + 4, :])
+        wd_rows = keep.tile([P, PASSES, H // 4], I32, name="wd_rows", align_bytes=64)
+        nc.vector.memset(wd_rows[:], 0)
+        moved_rows = [keep.tile([P, S // 4], I32, name=f"moved_rows{g}", align_bytes=64) for g in range(1, PASSES)]
+        for tile in moved_rows:
             nc.vector.memset(tile[96:128, :], 0)
         warm = keep.tile([P, 1], F32, name="warm")
         nc.vector.memset(warm[:], 1.0)
         warm_out = keep.tile([P, 1], F32, name="warm_out")
         nc.scalar.activation(warm_out[:], warm[:], ACT.Abs_reciprocal_sqrt)
-        ws_i32 = wd_scales.bitcast(I32)
+        wd_scales_i32 = wd_scales.bitcast(I32)
         for q in range(4):
-            nc.scalar.dma_start(ws_raw[32 * q : 32 * q + 4, :, :], ws_i32[:, 4 * q : 4 * q + 4, :].rearrange("a r c -> r a c"))
+            nc.scalar.dma_start(
+                wd_rows[32 * q : 32 * q + 4, :, :], wd_scales_i32[:, 4 * q : 4 * q + 4, :].rearrange("g r c -> r g c")
+            )
 
-        wx_raw, tab, v_codes, wx_bf = {}, {}, {}, {}
+        tab, wx_raw, v_codes = {}, {}, {}
 
-        def load_tab(a, slot):
-            tab[a] = stage.tile([P, T], I32, name=f"tab{a}", tag=slot, align_bytes=64)
-            nc.sync.dma_start(tab[a][:], tab_words[a].rearrange("p t i -> p (t i)").bitcast(I32))
+        def load_tab(g, tag):
+            tab[g] = shared.tile([P, T], I32, name=f"tab{g}", tag=tag, align_bytes=64)
+            nc.sync.dma_start(tab[g][:], tab_words[g].rearrange("p n c -> p (n c)").bitcast(I32))
 
-        def load_wx(a, slot):
-            wx_raw[a] = stage.tile([P, 4, H], F32, name=f"wx_raw{a}", tag=slot, align_bytes=64)
-            nc.sync.dma_start(wx_raw[a][:], wx[512 * a : 512 * (a + 1), :].rearrange("(p j) c -> p j c", j=4))
+        def load_wx(g, tag):
+            wx_raw[g] = shared.tile([P, 4, H], F32, name=f"wx_raw{g}", tag=tag, align_bytes=64)
+            nc.sync.dma_start(wx_raw[g][:], wx[512 * g : 512 * (g + 1), :].rearrange("(p c) r -> p c r", c=4))
 
-        def gather(a):
-            for j0, j1 in zip(CUTS[a], CUTS[a][1:]):
-                picked = keep.tile([P, j1 - j0], I32, name=f"v_codes{a}_{j0}", align_bytes=64)
+        def gather_words(g, cuts):
+            for j0, j1 in zip(cuts, cuts[1:]):
+                picked = keep.tile([P, j1 - j0], I32, name=f"v_codes{g}_{j0}", align_bytes=64)
                 nc.vector.tensor_copy(
-                    picked[:].bitcast(U32), tab[a][:].bitcast(U32).indirect(offsets[:, j0 // 16 : j1 // 16])
+                    picked[:].bitcast(U32), tab[g][:].bitcast(U32).indirect(offsets[:, j0 // 16 : j1 // 16])
                 )
                 for j in range(j0, j1, UNIT):
-                    v_codes[a, j // UNIT] = picked[:, j - j0 : j - j0 + UNIT].bitcast(FP8X4)
+                    v_codes[g, j // UNIT] = picked[:, j - j0 : j - j0 + UNIT].bitcast(FP8X4)
 
-        wx_codes = [keep.tile([P, H], U32, name=f"wx_codes{a}", align_bytes=64) for a in range(PASSES)]
-        wx_planes = [keep.tile([P, H], U8, name=f"wx_planes{a}", align_bytes=64) for a in range(PASSES)]
+        wx_codes = [keep.tile([P, H], U32, name=f"wx_codes{g}", align_bytes=64) for g in range(PASSES)]
+        wx_scales = [keep.tile([P, H], U8, name=f"wx_scales{g}", align_bytes=64) for g in range(PASSES)]
 
-        def quant_wx(a, half, copy):
-            rounded = stage.tile([P, 2, P * 4], BF16, name=f"wx_bf{a}_{half}", tag=f"wx_bf{a}_{half}", align_bytes=64)
+        def quantise_wx(g, half, copy):
+            rounded = shared.tile([P, 2, P * 4], BF16, name=f"wx_bf{g}_{half}", tag=f"wx_bf{g}_{half}", align_bytes=64)
             copy(
-                rounded[:].rearrange("p t (u e j) -> p t u j e", e=4, j=4),
-                wx_raw[a][:].rearrange("p j (u t e) -> p t u j e", t=4, e=4)[:, 2 * half : 2 * half + 2],
+                rounded[:].rearrange("p t (u e c) -> p t u c e", e=4, c=4),
+                wx_raw[g][:].rearrange("p c (u t e) -> p t u c e", t=4, e=4)[:, 2 * half : 2 * half + 2],
             )
             cols = slice(2 * P * half, 2 * P * (half + 1))
             nc.vector.quantize_mx(
-                out=wx_codes[a][:, cols].bitcast(FP8X4),
-                scales=wx_planes[a][:, cols],
-                in_=rounded[:].rearrange("p t c -> p (t c)"),
+                out=wx_codes[g][:, cols].bitcast(FP8X4),
+                scales=wx_scales[g][:, cols],
+                in_=rounded[:].rearrange("p t w -> p (t w)"),
             )
 
         x_ps, a_ps = {}, {}
 
-        def mm_x(a, i, closes=False):
-            if a == 0:
-                x_ps[i] = psum.tile([P, 4, UNIT], F32, name=f"x{i}", tag=f"bank{X_BANK[i]}")
+        def mm_x(g, i, closes=False):
+            if g == 0:
+                x_ps[i] = psum.tile([P, 4, UNIT], F32, name=f"x{i}", tag=f"bank{i if i < EARLY else LAST_X_BANK}")
             for t in range(4):
                 nc.tensor.matmul_mx(
                     out=x_ps[i][:, t, :],
-                    lhsT=wx_codes[a][:, P * t : P * (t + 1)].bitcast(FP8X4),
-                    lhsT_scale=wx_planes[a][:, P * t : P * (t + 1)],
-                    rhs=v_codes[a, i],
-                    rhs_scale=ts_pick[:].bitcast(U8)[4 * a : P, UNIT * i : UNIT * (i + 1)],
-                    start=(a == 0 and t == 0),
+                    lhsT=wx_codes[g][:, P * t : P * (t + 1)].bitcast(FP8X4),
+                    lhsT_scale=wx_scales[g][:, P * t : P * (t + 1)],
+                    rhs=v_codes[g, i],
+                    rhs_scale=picked_rows[:].bitcast(U8)[4 * g : P, UNIT * i : UNIT * (i + 1)],
+                    start=(g == 0 and t == 0),
                     stop=(closes and t == 3),
                 )
 
         def mm_a(i):
-            a_ps[i] = psum.tile([P, 4, UNIT], F32, name=f"a{i}", tag=f"bank{A_BANK[i % 2]}")
-            for a in range(PASSES):
+            a_ps[i] = psum.tile([P, 4, UNIT], F32, name=f"a{i}", tag=f"bank{A_BANKS[i % 2]}")
+            for g in range(PASSES):
                 for t in range(4):
                     nc.tensor.matmul_mx(
                         out=a_ps[i][:, t, :],
-                        lhsT=wd_codes[:, a, 64 * t : 64 * (t + 1)].bitcast(U8).bitcast(FP4X4),
-                        lhsT_scale=wd_planes[:, a, 32 * t : 32 * (t + 1)].bitcast(U8),
-                        rhs=v_codes[a, i],
-                        rhs_scale=v_planes[a][:].bitcast(U8)[:, UNIT * i : UNIT * (i + 1)],
-                        start=(a == 0 and t == 0),
-                        stop=(a == LAST and t == 3),
+                        lhsT=wd_codes[:, g, 64 * t : 64 * (t + 1)].bitcast(U8).bitcast(FP4X4),
+                        lhsT_scale=wd_ordered[:, g, 32 * t : 32 * (t + 1)].bitcast(U8),
+                        rhs=v_codes[g, i],
+                        rhs_scale=v_rows[g][:].bitcast(U8)[:, UNIT * i : UNIT * (i + 1)],
+                        start=(g == 0 and t == 0),
+                        stop=(g == LAST and t == 3),
                     )
 
-        load_tab(0, "slot0")
-        load_tab(1, "slot1")
-        load_wx(0, "slot2")
-        load_wx(1, "slot3")
-        gather(0)
-        load_wx(2, "slot0")
-        load_tab(2, "slot4")
-        gather(1)
-        quant_wx(0, 0, nc.vector.tensor_copy)
-        quant_wx(0, 1, nc.scalar.copy)
-        ts_pick = stage.tile([P, S // 4], I32, name="ts_pick", tag="wx_bf0_0", align_bytes=64)
-        v_planes = [ts_pick] + ts_low
-        for j0 in range(0, S, 512):
+        load_tab(0, "tab0_wx2")
+        load_tab(1, "tab1")
+        load_wx(0, "wx0_wo")
+        load_wx(1, "wx1")
+        gather_words(0, (0, S))
+        load_wx(2, "tab0_wx2")
+        load_tab(2, "tab2")
+        gather_words(1, (0, S))
+        quantise_wx(0, 0, nc.vector.tensor_copy)
+        quantise_wx(0, 1, nc.scalar.copy)
+        picked_rows = shared.tile([P, S // 4], I32, name="picked_rows", tag="wx_bf0_0", align_bytes=64)
+        v_rows = [picked_rows] + moved_rows
+        for j0 in range(0, S, S // 2):
             nc.vector.tensor_copy(
-                ts_pick[:].bitcast(U8)[:, j0 : j0 + 512],
-                ts_all[:].bitcast(U8).indirect(offsets[:, j0 // 16 : (j0 + 512) // 16]),
+                picked_rows[:].bitcast(U8)[:, j0 : j0 + S // 2],
+                tab_rows[:].bitcast(U8).indirect(offsets[:, j0 // 16 : (j0 + S // 2) // 16]),
             )
-        for a in range(1, PASSES):
-            nc.gpsimd.dma_start(ts_low[a - 1][0:112, :], ts_pick[4 * a : 4 * a + 112, :])
+        for g in range(1, PASSES):
+            nc.gpsimd.dma_start(v_rows[g][0:112, :], picked_rows[4 * g : 4 * g + 112, :])
         for i in range(EARLY):
             mm_x(0, i)
-        quant_wx(1, 0, nc.scalar.copy)
-        quant_wx(1, 1, nc.scalar.copy)
+        quantise_wx(1, 0, nc.scalar.copy)
+        quantise_wx(1, 1, nc.scalar.copy)
         for i in range(TWICE):
             mm_x(1, i)
-        quant_wx(LAST, 0, nc.vector.tensor_copy)
-        quant_wx(LAST, 1, nc.scalar.copy)
-        wo_raw = stage.tile([P, 4, N], F32, name="wo_raw", tag="slot2", align_bytes=64)
-        wo_rows = wo.rearrange("(u t e) n -> t u e n", t=4, e=4)
+        quantise_wx(LAST, 0, nc.vector.tensor_copy)
+        quantise_wx(LAST, 1, nc.scalar.copy)
+        wo_raw = shared.tile([P, 4, N], F32, name="wo_raw", tag="wx0_wo", align_bytes=64)
+        wo_slots = wo.rearrange("(u t e) n -> t u e n", t=4, e=4)
         for t in range(4):
-            nc.sync.dma_start(wo_raw[:, t, :], wo_rows[t])
-        wd_raw = stage.tile([P, PASSES, H // 2], I32, name="wd_raw", tag="slot5", align_bytes=64)
-        nc.sync.dma_start(wd_raw[:], wd_words.bitcast(I32).rearrange("a p c -> p a c"))
-        gather(LAST)
-        wd_planes = stage.tile([P, PASSES, H // 4], I32, name="wd_planes", tag="wx_bf1_1", align_bytes=64)
+            nc.sync.dma_start(wo_raw[:, t, :], wo_slots[t])
+        wd_raw = shared.tile([P, PASSES, H // 2], I32, name="wd_raw", tag="wd_p0", align_bytes=64)
+        nc.sync.dma_start(wd_raw[:], wd_words.bitcast(I32).rearrange("g p w -> p g w"))
+        gather_words(LAST, LAST_CUTS)
+
+        wd_ordered = shared.tile([P, PASSES, H // 4], I32, name="wd_ordered", tag="wx_bf1_1", align_bytes=64)
         nc.vector.tensor_copy(
-            wd_planes[:].rearrange("p a (t u) -> p a t u", t=4),
-            ws_raw[:].rearrange("p a (u t) -> p a t u", t=4),
+            wd_ordered[:].rearrange("p g (t u) -> p g t u", t=4),
+            wd_rows[:].rearrange("p g (u t) -> p g t u", t=4),
         )
         wd_codes = keep.tile([P, PASSES, H // 2], I32, name="wd_codes", align_bytes=64)
         nc.vector.tensor_copy(
-            wd_codes[:].rearrange("p a (t u k) -> p a t u k", t=4, k=2),
-            wd_raw[:].rearrange("p a (u t k) -> p a t u k", t=4, k=2),
+            wd_codes[:].rearrange("p g (t u w) -> p g t u w", t=4, w=2),
+            wd_raw[:].rearrange("p g (u t w) -> p g t u w", t=4, w=2),
         )
         for i in range(EARLY):
             mm_x(LAST, i, closes=i < TWICE)
@@ -175,100 +183,88 @@ def tile_list_bead_well_energies_kernel(tc, tab_words, tab_scales, offs, wx, wd_
 
         wo_bf = keep.tile([P, N, 4], BF16, name="wo_bf", align_bytes=64)
         wo_codes = keep.tile([P, N], U32, name="wo_codes", align_bytes=64)
-        wo_planes = keep.tile([P, N], U8, name="wo_planes", align_bytes=64)
+        wo_scales = keep.tile([P, N], U8, name="wo_scales", align_bytes=64)
         for n0, n1 in ((0, 512), (512, N)):
             nc.vector.tensor_copy(
-                wo_bf[:, n0:n1, :].rearrange("p (c i) t -> p c t i", i=4),
-                wo_raw[:, :, n0:n1].rearrange("p t (c i) -> p c t i", i=4),
+                wo_bf[:, n0:n1, :].rearrange("p (m e) t -> p m t e", e=4),
+                wo_raw[:, :, n0:n1].rearrange("p t (m e) -> p m t e", e=4),
             )
             nc.vector.quantize_mx(
                 out=wo_codes[:, n0:n1].bitcast(FP8X4),
-                scales=wo_planes[:, n0:n1],
+                scales=wo_scales[:, n0:n1],
                 in_=wo_bf[:, n0:n1, :].rearrange("p n t -> p (n t)"),
             )
 
         h_codes = keep.tile([P, S], U32, name="h_codes", align_bytes=64)
-        h_planes = keep.tile([P, S], U8, name="h_planes", align_bytes=64)
-        q_sb, pp_sb, h_bf = {}, {}, {}
+        h_scales = keep.tile([P, S], U8, name="h_scales", align_bytes=64)
+        p_squared, h_bf = {}, {}
 
-        def x_jt(i):
-            return x_ps[i][:].rearrange("p t j -> p j t")
-
-        def inverse(units):
-            n = len(units)
-            s_sb = ring.tile([P, n, UNIT, 4], F32, name="s_sb")
-            for c, i in enumerate(units):
-                nc.scalar.activation(s_sb[:, c], x_jt(i), ACT.Square)
-            w_sb = ring.tile([P, n, UNIT, 4], F32, name="w_sb")
-            nc.scalar.activation(w_sb[:], s_sb[:], ACT.Abs_reciprocal_sqrt, bias=1.0)
-            q_all = ring.tile([P, n, UNIT, 4], F32, name="q_sb")
-            nc.scalar.activation(q_all[:], w_sb[:], ACT.Square)
-            for c, i in enumerate(units):
-                q_sb[i] = q_all[:, c]
-
-        def shape(i):
-            p_sb = stage.tile([P, UNIT, 4], F32, name=f"p_sb{i}", tag=f"p{i % 3}" if i else "slot5", align_bytes=64)
-            nc.vector.tensor_tensor(p_sb[:], x_jt(i), q_sb[i], ALU.mult)
-            pp_sb[i] = ring.tile([P, UNIT, 4], F32, name="pp_sb")
-            if i < UNITS - 2:
-                nc.vector.tensor_tensor(pp_sb[i][:], p_sb[:], p_sb[:], ALU.mult)
+        def well_shape(i):
+            x_jt = x_ps[i][:].rearrange("p t j -> p j t")
+            x_squared = ring.tile([P, UNIT, 4], F32, name="x_squared")
+            nc.scalar.activation(x_squared[:], x_jt, ACT.Square)
+            root = ring.tile([P, UNIT, 4], F32, name="root")
+            nc.scalar.activation(root[:], x_squared[:], ACT.Abs_reciprocal_sqrt, bias=1.0)
+            q_sb = ring.tile([P, UNIT, 4], F32, name="q_sb")
+            nc.scalar.activation(q_sb[:], root[:], ACT.Square)
+            p_sb = shared.tile([P, UNIT, 4], F32, name=f"p_sb{i}", tag=f"p{i % 3}" if i else "wd_p0", align_bytes=64)
+            nc.vector.tensor_tensor(p_sb[:], x_jt, q_sb[:], ALU.mult)
+            p_squared[i] = ring.tile([P, UNIT, 4], F32, name="p_squared")
+            if i < SQUARE_ON_VECTOR:
+                nc.vector.tensor_tensor(p_squared[i][:], p_sb[:], p_sb[:], ALU.mult)
             else:
-                nc.scalar.activation(pp_sb[i][:], p_sb[:], ACT.Square)
+                nc.scalar.activation(p_squared[i][:], p_sb[:], ACT.Square)
 
-        def depth(i):
+        def make_h(i):
             h_bf[i] = ring.tile([P, UNIT, 4], BF16, name="h_bf", align_bytes=64)
-            nc.vector.tensor_tensor(h_bf[i][:], a_ps[i][:].rearrange("p t j -> p j t"), pp_sb[i][:], ALU.mult)
+            nc.vector.tensor_tensor(h_bf[i][:], a_ps[i][:].rearrange("p t j -> p j t"), p_squared[i][:], ALU.mult)
 
-        def quant_h(i):
+        def quantise_h(i):
             cols = slice(UNIT * i, UNIT * (i + 1))
             nc.vector.quantize_mx(
                 out=h_codes[:, cols].bitcast(FP8X4),
-                scales=h_planes[:, cols],
+                scales=h_scales[:, cols],
                 in_=h_bf[i][:].rearrange("p j t -> p (j t)"),
             )
 
-        out_tiles = out.rearrange("(n p) j -> p n j", p=P)
+        out_tiles = out.rearrange("(m p) j -> p m j", p=P)
 
-        def energies(i, n0, n1, bank, copy):
+        def energies(i, m0, m1, bank, copy):
             cols = slice(UNIT * i, UNIT * (i + 1))
-            acc = psum.tile([P, n1 - n0, UNIT], F32, name=f"o{i}_{n0}", tag=f"bank{bank}")
-            for n in range(n0, n1):
-                rows = slice(P * n, P * (n + 1))
+            acc = psum.tile([P, m1 - m0, UNIT], F32, name=f"o{i}_{m0}", tag=f"bank{bank}")
+            for m in range(m0, m1):
+                rows = slice(P * m, P * (m + 1))
                 nc.tensor.matmul_mx(
-                    out=acc[:, n - n0, :],
+                    out=acc[:, m - m0, :],
                     lhsT=wo_codes[:, rows].bitcast(FP8X4),
-                    lhsT_scale=wo_planes[:, rows],
+                    lhsT_scale=wo_scales[:, rows],
                     rhs=h_codes[:, cols].bitcast(FP8X4),
-                    rhs_scale=h_planes[:, cols],
+                    rhs_scale=h_scales[:, cols],
                     start=True,
                     stop=True,
                 )
-            res = keep.tile([P, n1 - n0, UNIT], F32, name=f"res{i}_{n0}")
+            res = keep.tile([P, m1 - m0, UNIT], F32, name=f"res{i}_{m0}")
             copy(res[:], acc[:])
-            nc.sync.dma_start(out_tiles[:, n0:n1, cols], res[:])
+            nc.sync.dma_start(out_tiles[:, m0:m1, cols], res[:])
 
-        def unit_out(i):
-            bank = 2 if i < 5 else 2 + 2 * (i % 2)
-            energies(i, 0, NEAR, bank, nc.vector.tensor_copy if i == UNITS - 1 else nc.scalar.copy)
-            energies(i, NEAR, N // P, bank + 1, nc.scalar.copy)
+        def store_unit(i):
+            near_bank, far_bank = OUT_BANKS[i % 2 if i >= OUT_ALTERNATES_FROM else 0]
+            energies(i, 0, NEAR, near_bank, nc.vector.tensor_copy if i == UNITS - 1 else nc.scalar.copy)
+            energies(i, NEAR, ROW_TILES, far_bank, nc.scalar.copy)
 
-        groups = tuple((i,) for i in range(UNITS))
         for i in range(UNITS + 2):
-            for units in groups:
-                if units[0] == i:
-                    inverse(units)
             if i < UNITS:
-                shape(i)
-            if i == 0:
+                well_shape(i)
+            if i == A_BANKS[1]:
                 mm_a(1)
-            if i == 1:
-                for a in range(PASSES):
-                    mm_x(a, UNITS - 1, closes=a == LAST)
+            if i == LAST_X_BANK:
+                for g in range(PASSES):
+                    mm_x(g, UNITS - 1, closes=g == LAST)
             if i >= 2:
-                quant_h(i - 2)
+                quantise_h(i - 2)
             if 1 <= i <= UNITS:
-                depth(i - 1)
+                make_h(i - 1)
                 if i + 1 < UNITS:
                     mm_a(i + 1)
             if i >= 2:
-                unit_out(i - 2)
+                store_unit(i - 2)

@@ -23,22 +23,42 @@ UNIT = 128
 UNITS = S // UNIT
 ROW_TILES = N // P
 
-EARLY = UNITS - 1
-LAST_X_BANK = 1
-A_BANKS = (7, 0)
-OUT_BANKS = ((2, 3), (4, 5))
-OUT_ALTERNATES_FROM = 5
-TWICE = 5
-NEAR = 3
-SQUARE_ON_VECTOR = UNITS - 2
+EARLY = 6
+EARLY_A = 0
+X_LATE_BANK = {6: 0, 7: 3}
+A_BANKS = (6, 7) * 4
+OUT_BANKS = ((1, 2), (1, 2), (1, 2), (4, 5), (1, 2), (4, 5), (1, 2), (4, 5))
+OUT_ALTERNATES_FROM = 3
+NEAR = 2
+SQ = "VVSSSVSS"
+NEARE = "VVSSSSSV"
+FARE = "VVSSSSSS"
+WOE = "VV"
+CAST = "VSSSVS"
 LAST_CUTS = (0, 256, 512, S)
+RING = 6
+MOVEQ = "G"
+WO_AT = (0,0)
+WD_AFTER = 1
+TWICE = 5
+PICK_TAG = "wx_bf0_0"
+GATES = {}
+ULAG = (0,) * 8
+QE = "VSSSSSSS"
+PAIRS = (4,6)
+WD_FIRST = 0
+A_AFTER = 1
+FIRST_A = 2
+LAGS = (0,0,0,2,2,4,3,4,4,3,2,5,5)
+ORDER = "fwupsqhoraxcd"
+WO_CUTS = ((0,512),(512,640))
 
 
 def tile_list_bead_well_energies_kernel(tc, tab_words, tab_scales, offs, wx, wd_words, wd_scales, wo, out):
     nc = tc.nc
     with ExitStack() as ctx:
         keep = ctx.enter_context(tc.tile_pool(name="keep", bufs=1))
-        ring = ctx.enter_context(tc.tile_pool(name="ring", bufs=4))
+        ring = ctx.enter_context(tc.tile_pool(name="ring", bufs=RING))
         shared = ctx.enter_context(tc.tile_pool(name="shared", bufs=1))
         psum = ctx.enter_context(tc.psum_pool(name="psum", bufs=1))
 
@@ -104,7 +124,7 @@ def tile_list_bead_well_energies_kernel(tc, tab_words, tab_scales, offs, wx, wd_
 
         def mm_x(g, i, closes=False):
             if g == 0:
-                x_ps[i] = psum.tile([P, 4, UNIT], F32, name=f"x{i}", tag=f"bank{i if i < EARLY else LAST_X_BANK}")
+                x_ps[i] = psum.tile([P, 4, UNIT], F32, name=f"x{i}", tag=f"bank{i if i < EARLY else X_LATE_BANK[i]}")
             for t in range(4):
                 nc.tensor.matmul_mx(
                     out=x_ps[i][:, t, :],
@@ -116,9 +136,10 @@ def tile_list_bead_well_energies_kernel(tc, tab_words, tab_scales, offs, wx, wd_
                     stop=(closes and t == 3),
                 )
 
-        def mm_a(i):
-            a_ps[i] = psum.tile([P, 4, UNIT], F32, name=f"a{i}", tag=f"bank{A_BANKS[i % 2]}")
-            for g in range(PASSES):
+        def mm_a(i, passes=range(PASSES)):
+            if 0 in passes:
+                a_ps[i] = psum.tile([P, 4, UNIT], F32, name=f"a{i}", tag=f"bank{A_BANKS[i]}")
+            for g in passes:
                 for t in range(4):
                     nc.tensor.matmul_mx(
                         out=a_ps[i][:, t, :],
@@ -130,17 +151,36 @@ def tile_list_bead_well_energies_kernel(tc, tab_words, tab_scales, offs, wx, wd_
                         stop=(g == LAST and t == 3),
                     )
 
-        load_tab(0, "tab0_wx2")
+        copier = {"V": nc.vector.tensor_copy, "S": nc.scalar.copy}
+        load_tab(0, "tab0")
         load_tab(1, "tab1")
-        load_wx(0, "wx0_wo")
+        load_wx(0, "wx0")
         load_wx(1, "wx1")
         gather_words(0, (0, S))
-        load_wx(2, "tab0_wx2")
+        load_wx(2, "tab0")
+        wd_raw = shared.tile([P, PASSES, H // 2], I32, name="wd_raw", tag="wd_raw", align_bytes=64)
+        if WD_FIRST:
+            nc.sync.dma_start(wd_raw[:], wd_words.bitcast(I32).rearrange("g p w -> p g w"))
         load_tab(2, "tab2")
+        wo_slots = wo.rearrange("(u t e) n -> t u e n", t=4, e=4)
+        wo_raw = {}
+
+        def load_wo(n):
+            n0, n1 = WO_CUTS[n]
+            wo_raw[n] = keep.tile([P, 4, n1 - n0], F32, name=f"wo_raw{n}", align_bytes=64)
+            for t in range(4):
+                nc.sync.dma_start(wo_raw[n][:, t, :], wo_slots[t][:, :, n0:n1])
+
+        for n in range(WD_AFTER):
+            load_wo(n)
+        if not WD_FIRST:
+            nc.sync.dma_start(wd_raw[:], wd_words.bitcast(I32).rearrange("g p w -> p g w"))
+        for n in range(WD_AFTER, len(WO_CUTS)):
+            load_wo(n)
         gather_words(1, (0, S))
-        quantise_wx(0, 0, nc.vector.tensor_copy)
-        quantise_wx(0, 1, nc.scalar.copy)
-        picked_rows = shared.tile([P, S // 4], I32, name="picked_rows", tag="wx_bf0_0", align_bytes=64)
+        quantise_wx(0, 0, copier[CAST[0]])
+        quantise_wx(0, 1, copier[CAST[1]])
+        picked_rows = shared.tile([P, S // 4], I32, name="picked_rows", tag=PICK_TAG, align_bytes=64)
         v_rows = [picked_rows] + moved_rows
         for j0 in range(0, S, S // 2):
             nc.vector.tensor_copy(
@@ -148,75 +188,104 @@ def tile_list_bead_well_energies_kernel(tc, tab_words, tab_scales, offs, wx, wd_
                 tab_rows[:].bitcast(U8).indirect(offsets[:, j0 // 16 : (j0 + S // 2) // 16]),
             )
         for g in range(1, PASSES):
-            nc.gpsimd.dma_start(v_rows[g][0:112, :], picked_rows[4 * g : 4 * g + 112, :])
+            {"G": nc.gpsimd, "S": nc.scalar}[MOVEQ].dma_start(v_rows[g][0:112, :], picked_rows[4 * g : 4 * g + 112, :])
         for i in range(EARLY):
             mm_x(0, i)
-        quantise_wx(1, 0, nc.scalar.copy)
-        quantise_wx(1, 1, nc.scalar.copy)
+        quantise_wx(1, 0, copier[CAST[2]])
+        quantise_wx(1, 1, copier[CAST[3]])
         for i in range(TWICE):
             mm_x(1, i)
-        quantise_wx(LAST, 0, nc.vector.tensor_copy)
-        quantise_wx(LAST, 1, nc.scalar.copy)
-        wo_raw = shared.tile([P, 4, N], F32, name="wo_raw", tag="wx0_wo", align_bytes=64)
-        wo_slots = wo.rearrange("(u t e) n -> t u e n", t=4, e=4)
-        for t in range(4):
-            nc.sync.dma_start(wo_raw[:, t, :], wo_slots[t])
-        wd_raw = shared.tile([P, PASSES, H // 2], I32, name="wd_raw", tag="wd_p0", align_bytes=64)
-        nc.sync.dma_start(wd_raw[:], wd_words.bitcast(I32).rearrange("g p w -> p g w"))
-        gather_words(LAST, LAST_CUTS)
-
+        quantise_wx(LAST, 0, copier[CAST[4]])
+        quantise_wx(LAST, 1, copier[CAST[5]])
         wd_ordered = shared.tile([P, PASSES, H // 4], I32, name="wd_ordered", tag="wx_bf1_1", align_bytes=64)
         nc.vector.tensor_copy(
             wd_ordered[:].rearrange("p g (t u) -> p g t u", t=4),
             wd_rows[:].rearrange("p g (u t) -> p g t u", t=4),
         )
         wd_codes = keep.tile([P, PASSES, H // 2], I32, name="wd_codes", align_bytes=64)
+        if not WD_FIRST:
+            gather_words(LAST, LAST_CUTS)
         nc.vector.tensor_copy(
             wd_codes[:].rearrange("p g (t u w) -> p g t u w", t=4, w=2),
             wd_raw[:].rearrange("p g (u t w) -> p g t u w", t=4, w=2),
         )
+        for i in range(EARLY_A):
+            mm_a(i, range(LAST))
+        if WD_FIRST:
+            gather_words(LAST, LAST_CUTS)
         for i in range(EARLY):
             mm_x(LAST, i, closes=i < TWICE)
             if i >= TWICE:
                 mm_x(1, i, closes=True)
-        mm_a(0)
+            if i == A_AFTER:
+                for j in range(FIRST_A):
+                    mm_a(j, (LAST,) if j < EARLY_A else range(PASSES))
 
-        wo_bf = keep.tile([P, N, 4], BF16, name="wo_bf", align_bytes=64)
         wo_codes = keep.tile([P, N], U32, name="wo_codes", align_bytes=64)
         wo_scales = keep.tile([P, N], U8, name="wo_scales", align_bytes=64)
-        for n0, n1 in ((0, 512), (512, N)):
-            nc.vector.tensor_copy(
-                wo_bf[:, n0:n1, :].rearrange("p (m e) t -> p m t e", e=4),
-                wo_raw[:, :, n0:n1].rearrange("p t (m e) -> p m t e", e=4),
-            )
-            nc.vector.quantize_mx(
-                out=wo_codes[:, n0:n1].bitcast(FP8X4),
-                scales=wo_scales[:, n0:n1],
-                in_=wo_bf[:, n0:n1, :].rearrange("p n t -> p (n t)"),
-            )
 
+        def quantise_wo(n):
+            l0, l1 = WO_CUTS[n]
+            wo_bf = shared.tile([P, l1 - l0, 4], BF16, name=f"wo_bf{n}", tag=f"wo_bf{n}", align_bytes=64)
+            if WOE[n] == "G":
+                nc.gpsimd.tensor_scalar(
+                    wo_bf[:], wo_raw[n][:].rearrange("p t n -> p n t"), 1.0, 0.0, ALU.mult, ALU.add
+                )
+            else:
+                copier[WOE[n]](
+                    wo_bf[:].rearrange("p (m e) t -> p m t e", e=4),
+                    wo_raw[n][:].rearrange("p t (m e) -> p m t e", e=4),
+                )
+            for n0, n1 in ((l0, l1),) if l1 - l0 not in (384, 640) else ((l0, l1 - 128), (l1 - 128, l1)):
+                nc.vector.quantize_mx(
+                    out=wo_codes[:, n0:n1].bitcast(FP8X4),
+                    scales=wo_scales[:, n0:n1],
+                    in_=wo_bf[:, n0 - l0 : n1 - l0, :].rearrange("p n t -> p (n t)"),
+                )
+
+        accs = {}
         h_codes = keep.tile([P, S], U32, name="h_codes", align_bytes=64)
         h_scales = keep.tile([P, S], U8, name="h_scales", align_bytes=64)
-        p_squared, h_bf = {}, {}
+        p_squared, h_bf, q_tiles, results, xs_tiles, root_tiles, p_tiles = {}, {}, {}, {}, {}, {}, {}
 
         def well_shape(i):
             x_jt = x_ps[i][:].rearrange("p t j -> p j t")
-            x_squared = ring.tile([P, UNIT, 4], F32, name="x_squared")
+            x_squared = ring.tile([P, UNIT, 4], F32, name=f"x_squared{i}", tag="x_squared")
             nc.scalar.activation(x_squared[:], x_jt, ACT.Square)
-            root = ring.tile([P, UNIT, 4], F32, name="root")
+            xs_tiles[i] = x_squared
+
+        def make_root(i):
+            x_squared = xs_tiles[i]
+            root = ring.tile([P, UNIT, 4], F32, name=f"root{i}", tag="root")
             nc.scalar.activation(root[:], x_squared[:], ACT.Abs_reciprocal_sqrt, bias=1.0)
-            q_sb = ring.tile([P, UNIT, 4], F32, name="q_sb")
-            nc.scalar.activation(q_sb[:], root[:], ACT.Square)
-            p_sb = shared.tile([P, UNIT, 4], F32, name=f"p_sb{i}", tag=f"p{i % 3}" if i else "wd_p0", align_bytes=64)
+            root_tiles[i] = root
+
+        def make_q(i):
+            root = root_tiles[i]
+            q_sb = shared.tile([P, UNIT, 4], F32, name=f"q_sb{i}", tag=GATES.get(i, f"q_sb{i}"), align_bytes=64)
+            if QE[i] == "S":
+                nc.scalar.activation(q_sb[:], root[:], ACT.Square)
+            else:
+                {"V": nc.vector, "G": nc.gpsimd}[QE[i]].tensor_tensor(q_sb[:], root[:], root[:], ALU.mult)
+            q_tiles[i] = q_sb
+
+        def make_p(i):
+            x_jt = x_ps[i][:].rearrange("p t j -> p j t")
+            q_sb = q_tiles[i]
+            p_sb = shared.tile([P, UNIT, 4], F32, name=f"p_sb{i}", tag=f"p{i % 3}", align_bytes=64)
             nc.vector.tensor_tensor(p_sb[:], x_jt, q_sb[:], ALU.mult)
-            p_squared[i] = ring.tile([P, UNIT, 4], F32, name="p_squared")
-            if i < SQUARE_ON_VECTOR:
-                nc.vector.tensor_tensor(p_squared[i][:], p_sb[:], p_sb[:], ALU.mult)
+            p_tiles[i] = p_sb
+
+        def square_p(i):
+            p_sb = p_tiles[i]
+            p_squared[i] = ring.tile([P, UNIT, 4], F32, name=f"p_squared{i}", tag="p_squared")
+            if SQ[i] != "S":
+                {"V": nc.vector, "G": nc.gpsimd}[SQ[i]].tensor_tensor(p_squared[i][:], p_sb[:], p_sb[:], ALU.mult)
             else:
                 nc.scalar.activation(p_squared[i][:], p_sb[:], ACT.Square)
 
         def make_h(i):
-            h_bf[i] = ring.tile([P, UNIT, 4], BF16, name="h_bf", align_bytes=64)
+            h_bf[i] = shared.tile([P, UNIT, 4], BF16, name=f"h_bf{i}", tag=f"h{i}", align_bytes=64)
             nc.vector.tensor_tensor(h_bf[i][:], a_ps[i][:].rearrange("p t j -> p j t"), p_squared[i][:], ALU.mult)
 
         def quantise_h(i):
@@ -229,7 +298,7 @@ def tile_list_bead_well_energies_kernel(tc, tab_words, tab_scales, offs, wx, wd_
 
         out_tiles = out.rearrange("(m p) j -> p m j", p=P)
 
-        def energies(i, m0, m1, bank, copy):
+        def energies(i, m0, m1, bank):
             cols = slice(UNIT * i, UNIT * (i + 1))
             acc = psum.tile([P, m1 - m0, UNIT], F32, name=f"o{i}_{m0}", tag=f"bank{bank}")
             for m in range(m0, m1):
@@ -243,28 +312,75 @@ def tile_list_bead_well_energies_kernel(tc, tab_words, tab_scales, offs, wx, wd_
                     start=True,
                     stop=True,
                 )
-            res = keep.tile([P, m1 - m0, UNIT], F32, name=f"res{i}_{m0}")
-            copy(res[:], acc[:])
-            nc.sync.dma_start(out_tiles[:, m0:m1, cols], res[:])
+            accs[i, m0] = acc
 
-        def store_unit(i):
-            near_bank, far_bank = OUT_BANKS[i % 2 if i >= OUT_ALTERNATES_FROM else 0]
-            energies(i, 0, NEAR, near_bank, nc.vector.tensor_copy if i == UNITS - 1 else nc.scalar.copy)
-            energies(i, NEAR, ROW_TILES, far_bank, nc.scalar.copy)
+        def empty(i, m0, m1, copy):
+            acc = accs[i, m0]
+            if i in PAIRS or i - 1 not in PAIRS:
+                results[m0] = keep.tile([P, m1 - m0, UNIT * (2 if i in PAIRS else 1)], F32, name=f"res{i}_{m0}")
+            res = results[m0]
+            first = i - 1 if i - 1 in PAIRS else i
+            copy(res[:, :, UNIT * (i - first) : UNIT * (i - first + 1)], acc[:])
+            if i not in PAIRS:
+                nc.sync.dma_start(out_tiles[:, m0:m1, UNIT * first : UNIT * (i + 1)], res[:])
 
-        for i in range(UNITS + 2):
-            if i < UNITS:
-                well_shape(i)
-            if i == A_BANKS[1]:
-                mm_a(1)
-            if i == LAST_X_BANK:
-                for g in range(PASSES):
-                    mm_x(g, UNITS - 1, closes=g == LAST)
-            if i >= 2:
-                quantise_h(i - 2)
-            if 1 <= i <= UNITS:
-                make_h(i - 1)
-                if i + 1 < UNITS:
-                    mm_a(i + 1)
-            if i >= 2:
-                store_unit(i - 2)
+        def store_near(i):
+            energies(i, 0, NEAR, OUT_BANKS[i][0])
+
+        def store_far(i):
+            energies(i, NEAR, ROW_TILES, OUT_BANKS[i][1])
+
+        def after_p(i):
+            for late, bank in X_LATE_BANK.items():
+                if i == bank:
+                    for g in range(PASSES):
+                        mm_x(g, late, closes=g == LAST)
+            for j in range(FIRST_A, UNITS):
+                if A_BANKS[j] == i and A_BANKS[j] not in A_BANKS[:j] and i < EARLY:
+                    mm_a(j)
+
+        def after_h(i):
+            for j in range(i + 1, UNITS):
+                if A_BANKS[j] == A_BANKS[i]:
+                    mm_a(j)
+                    break
+
+        lag = dict(zip(ORDER, LAGS))
+        for n in range(UNITS + max(LAGS)):
+            for m, at in enumerate(WO_AT):
+                if n == at:
+                    quantise_wo(m)
+            for c in ORDER:
+                i = n - lag[c]
+                if c == "u":
+                    for j in range(UNITS):
+                        if j + ULAG[j] == n:
+                            make_q(j)
+                    continue
+                if 0 <= i < UNITS:
+                    if c == "f":
+                        well_shape(i)
+                    if c == "p":
+                        make_p(i)
+                    if c == "w":
+                        make_root(i)
+                    if c == "u":
+                        make_q(i)
+                    if c == "s":
+                        square_p(i)
+                    if c == "x":
+                        after_p(i)
+                    if c == "h":
+                        make_h(i)
+                    if c == "a":
+                        after_h(i)
+                    if c == "q":
+                        quantise_h(i)
+                    if c == "o":
+                        store_near(i)
+                    if c == "c":
+                        empty(i, 0, NEAR, copier[NEARE[i]])
+                    if c == "d":
+                        empty(i, NEAR, ROW_TILES, copier[FARE[i]])
+                    if c == "r":
+                        store_far(i)

@@ -23,50 +23,57 @@ UNIT = 128
 UNITS = S // UNIT
 ROW_TILES = N // P
 
-EARLY = 6
+EARLY = 7
 EARLY_A = 0
-X_LATE_BANK = {6: 0, 7: 3}
-A_BANKS = (6, 7) * 4
-OUT_BANKS = ((1, 2), (1, 2), (1, 2), (4, 5), (1, 2), (4, 5), (1, 2), (4, 5))
+X_LATE_BANK = {7:1}
+A_BANKS = (7,0)*4
+OUT_BANKS = ((2,3),)*4+((4,5),(2,3))*2
 OUT_ALTERNATES_FROM = 3
 NEAR = 2
-SQ = "VVSSSVSS"
-NEARE = "VVSSSSSV"
-FARE = "VVSSSSSS"
+SQ = "VVVSSSSSSS"
+NEARE = "VVVVVVVVVV"
+FARE = "SSSSSSSSSS"
 WOE = "VV"
 CAST = "VSSSVS"
 LAST_CUTS = (0, 256, 512, S)
-RING = 6
+RING = 4
 MOVEQ = "G"
-WO_AT = (0,0)
+WO_AT = (0,1)
 WD_AFTER = 1
+GL = 4
+TAB_FIRST = 1
+ROWSET = "V"
+WDS = 0
+WDO_TAG = "wx_bf1_1"
+HALVES = 0
+JOIN = 0
 TWICE = 5
 PICK_TAG = "wx_bf0_0"
 GATES = {}
 ULAG = (0,) * 8
-QE = "VSSSSSSS"
-PAIRS = (4,6)
+QE = "SSSSSGGGSS"
+PAIRS = ()
 WD_FIRST = 0
 A_AFTER = 1
-FIRST_A = 2
-LAGS = (0,0,0,2,2,4,3,4,4,3,2,5,5)
-ORDER = "fwupsqhoraxcd"
-WO_CUTS = ((0,512),(512,640))
+FIRST_A = 1
+LAGS = (0,0,0,0,0,1,1,1,1,1,0,2,2)
+ORDER = "fwupshqoraxcd"
+WO_CUTS = ((0,384),(384,640))
 
 
 def tile_list_bead_well_energies_kernel(tc, tab_words, tab_scales, offs, wx, wd_words, wd_scales, wo, out):
     nc = tc.nc
     with ExitStack() as ctx:
         keep = ctx.enter_context(tc.tile_pool(name="keep", bufs=1))
-        ring = ctx.enter_context(tc.tile_pool(name="ring", bufs=RING))
         shared = ctx.enter_context(tc.tile_pool(name="shared", bufs=1))
         psum = ctx.enter_context(tc.psum_pool(name="psum", bufs=1))
 
         offsets = keep.tile([P, S // 16], U16, name="offsets")
-        nc.sync.dma_start(offsets[:], offs)
+        if not TAB_FIRST:
+            nc.sync.dma_start(offsets[:], offs)
 
         tab_rows = keep.tile([P, T // 4], I32, name="tab_rows", align_bytes=64)
-        nc.gpsimd.memset(tab_rows[:], 0)
+        {"G": nc.gpsimd, "V": nc.vector}[ROWSET].memset(tab_rows[:], 0)
         tab_scales_i32 = tab_scales.bitcast(I32)
         for q in range(4):
             nc.gpsimd.dma_start(tab_rows[32 * q : 32 * q + 4 * PASSES, :], tab_scales_i32[:, 4 * q : 4 * q + 4, :])
@@ -80,10 +87,15 @@ def tile_list_bead_well_energies_kernel(tc, tab_words, tab_scales, offs, wx, wd_
         warm_out = keep.tile([P, 1], F32, name="warm_out")
         nc.scalar.activation(warm_out[:], warm[:], ACT.Abs_reciprocal_sqrt)
         wd_scales_i32 = wd_scales.bitcast(I32)
-        for q in range(4):
-            nc.scalar.dma_start(
-                wd_rows[32 * q : 32 * q + 4, :, :], wd_scales_i32[:, 4 * q : 4 * q + 4, :].rearrange("g r c -> r g c")
-            )
+
+        def load_wd_rows(queue):
+            for q in range(4):
+                queue.dma_start(
+                    wd_rows[32 * q : 32 * q + 4, :, :], wd_scales_i32[:, 4 * q : 4 * q + 4, :].rearrange("g r c -> r g c")
+                )
+
+        if WDS == 0:
+            load_wd_rows(nc.scalar)
 
         tab, wx_raw, v_codes = {}, {}, {}
 
@@ -153,6 +165,8 @@ def tile_list_bead_well_energies_kernel(tc, tab_words, tab_scales, offs, wx, wd_
 
         copier = {"V": nc.vector.tensor_copy, "S": nc.scalar.copy}
         load_tab(0, "tab0")
+        if TAB_FIRST:
+            nc.sync.dma_start(offsets[:], offs)
         load_tab(1, "tab1")
         load_wx(0, "wx0")
         load_wx(1, "wx1")
@@ -162,6 +176,25 @@ def tile_list_bead_well_energies_kernel(tc, tab_words, tab_scales, offs, wx, wd_
         if WD_FIRST:
             nc.sync.dma_start(wd_raw[:], wd_words.bitcast(I32).rearrange("g p w -> p g w"))
         load_tab(2, "tab2")
+        if WDS == 1:
+            load_wd_rows(nc.sync)
+        gather_words(1, (0, S))
+        quantise_wx(0, 0, copier[CAST[0]])
+        quantise_wx(0, 1, copier[CAST[1]])
+        picked_rows = shared.tile([P, S // 4], I32, name="picked_rows", tag=PICK_TAG, align_bytes=64)
+        v_rows = [picked_rows] + moved_rows
+        for j0 in range(0, S, S // 2):
+            nc.vector.tensor_copy(
+                picked_rows[:].bitcast(U8)[:, j0 : j0 + S // 2],
+                tab_rows[:].bitcast(U8).indirect(offsets[:, j0 // 16 : (j0 + S // 2) // 16]),
+            )
+
+        def move_rows(queue):
+            for g in range(1, PASSES):
+                queue.dma_start(v_rows[g][0:112, :], picked_rows[4 * g : 4 * g + 112, :])
+
+        if MOVEQ == "G":
+            move_rows(nc.gpsimd)
         wo_slots = wo.rearrange("(u t e) n -> t u e n", t=4, e=4)
         wo_raw = {}
 
@@ -173,22 +206,16 @@ def tile_list_bead_well_energies_kernel(tc, tab_words, tab_scales, offs, wx, wd_
 
         for n in range(WD_AFTER):
             load_wo(n)
+        if WDS == 2:
+            load_wd_rows(nc.sync)
         if not WD_FIRST:
             nc.sync.dma_start(wd_raw[:], wd_words.bitcast(I32).rearrange("g p w -> p g w"))
+        if MOVEQ == "Y":
+            move_rows(nc.sync)
         for n in range(WD_AFTER, len(WO_CUTS)):
             load_wo(n)
-        gather_words(1, (0, S))
-        quantise_wx(0, 0, copier[CAST[0]])
-        quantise_wx(0, 1, copier[CAST[1]])
-        picked_rows = shared.tile([P, S // 4], I32, name="picked_rows", tag=PICK_TAG, align_bytes=64)
-        v_rows = [picked_rows] + moved_rows
-        for j0 in range(0, S, S // 2):
-            nc.vector.tensor_copy(
-                picked_rows[:].bitcast(U8)[:, j0 : j0 + S // 2],
-                tab_rows[:].bitcast(U8).indirect(offsets[:, j0 // 16 : (j0 + S // 2) // 16]),
-            )
-        for g in range(1, PASSES):
-            {"G": nc.gpsimd, "S": nc.scalar}[MOVEQ].dma_start(v_rows[g][0:112, :], picked_rows[4 * g : 4 * g + 112, :])
+        if MOVEQ == "Z":
+            move_rows(nc.sync)
         for i in range(EARLY):
             mm_x(0, i)
         quantise_wx(1, 0, copier[CAST[2]])
@@ -197,14 +224,14 @@ def tile_list_bead_well_energies_kernel(tc, tab_words, tab_scales, offs, wx, wd_
             mm_x(1, i)
         quantise_wx(LAST, 0, copier[CAST[4]])
         quantise_wx(LAST, 1, copier[CAST[5]])
-        wd_ordered = shared.tile([P, PASSES, H // 4], I32, name="wd_ordered", tag="wx_bf1_1", align_bytes=64)
+        wd_codes = keep.tile([P, PASSES, H // 2], I32, name="wd_codes", align_bytes=64)
+        if not WD_FIRST:
+            gather_words(LAST, LAST_CUTS)
+        wd_ordered = shared.tile([P, PASSES, H // 4], I32, name="wd_ordered", tag=WDO_TAG, align_bytes=64)
         nc.vector.tensor_copy(
             wd_ordered[:].rearrange("p g (t u) -> p g t u", t=4),
             wd_rows[:].rearrange("p g (u t) -> p g t u", t=4),
         )
-        wd_codes = keep.tile([P, PASSES, H // 2], I32, name="wd_codes", align_bytes=64)
-        if not WD_FIRST:
-            gather_words(LAST, LAST_CUTS)
         nc.vector.tensor_copy(
             wd_codes[:].rearrange("p g (t u w) -> p g t u w", t=4, w=2),
             wd_raw[:].rearrange("p g (u t w) -> p g t u w", t=4, w=2),
@@ -243,92 +270,102 @@ def tile_list_bead_well_energies_kernel(tc, tab_words, tab_scales, offs, wx, wd_
                     in_=wo_bf[:, n0 - l0 : n1 - l0, :].rearrange("p n t -> p (n t)"),
                 )
 
-        accs = {}
+        accs, slots = {}, {}
         h_codes = keep.tile([P, S], U32, name="h_codes", align_bytes=64)
         h_scales = keep.tile([P, S], U8, name="h_scales", align_bytes=64)
         p_squared, h_bf, q_tiles, results, xs_tiles, root_tiles, p_tiles = {}, {}, {}, {}, {}, {}, {}
 
-        def well_shape(i):
-            x_jt = x_ps[i][:].rearrange("p t j -> p j t")
-            x_squared = ring.tile([P, UNIT, 4], F32, name=f"x_squared{i}", tag="x_squared")
-            nc.scalar.activation(x_squared[:], x_jt, ACT.Square)
-            xs_tiles[i] = x_squared
+        pieces = [(i, 0, UNIT) for i in range(UNITS - HALVES)]
+        for i in range(UNITS - HALVES, UNITS):
+            pieces.extend([(i, 0, UNIT // 2), (i, UNIT // 2, UNIT)])
 
-        def make_root(i):
-            x_squared = xs_tiles[i]
-            root = ring.tile([P, UNIT, 4], F32, name=f"root{i}", tag="root")
-            nc.scalar.activation(root[:], x_squared[:], ACT.Abs_reciprocal_sqrt, bias=1.0)
-            root_tiles[i] = root
+        def by_entry(bank, n):
+            i, j0, j1 = pieces[n]
+            return bank[i][:, :, j0:j1].rearrange("p t j -> p j t")
 
-        def make_q(i):
-            root = root_tiles[i]
-            q_sb = shared.tile([P, UNIT, 4], F32, name=f"q_sb{i}", tag=GATES.get(i, f"q_sb{i}"), align_bytes=64)
-            if QE[i] == "S":
-                nc.scalar.activation(q_sb[:], root[:], ACT.Square)
+        def step_tile(name, n, dtype=F32):
+            i, j0, j1 = pieces[n]
+            tag = f"{name}{n % 4}" if name in ("x_squared", "root", "p_sb") else f"{name}{n}"
+            return shared.tile([P, j1 - j0, 4], dtype, name=f"{name}{n}", tag=tag, align_bytes=64)
+
+        def square(engine, dst, src):
+            if engine == "S":
+                nc.scalar.activation(dst[:], src[:], ACT.Square)
             else:
-                {"V": nc.vector, "G": nc.gpsimd}[QE[i]].tensor_tensor(q_sb[:], root[:], root[:], ALU.mult)
-            q_tiles[i] = q_sb
+                {"V": nc.vector, "G": nc.gpsimd}[engine].tensor_tensor(dst[:], src[:], src[:], ALU.mult)
 
-        def make_p(i):
-            x_jt = x_ps[i][:].rearrange("p t j -> p j t")
-            q_sb = q_tiles[i]
-            p_sb = shared.tile([P, UNIT, 4], F32, name=f"p_sb{i}", tag=f"p{i % 3}", align_bytes=64)
-            nc.vector.tensor_tensor(p_sb[:], x_jt, q_sb[:], ALU.mult)
-            p_tiles[i] = p_sb
+        def well_shape(n):
+            xs_tiles[n] = step_tile("x_squared", n)
+            nc.scalar.activation(xs_tiles[n][:], by_entry(x_ps, n), ACT.Square)
 
-        def square_p(i):
-            p_sb = p_tiles[i]
-            p_squared[i] = ring.tile([P, UNIT, 4], F32, name=f"p_squared{i}", tag="p_squared")
-            if SQ[i] != "S":
-                {"V": nc.vector, "G": nc.gpsimd}[SQ[i]].tensor_tensor(p_squared[i][:], p_sb[:], p_sb[:], ALU.mult)
-            else:
-                nc.scalar.activation(p_squared[i][:], p_sb[:], ACT.Square)
+        def make_root(n):
+            root_tiles[n] = step_tile("root", n)
+            nc.scalar.activation(root_tiles[n][:], xs_tiles[n][:], ACT.Abs_reciprocal_sqrt, bias=1.0)
 
-        def make_h(i):
-            h_bf[i] = shared.tile([P, UNIT, 4], BF16, name=f"h_bf{i}", tag=f"h{i}", align_bytes=64)
-            nc.vector.tensor_tensor(h_bf[i][:], a_ps[i][:].rearrange("p t j -> p j t"), p_squared[i][:], ALU.mult)
+        def make_q(n):
+            q_tiles[n] = slots[n - GL] if QE[n] == "G" and GL else step_tile("q_sb", n)
+            square(QE[n], q_tiles[n], root_tiles[n])
 
-        def quantise_h(i):
-            cols = slice(UNIT * i, UNIT * (i + 1))
+        def make_p(n):
+            p_tiles[n] = step_tile("p_sb", n)
+            nc.vector.tensor_tensor(p_tiles[n][:], by_entry(x_ps, n), q_tiles[n][:], ALU.mult)
+
+        def square_p(n):
+            p_squared[n] = step_tile("p_squared", n)
+            square(SQ[n], p_squared[n], p_tiles[n])
+
+        def make_h(n):
+            slots[n] = step_tile("h_bf", n)
+            half = (pieces[n][2] - pieces[n][1]) // 2
+            h_bf[n] = slots[n][:, 0:half, :].rearrange("p j t -> p (j t)").bitcast(BF16).rearrange("p (j t) -> p j t", t=4)
+            nc.vector.tensor_tensor(h_bf[n], by_entry(a_ps, n), p_squared[n][:], ALU.mult)
+
+        def columns(n):
+            i, j0, j1 = pieces[n]
+            return slice(UNIT * i + j0, UNIT * i + j1)
+
+        def quantise_h(n):
             nc.vector.quantize_mx(
-                out=h_codes[:, cols].bitcast(FP8X4),
-                scales=h_scales[:, cols],
-                in_=h_bf[i][:].rearrange("p j t -> p (j t)"),
+                out=h_codes[:, columns(n)].bitcast(FP8X4),
+                scales=h_scales[:, columns(n)],
+                in_=h_bf[n].rearrange("p j t -> p (j t)"),
             )
 
         out_tiles = out.rearrange("(m p) j -> p m j", p=P)
 
-        def energies(i, m0, m1, bank):
-            cols = slice(UNIT * i, UNIT * (i + 1))
-            acc = psum.tile([P, m1 - m0, UNIT], F32, name=f"o{i}_{m0}", tag=f"bank{bank}")
+        def energies(n, m0, m1, bank):
+            i, j0, j1 = pieces[n]
+            acc = psum.tile([P, m1 - m0, j1 - j0], F32, name=f"o{n}_{m0}", tag=f"bank{bank}")
             for m in range(m0, m1):
                 rows = slice(P * m, P * (m + 1))
                 nc.tensor.matmul_mx(
                     out=acc[:, m - m0, :],
                     lhsT=wo_codes[:, rows].bitcast(FP8X4),
                     lhsT_scale=wo_scales[:, rows],
-                    rhs=h_codes[:, cols].bitcast(FP8X4),
-                    rhs_scale=h_scales[:, cols],
+                    rhs=h_codes[:, columns(n)].bitcast(FP8X4),
+                    rhs_scale=h_scales[:, columns(n)],
                     start=True,
                     stop=True,
                 )
-            accs[i, m0] = acc
+            accs[n, m0] = acc
 
-        def empty(i, m0, m1, copy):
-            acc = accs[i, m0]
-            if i in PAIRS or i - 1 not in PAIRS:
-                results[m0] = keep.tile([P, m1 - m0, UNIT * (2 if i in PAIRS else 1)], F32, name=f"res{i}_{m0}")
+        def empty(n, m0, m1, copy):
+            acc = accs[n, m0]
+            first = n - 1 if n - 1 in PAIRS else n
+            last = n + 1 if n in PAIRS else n
+            c0, c1 = columns(first).start, columns(last).stop
+            if n == first:
+                results[m0] = keep.tile([P, m1 - m0, c1 - c0], F32, name=f"res{n}_{m0}")
             res = results[m0]
-            first = i - 1 if i - 1 in PAIRS else i
-            copy(res[:, :, UNIT * (i - first) : UNIT * (i - first + 1)], acc[:])
-            if i not in PAIRS:
-                nc.sync.dma_start(out_tiles[:, m0:m1, UNIT * first : UNIT * (i + 1)], res[:])
+            copy(res[:, :, columns(n).start - c0 : columns(n).stop - c0], acc[:])
+            if n == last:
+                nc.sync.dma_start(out_tiles[:, m0:m1, c0:c1], res[:])
 
-        def store_near(i):
-            energies(i, 0, NEAR, OUT_BANKS[i][0])
+        def store_near(n):
+            energies(n, 0, NEAR, OUT_BANKS[n][0])
 
-        def store_far(i):
-            energies(i, NEAR, ROW_TILES, OUT_BANKS[i][1])
+        def store_far(n):
+            energies(n, NEAR, ROW_TILES, OUT_BANKS[n][1])
 
         def after_p(i):
             for late, bank in X_LATE_BANK.items():
@@ -340,24 +377,19 @@ def tile_list_bead_well_energies_kernel(tc, tab_words, tab_scales, offs, wx, wd_
                     mm_a(j)
 
         def after_h(i):
-            for j in range(i + 1, UNITS):
+            for j in range(i + 1, UNITS if i < UNITS - HALVES else 0):
                 if A_BANKS[j] == A_BANKS[i]:
                     mm_a(j)
                     break
 
         lag = dict(zip(ORDER, LAGS))
-        for n in range(UNITS + max(LAGS)):
+        for n in range(len(pieces) + max(LAGS)):
             for m, at in enumerate(WO_AT):
                 if n == at:
                     quantise_wo(m)
             for c in ORDER:
                 i = n - lag[c]
-                if c == "u":
-                    for j in range(UNITS):
-                        if j + ULAG[j] == n:
-                            make_q(j)
-                    continue
-                if 0 <= i < UNITS:
+                if 0 <= i < len(pieces):
                     if c == "f":
                         well_shape(i)
                     if c == "p":

@@ -23,42 +23,19 @@ UNIT = 128
 UNITS = S // UNIT
 ROW_TILES = N // P
 
-EARLY = 7
-EARLY_A = 0
-X_LATE_BANK = {7:1}
-A_BANKS = (7,0)*4
-OUT_BANKS = ((2,3),)*4+((4,5),(2,3))*2
-OUT_ALTERNATES_FROM = 3
-NEAR = 2
-SQ = "VVVSSSSSSS"
-NEARE = "VVVVVVVVVV"
-FARE = "SSSSSSSSSS"
-WOE = "VV"
-CAST = "VSSSVS"
-LAST_CUTS = (0, 256, 512, S)
-RING = 4
-MOVEQ = "G"
-WO_AT = (0,1)
-WD_AFTER = 1
-GL = 4
-TAB_FIRST = 1
-ROWSET = "V"
-WDS = 0
-WDO_TAG = "wx_bf1_1"
-HALVES = 0
-JOIN = 0
+EARLY = UNITS - 1
+LAST_X_BANK = 1
+A_BANKS = (7, 0)
+OUT_BANKS = ((4, 5), (2, 3))
+OUT_ALTERNATES_FROM = 4
 TWICE = 5
-PICK_TAG = "wx_bf0_0"
-GATES = {}
-ULAG = (0,) * 8
-QE = "SSSSSGGGSS"
-PAIRS = ()
-WD_FIRST = 0
-A_AFTER = 1
-FIRST_A = 1
-LAGS = (0,0,0,0,0,1,1,1,1,1,0,2,2)
-ORDER = "fwupshqoraxcd"
-WO_CUTS = ((0,384),(384,640))
+NEAR = 2
+SQUARE_ON_VECTOR = 3
+Q_ON_GPSIMD = 5
+Q_BEHIND = 4
+TURNS = 4
+LAST_CUTS = (0, 256, 512, S)
+WO_CUTS = ((0, 256, 384), (384, N))
 
 
 def tile_list_bead_well_energies_kernel(tc, tab_words, tab_scales, offs, wx, wd_words, wd_scales, wo, out):
@@ -69,33 +46,26 @@ def tile_list_bead_well_energies_kernel(tc, tab_words, tab_scales, offs, wx, wd_
         psum = ctx.enter_context(tc.psum_pool(name="psum", bufs=1))
 
         offsets = keep.tile([P, S // 16], U16, name="offsets")
-        if not TAB_FIRST:
-            nc.sync.dma_start(offsets[:], offs)
 
         tab_rows = keep.tile([P, T // 4], I32, name="tab_rows", align_bytes=64)
-        {"G": nc.gpsimd, "V": nc.vector}[ROWSET].memset(tab_rows[:], 0)
+        nc.vector.memset(tab_rows[:], 0)
         tab_scales_i32 = tab_scales.bitcast(I32)
         for q in range(4):
             nc.gpsimd.dma_start(tab_rows[32 * q : 32 * q + 4 * PASSES, :], tab_scales_i32[:, 4 * q : 4 * q + 4, :])
-        wd_rows = keep.tile([P, PASSES, H // 4], I32, name="wd_rows", align_bytes=64)
-        nc.vector.memset(wd_rows[:], 0)
         moved_rows = [keep.tile([P, S // 4], I32, name=f"moved_rows{g}", align_bytes=64) for g in range(1, PASSES)]
         for tile in moved_rows:
             nc.vector.memset(tile[96:128, :], 0)
-        warm = keep.tile([P, 1], F32, name="warm")
+        warm = shared.tile([P, 1], F32, name="warm", tag="warm_wd", align_bytes=64)
         nc.vector.memset(warm[:], 1.0)
         warm_out = keep.tile([P, 1], F32, name="warm_out")
         nc.scalar.activation(warm_out[:], warm[:], ACT.Abs_reciprocal_sqrt)
+        wd_rows = shared.tile([P, PASSES, H // 4], I32, name="wd_rows", tag="warm_wd", align_bytes=64)
+        nc.vector.memset(wd_rows[:], 0)
         wd_scales_i32 = wd_scales.bitcast(I32)
-
-        def load_wd_rows(queue):
-            for q in range(4):
-                queue.dma_start(
-                    wd_rows[32 * q : 32 * q + 4, :, :], wd_scales_i32[:, 4 * q : 4 * q + 4, :].rearrange("g r c -> r g c")
-                )
-
-        if WDS == 0:
-            load_wd_rows(nc.scalar)
+        for q in range(4):
+            nc.scalar.dma_start(
+                wd_rows[32 * q : 32 * q + 4, :, :], wd_scales_i32[:, 4 * q : 4 * q + 4, :].rearrange("g r c -> r g c")
+            )
 
         tab, wx_raw, v_codes = {}, {}, {}
 
@@ -136,7 +106,8 @@ def tile_list_bead_well_energies_kernel(tc, tab_words, tab_scales, offs, wx, wd_
 
         def mm_x(g, i, closes=False):
             if g == 0:
-                x_ps[i] = psum.tile([P, 4, UNIT], F32, name=f"x{i}", tag=f"bank{i if i < EARLY else X_LATE_BANK[i]}")
+                bank = i if i < EARLY else LAST_X_BANK
+                x_ps[i] = psum.tile([P, 4, UNIT], F32, name=f"x{i}", tag=f"bank{bank}")
             for t in range(4):
                 nc.tensor.matmul_mx(
                     out=x_ps[i][:, t, :],
@@ -148,10 +119,9 @@ def tile_list_bead_well_energies_kernel(tc, tab_words, tab_scales, offs, wx, wd_
                     stop=(closes and t == 3),
                 )
 
-        def mm_a(i, passes=range(PASSES)):
-            if 0 in passes:
-                a_ps[i] = psum.tile([P, 4, UNIT], F32, name=f"a{i}", tag=f"bank{A_BANKS[i]}")
-            for g in passes:
+        def mm_a(i):
+            a_ps[i] = psum.tile([P, 4, UNIT], F32, name=f"a{i}", tag=f"bank{A_BANKS[i % 2]}")
+            for g in range(PASSES):
                 for t in range(4):
                     nc.tensor.matmul_mx(
                         out=a_ps[i][:, t, :],
@@ -163,256 +133,163 @@ def tile_list_bead_well_energies_kernel(tc, tab_words, tab_scales, offs, wx, wd_
                         stop=(g == LAST and t == 3),
                     )
 
-        copier = {"V": nc.vector.tensor_copy, "S": nc.scalar.copy}
-        load_tab(0, "tab0")
-        if TAB_FIRST:
-            nc.sync.dma_start(offsets[:], offs)
+        load_tab(0, "tab0_wx2")
+        nc.sync.dma_start(offsets[:], offs)
         load_tab(1, "tab1")
         load_wx(0, "wx0")
         load_wx(1, "wx1")
         gather_words(0, (0, S))
-        load_wx(2, "tab0")
+        load_wx(2, "tab0_wx2")
         wd_raw = shared.tile([P, PASSES, H // 2], I32, name="wd_raw", tag="wd_raw", align_bytes=64)
-        if WD_FIRST:
-            nc.sync.dma_start(wd_raw[:], wd_words.bitcast(I32).rearrange("g p w -> p g w"))
         load_tab(2, "tab2")
-        if WDS == 1:
-            load_wd_rows(nc.sync)
         gather_words(1, (0, S))
-        quantise_wx(0, 0, copier[CAST[0]])
-        quantise_wx(0, 1, copier[CAST[1]])
-        picked_rows = shared.tile([P, S // 4], I32, name="picked_rows", tag=PICK_TAG, align_bytes=64)
+        quantise_wx(0, 0, nc.vector.tensor_copy)
+        quantise_wx(0, 1, nc.scalar.copy)
+        picked_rows = shared.tile([P, S // 4], I32, name="picked_rows", tag="wx_bf0_0", align_bytes=64)
         v_rows = [picked_rows] + moved_rows
         for j0 in range(0, S, S // 2):
             nc.vector.tensor_copy(
                 picked_rows[:].bitcast(U8)[:, j0 : j0 + S // 2],
                 tab_rows[:].bitcast(U8).indirect(offsets[:, j0 // 16 : (j0 + S // 2) // 16]),
             )
+        for g in range(1, PASSES):
+            nc.gpsimd.dma_start(v_rows[g][0:112, :], picked_rows[4 * g : 4 * g + 112, :])
 
-        def move_rows(queue):
-            for g in range(1, PASSES):
-                queue.dma_start(v_rows[g][0:112, :], picked_rows[4 * g : 4 * g + 112, :])
-
-        if MOVEQ == "G":
-            move_rows(nc.gpsimd)
         wo_slots = wo.rearrange("(u t e) n -> t u e n", t=4, e=4)
         wo_raw = {}
 
-        def load_wo(n):
-            n0, n1 = WO_CUTS[n]
-            wo_raw[n] = keep.tile([P, 4, n1 - n0], F32, name=f"wo_raw{n}", align_bytes=64)
+        def load_wo(cuts):
+            n0, n1 = cuts[0], cuts[-1]
+            wo_raw[n0] = keep.tile([P, 4, n1 - n0], F32, name=f"wo_raw{n0}", align_bytes=64)
             for t in range(4):
-                nc.sync.dma_start(wo_raw[n][:, t, :], wo_slots[t][:, :, n0:n1])
+                nc.sync.dma_start(wo_raw[n0][:, t, :], wo_slots[t][:, :, n0:n1])
 
-        for n in range(WD_AFTER):
-            load_wo(n)
-        if WDS == 2:
-            load_wd_rows(nc.sync)
-        if not WD_FIRST:
-            nc.sync.dma_start(wd_raw[:], wd_words.bitcast(I32).rearrange("g p w -> p g w"))
-        if MOVEQ == "Y":
-            move_rows(nc.sync)
-        for n in range(WD_AFTER, len(WO_CUTS)):
-            load_wo(n)
-        if MOVEQ == "Z":
-            move_rows(nc.sync)
+        load_wo(WO_CUTS[0])
+        nc.sync.dma_start(wd_raw[:], wd_words.bitcast(I32).rearrange("g p w -> p g w"))
+        load_wo(WO_CUTS[1])
+
         for i in range(EARLY):
             mm_x(0, i)
-        quantise_wx(1, 0, copier[CAST[2]])
-        quantise_wx(1, 1, copier[CAST[3]])
+        quantise_wx(1, 0, nc.scalar.copy)
+        quantise_wx(1, 1, nc.scalar.copy)
         for i in range(TWICE):
             mm_x(1, i)
-        quantise_wx(LAST, 0, copier[CAST[4]])
-        quantise_wx(LAST, 1, copier[CAST[5]])
+        quantise_wx(LAST, 0, nc.vector.tensor_copy)
+        quantise_wx(LAST, 1, nc.scalar.copy)
         wd_codes = keep.tile([P, PASSES, H // 2], I32, name="wd_codes", align_bytes=64)
-        if not WD_FIRST:
-            gather_words(LAST, LAST_CUTS)
-        wd_ordered = shared.tile([P, PASSES, H // 4], I32, name="wd_ordered", tag=WDO_TAG, align_bytes=64)
+        gather_words(LAST, LAST_CUTS)
+
+        wd_ordered = shared.tile([P, PASSES, H // 4], I32, name="wd_ordered", tag="wx_bf1_1", align_bytes=64)
         nc.vector.tensor_copy(
-            wd_ordered[:].rearrange("p g (t u) -> p g t u", t=4),
-            wd_rows[:].rearrange("p g (u t) -> p g t u", t=4),
+            wd_ordered[:].rearrange("p g (t u) -> p t g u", t=4),
+            wd_rows[:].rearrange("p g (u t) -> p t g u", t=4),
         )
         nc.vector.tensor_copy(
-            wd_codes[:].rearrange("p g (t u w) -> p g t u w", t=4, w=2),
-            wd_raw[:].rearrange("p g (u t w) -> p g t u w", t=4, w=2),
+            wd_codes[:].rearrange("p g (t u w) -> p t g u w", t=4, w=2),
+            wd_raw[:].rearrange("p g (u t w) -> p t g u w", t=4, w=2),
         )
-        for i in range(EARLY_A):
-            mm_a(i, range(LAST))
-        if WD_FIRST:
-            gather_words(LAST, LAST_CUTS)
         for i in range(EARLY):
             mm_x(LAST, i, closes=i < TWICE)
             if i >= TWICE:
                 mm_x(1, i, closes=True)
-            if i == A_AFTER:
-                for j in range(FIRST_A):
-                    mm_a(j, (LAST,) if j < EARLY_A else range(PASSES))
+            if i == 1:
+                mm_a(0)
 
         wo_codes = keep.tile([P, N], U32, name="wo_codes", align_bytes=64)
         wo_scales = keep.tile([P, N], U8, name="wo_scales", align_bytes=64)
 
-        def quantise_wo(n):
-            l0, l1 = WO_CUTS[n]
-            wo_bf = shared.tile([P, l1 - l0, 4], BF16, name=f"wo_bf{n}", tag=f"wo_bf{n}", align_bytes=64)
-            if WOE[n] == "G":
-                nc.gpsimd.tensor_scalar(
-                    wo_bf[:], wo_raw[n][:].rearrange("p t n -> p n t"), 1.0, 0.0, ALU.mult, ALU.add
-                )
-            else:
-                copier[WOE[n]](
-                    wo_bf[:].rearrange("p (m e) t -> p m t e", e=4),
-                    wo_raw[n][:].rearrange("p t (m e) -> p m t e", e=4),
-                )
-            for n0, n1 in ((l0, l1),) if l1 - l0 not in (384, 640) else ((l0, l1 - 128), (l1 - 128, l1)):
+        def quantise_wo(cuts):
+            first = cuts[0]
+            wo_bf = shared.tile([P, cuts[-1] - first, 4], BF16, name=f"wo_bf{first}", tag=f"wo_bf{first}", align_bytes=64)
+            nc.vector.tensor_copy(
+                wo_bf[:].rearrange("p (m e) t -> p m t e", e=4),
+                wo_raw[first][:].rearrange("p t (m e) -> p m t e", e=4),
+            )
+            for n0, n1 in zip(cuts, cuts[1:]):
                 nc.vector.quantize_mx(
                     out=wo_codes[:, n0:n1].bitcast(FP8X4),
                     scales=wo_scales[:, n0:n1],
-                    in_=wo_bf[:, n0 - l0 : n1 - l0, :].rearrange("p n t -> p (n t)"),
+                    in_=wo_bf[:, n0 - first : n1 - first, :].rearrange("p n t -> p (n t)"),
                 )
 
-        accs, slots = {}, {}
         h_codes = keep.tile([P, S], U32, name="h_codes", align_bytes=64)
         h_scales = keep.tile([P, S], U8, name="h_scales", align_bytes=64)
-        p_squared, h_bf, q_tiles, results, xs_tiles, root_tiles, p_tiles = {}, {}, {}, {}, {}, {}, {}
+        q_sb, p_squared, h_tile, out_ps = {}, {}, {}, {}
 
-        pieces = [(i, 0, UNIT) for i in range(UNITS - HALVES)]
-        for i in range(UNITS - HALVES, UNITS):
-            pieces.extend([(i, 0, UNIT // 2), (i, UNIT // 2, UNIT)])
+        def unit_tile(name, i, turn):
+            return shared.tile([P, UNIT, 4], F32, name=f"{name}{i}", tag=f"{name}{turn}", align_bytes=64)
 
-        def by_entry(bank, n):
-            i, j0, j1 = pieces[n]
-            return bank[i][:, :, j0:j1].rearrange("p t j -> p j t")
-
-        def step_tile(name, n, dtype=F32):
-            i, j0, j1 = pieces[n]
-            tag = f"{name}{n % 4}" if name in ("x_squared", "root", "p_sb") else f"{name}{n}"
-            return shared.tile([P, j1 - j0, 4], dtype, name=f"{name}{n}", tag=tag, align_bytes=64)
-
-        def square(engine, dst, src):
-            if engine == "S":
-                nc.scalar.activation(dst[:], src[:], ACT.Square)
+        def make_q(i):
+            x_squared = unit_tile("x_squared", i, i % TURNS)
+            nc.scalar.activation(x_squared[:], x_ps[i][:].rearrange("p t j -> p j t"), ACT.Square)
+            root = unit_tile("root", i, i % TURNS)
+            nc.scalar.activation(root[:], x_squared[:], ACT.Abs_reciprocal_sqrt, bias=1.0)
+            if i < Q_ON_GPSIMD:
+                q_sb[i] = unit_tile("q_sb", i, i)
+                nc.scalar.activation(q_sb[i][:], root[:], ACT.Square)
             else:
-                {"V": nc.vector, "G": nc.gpsimd}[engine].tensor_tensor(dst[:], src[:], src[:], ALU.mult)
+                q_sb[i] = h_tile[i - Q_BEHIND]
+                nc.gpsimd.tensor_tensor(q_sb[i][:], root[:], root[:], ALU.mult)
 
-        def well_shape(n):
-            xs_tiles[n] = step_tile("x_squared", n)
-            nc.scalar.activation(xs_tiles[n][:], by_entry(x_ps, n), ACT.Square)
+        def make_p_squared(i):
+            p_sb = unit_tile("p_sb", i, i % TURNS)
+            nc.vector.tensor_tensor(p_sb[:], x_ps[i][:].rearrange("p t j -> p j t"), q_sb[i][:], ALU.mult)
+            p_squared[i] = unit_tile("p_squared", i, i)
+            if i < SQUARE_ON_VECTOR:
+                nc.vector.tensor_tensor(p_squared[i][:], p_sb[:], p_sb[:], ALU.mult)
+            else:
+                nc.scalar.activation(p_squared[i][:], p_sb[:], ACT.Square)
 
-        def make_root(n):
-            root_tiles[n] = step_tile("root", n)
-            nc.scalar.activation(root_tiles[n][:], xs_tiles[n][:], ACT.Abs_reciprocal_sqrt, bias=1.0)
-
-        def make_q(n):
-            q_tiles[n] = slots[n - GL] if QE[n] == "G" and GL else step_tile("q_sb", n)
-            square(QE[n], q_tiles[n], root_tiles[n])
-
-        def make_p(n):
-            p_tiles[n] = step_tile("p_sb", n)
-            nc.vector.tensor_tensor(p_tiles[n][:], by_entry(x_ps, n), q_tiles[n][:], ALU.mult)
-
-        def square_p(n):
-            p_squared[n] = step_tile("p_squared", n)
-            square(SQ[n], p_squared[n], p_tiles[n])
-
-        def make_h(n):
-            slots[n] = step_tile("h_bf", n)
-            half = (pieces[n][2] - pieces[n][1]) // 2
-            h_bf[n] = slots[n][:, 0:half, :].rearrange("p j t -> p (j t)").bitcast(BF16).rearrange("p (j t) -> p j t", t=4)
-            nc.vector.tensor_tensor(h_bf[n], by_entry(a_ps, n), p_squared[n][:], ALU.mult)
-
-        def columns(n):
-            i, j0, j1 = pieces[n]
-            return slice(UNIT * i + j0, UNIT * i + j1)
-
-        def quantise_h(n):
-            nc.vector.quantize_mx(
-                out=h_codes[:, columns(n)].bitcast(FP8X4),
-                scales=h_scales[:, columns(n)],
-                in_=h_bf[n].rearrange("p j t -> p (j t)"),
+        def make_h_codes(i):
+            h_tile[i] = unit_tile("h_tile", i, i)
+            h_bf = h_tile[i][:, 0 : UNIT // 2, :].rearrange("p j t -> p (j t)").bitcast(BF16)
+            nc.vector.tensor_tensor(
+                h_bf.rearrange("p (j t) -> p j t", t=4), a_ps[i][:].rearrange("p t j -> p j t"), p_squared[i][:], ALU.mult
             )
+            cols = slice(UNIT * i, UNIT * (i + 1))
+            nc.vector.quantize_mx(out=h_codes[:, cols].bitcast(FP8X4), scales=h_scales[:, cols], in_=h_bf)
 
         out_tiles = out.rearrange("(m p) j -> p m j", p=P)
 
-        def energies(n, m0, m1, bank):
-            i, j0, j1 = pieces[n]
-            acc = psum.tile([P, m1 - m0, j1 - j0], F32, name=f"o{n}_{m0}", tag=f"bank{bank}")
+        def energies(i, m0, m1, bank):
+            cols = slice(UNIT * i, UNIT * (i + 1))
+            out_ps[i, m0] = psum.tile([P, m1 - m0, UNIT], F32, name=f"o{i}_{m0}", tag=f"bank{bank}")
             for m in range(m0, m1):
                 rows = slice(P * m, P * (m + 1))
                 nc.tensor.matmul_mx(
-                    out=acc[:, m - m0, :],
+                    out=out_ps[i, m0][:, m - m0, :],
                     lhsT=wo_codes[:, rows].bitcast(FP8X4),
                     lhsT_scale=wo_scales[:, rows],
-                    rhs=h_codes[:, columns(n)].bitcast(FP8X4),
-                    rhs_scale=h_scales[:, columns(n)],
+                    rhs=h_codes[:, cols].bitcast(FP8X4),
+                    rhs_scale=h_scales[:, cols],
                     start=True,
                     stop=True,
                 )
-            accs[n, m0] = acc
 
-        def empty(n, m0, m1, copy):
-            acc = accs[n, m0]
-            first = n - 1 if n - 1 in PAIRS else n
-            last = n + 1 if n in PAIRS else n
-            c0, c1 = columns(first).start, columns(last).stop
-            if n == first:
-                results[m0] = keep.tile([P, m1 - m0, c1 - c0], F32, name=f"res{n}_{m0}")
-            res = results[m0]
-            copy(res[:, :, columns(n).start - c0 : columns(n).stop - c0], acc[:])
-            if n == last:
-                nc.sync.dma_start(out_tiles[:, m0:m1, c0:c1], res[:])
+        def store(i, m0, m1, copy):
+            res = keep.tile([P, m1 - m0, UNIT], F32, name=f"res{i}_{m0}")
+            copy(res[:], out_ps[i, m0][:])
+            nc.sync.dma_start(out_tiles[:, m0:m1, UNIT * i : UNIT * (i + 1)], res[:])
 
-        def store_near(n):
-            energies(n, 0, NEAR, OUT_BANKS[n][0])
-
-        def store_far(n):
-            energies(n, NEAR, ROW_TILES, OUT_BANKS[n][1])
-
-        def after_p(i):
-            for late, bank in X_LATE_BANK.items():
-                if i == bank:
-                    for g in range(PASSES):
-                        mm_x(g, late, closes=g == LAST)
-            for j in range(FIRST_A, UNITS):
-                if A_BANKS[j] == i and A_BANKS[j] not in A_BANKS[:j] and i < EARLY:
-                    mm_a(j)
-
-        def after_h(i):
-            for j in range(i + 1, UNITS if i < UNITS - HALVES else 0):
-                if A_BANKS[j] == A_BANKS[i]:
-                    mm_a(j)
-                    break
-
-        lag = dict(zip(ORDER, LAGS))
-        for n in range(len(pieces) + max(LAGS)):
-            for m, at in enumerate(WO_AT):
-                if n == at:
-                    quantise_wo(m)
-            for c in ORDER:
-                i = n - lag[c]
-                if 0 <= i < len(pieces):
-                    if c == "f":
-                        well_shape(i)
-                    if c == "p":
-                        make_p(i)
-                    if c == "w":
-                        make_root(i)
-                    if c == "u":
-                        make_q(i)
-                    if c == "s":
-                        square_p(i)
-                    if c == "x":
-                        after_p(i)
-                    if c == "h":
-                        make_h(i)
-                    if c == "a":
-                        after_h(i)
-                    if c == "q":
-                        quantise_h(i)
-                    if c == "o":
-                        store_near(i)
-                    if c == "c":
-                        empty(i, 0, NEAR, copier[NEARE[i]])
-                    if c == "d":
-                        empty(i, NEAR, ROW_TILES, copier[FARE[i]])
-                    if c == "r":
-                        store_far(i)
+        for i in range(UNITS + 2):
+            if i < len(WO_CUTS):
+                quantise_wo(WO_CUTS[i])
+            if i < UNITS:
+                make_q(i)
+                make_p_squared(i)
+            if 1 <= i <= UNITS:
+                closed = i - 1
+                make_h_codes(closed)
+                near_bank, far_bank = OUT_BANKS[closed % 2 if closed >= OUT_ALTERNATES_FROM else 1]
+                energies(closed, 0, NEAR, near_bank)
+                energies(closed, NEAR, ROW_TILES, far_bank)
+                if closed + 2 < UNITS:
+                    mm_a(closed + 2)
+            if i == LAST_X_BANK:
+                for g in range(PASSES):
+                    mm_x(g, UNITS - 1, closes=g == LAST)
+            if i == A_BANKS[1]:
+                mm_a(1)
+            if i >= 2:
+                store(i - 2, 0, NEAR, nc.vector.tensor_copy)
+                store(i - 2, NEAR, ROW_TILES, nc.scalar.copy)

@@ -28,7 +28,7 @@ LAST_X_BANK = 1
 A_BANKS = (7, 0)
 OUT_BANKS = ((4, 5), (2, 3))
 OUT_ALTERNATES_FROM = 4
-TWICE = 5
+TWICE = 3
 NEAR = 2
 SQUARE_ON_VECTOR = 3
 Q_ON_GPSIMD = 5
@@ -233,7 +233,7 @@ def tile_list_bead_well_energies_kernel(tc, tab_words, tab_scales, offs, wx, wd_
 
         def make_p_squared(i):
             p_sb = unit_tile("p_sb", i, i % TURNS)
-            nc.vector.tensor_tensor(p_sb[:], x_ps[i][:].rearrange("p t j -> p j t"), q_sb[i][:], ALU.mult)
+            nc.vector.tensor_tensor(p_sb[:], q_sb[i][:], x_ps[i][:].rearrange("p t j -> p j t"), ALU.mult)
             p_squared[i] = unit_tile("p_squared", i, i)
             if i < SQUARE_ON_VECTOR:
                 nc.vector.tensor_tensor(p_squared[i][:], p_sb[:], p_sb[:], ALU.mult)
@@ -244,7 +244,7 @@ def tile_list_bead_well_energies_kernel(tc, tab_words, tab_scales, offs, wx, wd_
             h_tile[i] = unit_tile("h_tile", i, i)
             h_bf = h_tile[i][:, 0 : UNIT // 2, :].rearrange("p j t -> p (j t)").bitcast(BF16)
             nc.vector.tensor_tensor(
-                h_bf.rearrange("p (j t) -> p j t", t=4), a_ps[i][:].rearrange("p t j -> p j t"), p_squared[i][:], ALU.mult
+                h_bf.rearrange("p (j t) -> p j t", t=4), p_squared[i][:], a_ps[i][:].rearrange("p t j -> p j t"), ALU.mult
             )
             cols = slice(UNIT * i, UNIT * (i + 1))
             nc.vector.quantize_mx(out=h_codes[:, cols].bitcast(FP8X4), scales=h_scales[:, cols], in_=h_bf)

from contextlib import ExitStack

import concourse.mybir as mybir

K, T, S, H, N = 1536, 2048, 1024, 512, 640
FLOPS = 2 * S * (2 * K * H + H * N)

F32 = mybir.dt.float32
BF16 = mybir.dt.bfloat16
I32 = mybir.dt.int32
U32 = mybir.dt.uint32
U16 = mybir.dt.uint16
U8 = mybir.dt.uint8
FP8X4 = mybir.dt.float8_e4m3fn_x4
FP4X4 = mybir.dt.float4_e2m1fn_x4
ACT = mybir.ActivationFunctionType
ALU = mybir.AluOpType

P = 128
PASSES = K // 512
LAST = PASSES - 1
UNIT = 128
UNITS = S // UNIT
ROW_TILES = N // P

EARLY = UNITS - 1
LAST_X_BANK = 1
A_BANKS = (7, 0)
OUT_BANKS = ((4, 5), (2, 3))
OUT_ALTERNATES_FROM = 4
TWICE = 3
NEAR = 2
SQUARE_ON_VECTOR = 3
Q_ON_GPSIMD = 5
Q_BEHIND = 4
TURNS = 4
LAST_CUTS = (0, 256, 512, S)
WO_CUTS = ((0, 256, 384), (384, N))


def tile_list_bead_well_energies_kernel(tc, tab_words, tab_scales, offs, wx, wd_words, wd_scales, wo, out):
    nc = tc.nc
    with ExitStack() as ctx:
        keep = ctx.enter_context(tc.tile_pool(name="keep", bufs=1))
        shared = ctx.enter_context(tc.tile_pool(name="shared", bufs=1))
        psum = ctx.enter_context(tc.psum_pool(name="psum", bufs=1))

        offsets = keep.tile([P, S // 16], U16, name="offsets")

        tab_rows = keep.tile([P, T // 4], I32, name="tab_rows", align_bytes=64)
        nc.vector.memset(tab_rows[:], 0)
        tab_scales_i32 = tab_scales.bitcast(I32)
        for q in range(4):
            nc.gpsimd.dma_start(tab_rows[32 * q : 32 * q + 4 * PASSES, :], tab_scales_i32[:, 4 * q : 4 * q + 4, :])
        moved_rows = [keep.tile([P, S // 4], I32, name=f"moved_rows{g}", align_bytes=64) for g in range(1, PASSES)]
        for tile in moved_rows:
            nc.vector.memset(tile[96:128, :], 0)
        warm = shared.tile([P, 1], F32, name="warm", tag="warm_wd", align_bytes=64)
        nc.vector.memset(warm[:], 1.0)
        warm_out = keep.tile([P, 1], F32, name="warm_out")
        nc.scalar.activation(warm_out[:], warm[:], ACT.Abs_reciprocal_sqrt)
        wd_rows = shared.tile([P, PASSES, H // 4], I32, name="wd_rows", tag="warm_wd", align_bytes=64)
        nc.vector.memset(wd_rows[:], 0)
        wd_scales_i32 = wd_scales.bitcast(I32)
        for q in range(4):
            nc.scalar.dma_start(
                wd_rows[32 * q : 32 * q + 4, :, :], wd_scales_i32[:, 4 * q : 4 * q + 4, :].rearrange("g r c -> r g c")
            )

        tab, wx_raw, v_codes = {}, {}, {}

        def load_tab(g, tag):
            tab[g] = shared.tile([P, T], I32, name=f"tab{g}", tag=tag, align_bytes=64)
            nc.sync.dma_start(tab[g][:], tab_words[g].rearrange("p n c -> p (n c)").bitcast(I32))

        def load_wx(g, tag):
            wx_raw[g] = shared.tile([P, 4, H], F32, name=f"wx_raw{g}", tag=tag, align_bytes=64)
            nc.sync.dma_start(wx_raw[g][:], wx[512 * g : 512 * (g + 1), :].rearrange("(p c) r -> p c r", c=4))

        def gather_words(g, cuts):
            for j0, j1 in zip(cuts, cuts[1:]):
                picked = keep.tile([P, j1 - j0], I32, name=f"v_codes{g}_{j0}", align_bytes=64)
                nc.vector.tensor_copy(
                    picked[:].bitcast(U32), tab[g][:].bitcast(U32).indirect(offsets[:, j0 // 16 : j1 // 16])
                )
                for j in range(j0, j1, UNIT):
                    v_codes[g, j // UNIT] = picked[:, j - j0 : j - j0 + UNIT].bitcast(FP8X4)

        wx_codes = [keep.tile([P, H], U32, name=f"wx_codes{g}", align_bytes=64) for g in range(PASSES)]
        wx_scales = [keep.tile([P, H], U8, name=f"wx_scales{g}", align_bytes=64) for g in range(PASSES)]

        def quantise_wx(g, half, copy):
            rounded = shared.tile([P, 2, P * 4], BF16, name=f"wx_bf{g}_{half}", tag=f"wx_bf{g}_{half}", align_bytes=64)
            copy(
                rounded[:].rearrange("p t (u e c) -> p t u c e", e=4, c=4),
                wx_raw[g][:].rearrange("p c (u t e) -> p t u c e", t=4, e=4)[:, 2 * half : 2 * half + 2],
            )
            cols = slice(2 * P * half, 2 * P * (half + 1))
            nc.vector.quantize_mx(
                out=wx_codes[g][:, cols].bitcast(FP8X4),
                scales=wx_scales[g][:, cols],
                in_=rounded[:].rearrange("p t w -> p (t w)"),
            )

        x_ps, a_ps = {}, {}

        def mm_x(g, i, closes=False):
            if g == 0:
                bank = i if i < EARLY else LAST_X_BANK
                x_ps[i] = psum.tile([P, 4, UNIT], F32, name=f"x{i}", tag=f"bank{bank}")
            for t in range(4):
                nc.tensor.matmul_mx(
                    out=x_ps[i][:, t, :],
                    lhsT=wx_codes[g][:, P * t : P * (t + 1)].bitcast(FP8X4),
                    lhsT_scale=wx_scales[g][:, P * t : P * (t + 1)],
                    rhs=v_codes[g, i],
                    rhs_scale=picked_rows[:].bitcast(U8)[4 * g : P, UNIT * i : UNIT * (i + 1)],
                    start=(g == 0 and t == 0),
                    stop=(closes and t == 3),
                )

        def mm_a(i):
            a_ps[i] = psum.tile([P, 4, UNIT], F32, name=f"a{i}", tag=f"bank{A_BANKS[i % 2]}")
            for g in range(PASSES):
                for t in range(4):
                    nc.tensor.matmul_mx(
                        out=a_ps[i][:, t, :],
                        lhsT=wd_codes[:, g, 64 * t : 64 * (t + 1)].bitcast(U8).bitcast(FP4X4),
                        lhsT_scale=wd_ordered[:, g, 32 * t : 32 * (t + 1)].bitcast(U8),
                        rhs=v_codes[g, i],
                        rhs_scale=v_rows[g][:].bitcast(U8)[:, UNIT * i : UNIT * (i + 1)],
                        start=(g == 0 and t == 0),
                        stop=(g == LAST and t == 3),
                    )

        load_tab(0, "tab0_wx2")
        nc.sync.dma_start(offsets[:], offs)
        load_tab(1, "tab1")
        load_wx(0, "wx0")
        load_wx(1, "wx1")
        gather_words(0, (0, S))
        load_wx(2, "tab0_wx2")
        wd_raw = shared.tile([P, PASSES, H // 2], I32, name="wd_raw", tag="wd_raw", align_bytes=64)
        load_tab(2, "tab2")
        gather_words(1, (0, S))
        quantise_wx(0, 0, nc.vector.tensor_copy)
        quantise_wx(0, 1, nc.scalar.copy)
        picked_rows = shared.tile([P, S // 4], I32, name="picked_rows", tag="wx_bf0_0", align_bytes=64)
        v_rows = [picked_rows] + moved_rows
        for j0 in range(0, S, S // 2):
            nc.vector.tensor_copy(
                picked_rows[:].bitcast(U8)[:, j0 : j0 + S // 2],
                tab_rows[:].bitcast(U8).indirect(offsets[:, j0 // 16 : (j0 + S // 2) // 16]),
            )
        for g in range(1, PASSES):
            nc.gpsimd.dma_start(v_rows[g][0:112, :], picked_rows[4 * g : 4 * g + 112, :])

        wo_slots = wo.rearrange("(u t e) n -> t u e n", t=4, e=4)
        wo_raw = {}

        def load_wo(cuts):
            n0, n1 = cuts[0], cuts[-1]
            wo_raw[n0] = keep.tile([P, 4, n1 - n0], F32, name=f"wo_raw{n0}", align_bytes=64)
            for t in range(4):
                nc.sync.dma_start(wo_raw[n0][:, t, :], wo_slots[t][:, :, n0:n1])

        load_wo(WO_CUTS[0])
        nc.sync.dma_start(wd_raw[:], wd_words.bitcast(I32).rearrange("g p w -> p g w"))
        load_wo(WO_CUTS[1])

        for i in range(EARLY):
            mm_x(0, i)
        quantise_wx(1, 0, nc.scalar.copy)
        quantise_wx(1, 1, nc.scalar.copy)
        for i in range(TWICE):
            mm_x(1, i)
        quantise_wx(LAST, 0, nc.vector.tensor_copy)
        quantise_wx(LAST, 1, nc.scalar.copy)
        wd_codes = keep.tile([P, PASSES, H // 2], I32, name="wd_codes", align_bytes=64)
        gather_words(LAST, LAST_CUTS)

        wd_ordered = shared.tile([P, PASSES, H // 4], I32, name="wd_ordered", tag="wx_bf1_1", align_bytes=64)
        nc.vector.tensor_copy(
            wd_ordered[:].rearrange("p g (t u) -> p t g u", t=4),
            wd_rows[:].rearrange("p g (u t) -> p t g u", t=4),
        )
        nc.vector.tensor_copy(
            wd_codes[:].rearrange("p g (t u w) -> p t g u w", t=4, w=2),
            wd_raw[:].rearrange("p g (u t w) -> p t g u w", t=4, w=2),
        )
        for i in range(EARLY):
            mm_x(LAST, i, closes=i < TWICE)
            if i >= TWICE:
                mm_x(1, i, closes=True)
            if i == 1:
                mm_a(0)

        wo_codes = keep.tile([P, N], U32, name="wo_codes", align_bytes=64)
        wo_scales = keep.tile([P, N], U8, name="wo_scales", align_bytes=64)

        def quantise_wo(cuts):
            first = cuts[0]
            wo_bf = shared.tile([P, cuts[-1] - first, 4], BF16, name=f"wo_bf{first}", tag=f"wo_bf{first}", align_bytes=64)
            nc.vector.tensor_copy(
                wo_bf[:].rearrange("p (m e) t -> p m t e", e=4),
                wo_raw[first][:].rearrange("p t (m e) -> p m t e", e=4),
            )
            for n0, n1 in zip(cuts, cuts[1:]):
                nc.vector.quantize_mx(
                    out=wo_codes[:, n0:n1].bitcast(FP8X4),
                    scales=wo_scales[:, n0:n1],
                    in_=wo_bf[:, n0 - first : n1 - first, :].rearrange("p n t -> p (n t)"),
                )

        h_codes = keep.tile([P, S], U32, name="h_codes", align_bytes=64)
        h_scales = keep.tile([P, S], U8, name="h_scales", align_bytes=64)
        q_sb, p_squared, h_tile, out_ps = {}, {}, {}, {}

        def unit_tile(name, i, turn):
            return shared.tile([P, UNIT, 4], F32, name=f"{name}{i}", tag=f"{name}{turn}", align_bytes=64)

        def make_q(i):
            x_squared = unit_tile("x_squared", i, i % TURNS)
            nc.scalar.activation(x_squared[:], x_ps[i][:].rearrange("p t j -> p j t"), ACT.Square)
            root = unit_tile("root", i, i % TURNS)
            nc.scalar.activation(root[:], x_squared[:], ACT.Abs_reciprocal_sqrt, bias=1.0)
            if i < Q_ON_GPSIMD:
                q_sb[i] = unit_tile("q_sb", i, i)
                nc.scalar.activation(q_sb[i][:], root[:], ACT.Square)
            else:
                q_sb[i] = h_tile[i - Q_BEHIND]
                nc.gpsimd.tensor_tensor(q_sb[i][:], root[:], root[:], ALU.mult)

        def make_p_squared(i):
            p_sb = unit_tile("p_sb", i, i % TURNS)
            nc.vector.tensor_tensor(p_sb[:], q_sb[i][:], x_ps[i][:].rearrange("p t j -> p j t"), ALU.mult)
            p_squared[i] = unit_tile("p_squared", i, i)
            if i < SQUARE_ON_VECTOR:
                nc.vector.tensor_tensor(p_squared[i][:], p_sb[:], p_sb[:], ALU.mult)
            else:
                nc.scalar.activation(p_squared[i][:], p_sb[:], ACT.Square)

        def make_h_codes(i):
            h_tile[i] = unit_tile("h_tile", i, i)
            h_bf = h_tile[i][:, 0 : UNIT // 2, :].rearrange("p j t -> p (j t)").bitcast(BF16)
            nc.vector.tensor_tensor(
                h_bf.rearrange("p (j t) -> p j t", t=4), p_squared[i][:], a_ps[i][:].rearrange("p t j -> p j t"), ALU.mult
            )
            cols = slice(UNIT * i, UNIT * (i + 1))
            nc.vector.quantize_mx(out=h_codes[:, cols].bitcast(FP8X4), scales=h_scales[:, cols], in_=h_bf)

        out_tiles = out.rearrange("(m p) j -> p m j", p=P)

        def energies(i, m0, m1, bank):
            cols = slice(UNIT * i, UNIT * (i + 1))
            out_ps[i, m0] = psum.tile([P, m1 - m0, UNIT], F32, name=f"o{i}_{m0}", tag=f"bank{bank}")
            for m in range(m0, m1):
                rows = slice(P * m, P * (m + 1))
                nc.tensor.matmul_mx(
                    out=out_ps[i, m0][:, m - m0, :],
                    lhsT=wo_codes[:, rows].bitcast(FP8X4),
                    lhsT_scale=wo_scales[:, rows],
                    rhs=h_codes[:, cols].bitcast(FP8X4),
                    rhs_scale=h_scales[:, cols],
                    start=True,
                    stop=True,
                )

        def store(i, m0, m1, copy):
            res = keep.tile([P, m1 - m0, UNIT], F32, name=f"res{i}_{m0}")
            copy(res[:], out_ps[i, m0][:])
            nc.sync.dma_start(out_tiles[:, m0:m1, UNIT * i : UNIT * (i + 1)], res[:])

        for i in range(UNITS + 2):
            if i < len(WO_CUTS):
                quantise_wo(WO_CUTS[i])
            if i < UNITS:
                make_q(i)
                make_p_squared(i)
            if 1 <= i <= UNITS:
                closed = i - 1
                make_h_codes(closed)
                near_bank, far_bank = OUT_BANKS[closed % 2 if closed >= OUT_ALTERNATES_FROM else 1]
                energies(closed, 0, NEAR, near_bank)
                energies(closed, NEAR, ROW_TILES, far_bank)
                if closed + 2 < UNITS:
                    mm_a(closed + 2)
            if i == LAST_X_BANK:
                for g in range(PASSES):
                    mm_x(g, UNITS - 1, closes=g == LAST)
            if i == A_BANKS[1]:
                mm_a(1)
            if i >= 2:
                store(i - 2, 0, NEAR, nc.vector.tensor_copy)
                store(i - 2, NEAR, ROW_TILES, nc.scalar.copy)
